import numpy as np
import ml_dtypes


def mxq(x, axis, fmt="e4m3"):
    dtype, down = {"e4m3": (ml_dtypes.float8_e4m3fn, 7), "e5m2": (ml_dtypes.float8_e5m2, 14)}[fmt]
    v = np.moveaxis(np.asarray(x, np.float32).astype(ml_dtypes.bfloat16).astype(np.float64), axis, -1)
    blocks = v.reshape(v.shape[:-1] + (-1, 32))
    amax = np.abs(blocks).max(-1, keepdims=True)
    byte = np.maximum(np.where(amax > 0, np.frexp(amax)[1] - 1 + 127, 0) - down, 1)
    scale = np.exp2(byte - 127.0)
    codes = (blocks / scale).astype(np.float32).astype(dtype).astype(np.float64)
    return np.moveaxis((codes * scale).reshape(v.shape), -1, axis)


WIDE = False


def mx_kscale(k):
    if not WIDE:
        return np.ones(k)
    levels = np.array([18, -18])
    if k % 512:
        return np.exp2(np.random.permutation(np.resize(levels, k // 32))).repeat(32)
    a = np.empty((k // 512, 16))
    for p in range(k // 512):
        a[p, :8] = np.random.permutation(np.resize(levels, 8))
        for g in range(8):
            far = levels[np.abs(levels - a[p, g]) >= 10]
            a[p, g + 8] = far[np.random.randint(len(far))]
    return np.exp2(a.ravel()).repeat(32)


def f64(x):
    return np.asarray(x).astype(np.float64)


def striped(idx):
    return np.tile(np.asarray(idx).reshape(-1, 16).T, (8, 1)).astype(np.uint16)


def unstriped(offs):
    return offs[:16].T.reshape(-1).astype(np.int64)


E2M1 = np.array([0.0, 0.5, 1.0, 1.5, 2.0, 3.0, 4.0, 6.0, -0.0, -0.5, -1.0, -1.5, -2.0, -3.0, -4.0, -6.0])


def pack_weight(w, fmt):
    k, n = w.shape
    w = f64(np.asarray(w, np.float32).astype(ml_dtypes.bfloat16)).reshape(k // 32, 32, n)
    amax = np.abs(w).max(1)
    if fmt == "e4m3":
        byte = np.frexp(amax)[1] - 1 + 127 - 7
    else:
        mant, ex = np.frexp(amax / 6.0)
        byte = np.where(mant > 0.5, ex, ex - 1) + 127
    byte = np.clip(np.where(amax > 0, byte, 1), 1, 254)
    scaled = (w * np.exp2(127.0 - byte)[:, None, :]).reshape(k, n).astype(np.float32)
    by_word = np.ascontiguousarray(scaled.reshape(k // 512, 128, 4, n).transpose(0, 1, 3, 2))
    if fmt == "e4m3":
        words = by_word.astype(ml_dtypes.float8_e4m3fn).view(np.uint8)
    else:
        c = by_word.astype(ml_dtypes.float4_e2m1fn).view(np.uint8) & 0xF
        words = (c[..., 0::2] | (c[..., 1::2] << 4)).reshape(k // 512, 128, 2 * n)
    return np.ascontiguousarray(words), np.ascontiguousarray(byte.astype(np.uint8).reshape(k // 512, 16, n))


def unpack_weight(words, scales, fmt):
    g, _, n = scales.shape
    words = np.ascontiguousarray(words).reshape(g, 128, n, -1)
    if fmt == "e4m3":
        vals = words.view(ml_dtypes.float8_e4m3fn).astype(np.float64)
    else:
        nib = np.empty((g, 128, n, 4), np.uint8)
        nib[..., 0::2] = words & 0xF
        nib[..., 1::2] = words >> 4
        vals = E2M1[nib]
    vals = vals * np.repeat(np.exp2(scales.astype(np.float64) - 127.0), 8, axis=1)[..., None]
    return vals.transpose(0, 1, 3, 2).reshape(g * 512, n)


V, K, E, D, DV = 512, 4, 2048, 256, 512


def setup_inputs():
    n = np.random.standard_normal
    v = mx_kscale(DV)[:, None]
    coarse = lambda x: x.astype(np.float32).astype(ml_dtypes.bfloat16).astype(np.float64)
    wp = pack_weight(n((DV, D)) / np.sqrt(DV) / v, "e4m3")
    return {
        "dyT": (coarse(n((DV, V))) * v).astype(np.float32),
        "hE": (np.random.randint(1, 32, (DV, E)) / 32.0).astype(np.float32),
        "w_words": wp[0],
        "w_scales": wp[1],
        "offs": striped(np.random.randint(0, V, E)),
        "offs2": striped(np.random.permutation(E)),
    }


def reference(dyT, hE, w_words, w_scales, offs, offs2):
    h = f64(hE)
    dz = f64(dyT)[:, unstriped(offs)] * h * (1.0 - h)
    dm = unpack_weight(w_words, w_scales, "e4m3").T @ mxq(dz, 0, "e5m2")
    return dm[:, unstriped(offs2)].reshape(D, V, K).sum(-1)

@@ -1,0 +1,183 @@
+from contextlib import ExitStack
+
+import concourse.mybir as mybir
+
+V, K, E, D, DV = 512, 4, 2048, 256, 512
+FLOPS = 2 * DV * D * E
+
+F32 = mybir.dt.float32
+BF16 = mybir.dt.bfloat16
+I32 = mybir.dt.int32
+U32 = mybir.dt.uint32
+U16 = mybir.dt.uint16
+U8 = mybir.dt.uint8
+E4M3X4 = mybir.dt.float8_e4m3fn_x4
+E5M2X4 = mybir.dt.float8_e5m2_x4
+ALU = mybir.AluOpType
+COPY = mybir.ActivationFunctionType.Copy
+
+P = 128
+PACK = 4
+N_TILE = 512
+PAD = 32
+PIECES = [(0, 512), (512, 512), (1024, 512), (1536, 256), (1792, 128), (1920, 128)]
+SUM_PIECES = [(0, 0, 1024), (0, 1024, 1024), (1, 0, 1024), (1, 1024, 512), (1, 1536, 256), (1, 1792, 256)]
+SUM_ENGINE = "v"
+
+
+def tile_attend_gmp_sig_kernel(tc, dyT, hE, w_words, w_scales, offs, offs2, out):
+    nc = tc.nc
+    with ExitStack() as ctx:
+        keep = ctx.enter_context(tc.tile_pool(name="keep", bufs=1))
+        psum = ctx.enter_context(tc.psum_pool(name="psum", bufs=1))
+
+        dst = keep.tile([P, E // 16], U16, name="dst")
+        src = keep.tile([P, E // 16], U16, name="src")
+        dy = [keep.tile([P, V + PAD], F32, name="dy%d" % t) for t in range(PACK)]
+        h = [keep.tile([P, PACK, N_TILE], F32, name="h%d" % c) for c in range(4)]
+        u = [keep.tile([P, PACK, N_TILE], F32, name="u%d" % c) for c in range(4)]
+        w_codes = keep.tile([P, D], U32, name="w_codes", align_bytes=64)
+        w_plane = keep.tile([P, D], U8, name="w_plane", align_bytes=64)
+        codes = [keep.tile([P, N_TILE], U32, name="codes%d" % c, align_bytes=64) for c in range(4)]
+        planes = [keep.tile([P, N_TILE], U8, name="planes%d" % c, align_bytes=64) for c in range(4)]
+        dm = [keep.tile([P, E], F32, name="dm%d" % m) for m in range(2)]
+
+        dy_rows = dyT.rearrange("(p t) x -> t p x", t=PACK)
+        h_rows = hE.rearrange("(p t) e -> p t e", t=PACK)
+
+        for t in range(PACK):
+            nc.gpsimd.memset(dy[t][:, V:], 0.0)
+        nc.gpsimd.memset(w_plane[:].bitcast(I32), 0)
+
+        for t in range(PACK):
+            nc.sync.dma_start(h[0][:, t, :], h_rows[:, t, 0:N_TILE])
+            if t == 0:
+                nc.sync.dma_start(dst[:], offs)
+            nc.sync.dma_start(dy[t][:, :V], dy_rows[t])
+        for c in range(1, 4):
+            nc.sync.dma_start(h[c][:], h_rows[:, :, c * N_TILE : (c + 1) * N_TILE])
+        nc.sync.dma_start(w_codes[:].bitcast(I32), w_words[0].rearrange("p d r -> p (d r)").bitcast(I32))
+        for q in range(4):
+            nc.sync.dma_start(w_plane[32 * q : 32 * q + 4, :].bitcast(I32), w_scales[0, 4 * q : 4 * q + 4, :].bitcast(I32))
+        nc.sync.dma_start(src[:], offs2)
+
+        def slope(c, t0, t1):
+            nc.vector.scalar_tensor_tensor(
+                u[c][:, t0:t1, :], h[c][:, t0:t1, :], 1.0, h[c][:, t0:t1, :], ALU.subtract, ALU.mult
+            )
+
+        prod = {}
+        grouped = {}
+
+        def gather(i, t):
+            e0, n = PIECES[i]
+            c, c0 = divmod(e0, N_TILE)
+            if t == 0:
+                prod[i] = keep.tile([P, PACK, n], F32, name="prod%d" % i)
+            nc.vector.tensor_tensor(
+                prod[i][:, t, :],
+                dy[t][:].indirect(dst[:, e0 // 16 : (e0 + n) // 16]),
+                u[c][:, t, c0 : c0 + n],
+                ALU.mult,
+            )
+
+        def round_piece(i):
+            e0, n = PIECES[i]
+            grouped[i] = keep.tile([P, n, PACK], BF16, name="grouped%d" % i, align_bytes=64)
+            if i == len(PIECES) - 1:
+                nc.vector.tensor_scalar(grouped[i][:], prod[i][:].rearrange("p t e -> p e t"), -1.0, None, ALU.mult)
+            else:
+                nc.scalar.activation(grouped[i][:], prod[i][:].rearrange("p t e -> p e t"), COPY, scale=-1.0)
+
+        def quantise(i):
+            e0, n = PIECES[i]
+            c, c0 = divmod(e0, N_TILE)
+            nc.vector.quantize_mx(
+                out=codes[c][:, c0 : c0 + n].bitcast(E5M2X4),
+                scales=planes[c][:, c0 : c0 + n],
+                in_=grouped[i][:].rearrange("p e t -> p (e t)"),
+            )
+
+        def multiply(c):
+            for m in range(2):
+                acc = psum.tile([P, N_TILE], F32, name="acc%d_%d" % (c, m))
+                nc.tensor.matmul_mx(
+                    out=acc[:],
+                    lhsT=w_codes[:, m * P : (m + 1) * P].bitcast(E4M3X4),
+                    lhsT_scale=w_plane[:, m * P : (m + 1) * P],
+                    rhs=codes[c][:].bitcast(E5M2X4),
+                    rhs_scale=planes[c][:],
+                    start=True,
+                    stop=True,
+                )
+                cols = dm[m][:, c * N_TILE : (c + 1) * N_TILE]
+                if c == 3 and m == 0:
+                    nc.vector.tensor_copy(cols, acc[:])
+                else:
+                    nc.scalar.copy(cols, acc[:])
+
+        slope(0, 0, 1)
+        for t in range(PACK):
+            if t + 1 < PACK:
+                slope(0, t + 1, t + 2)
+            else:
+                slope(1, 0, PACK)
+            gather(0, t)
+        round_piece(0)
+        for i in range(1, len(PIECES)):
+            for t in range(PACK):
+                gather(i, t)
+                if t == 1 and i < 3:
+                    slope(i + 1, 0, PACK)
+                if t == (3 if i == len(PIECES) - 1 else 2):
+                    quantise(i - 1)
+                    if i - 1 < 3:
+                        multiply(i - 1)
+            round_piece(i)
+        quantise(len(PIECES) - 1)
+        multiply(3)
+
+        picked = {}
+
+        def pick(i):
+            m, s0, n = SUM_PIECES[i]
+            picked[i] = keep.tile([P, n], F32, name="picked%d" % i)
+            nc.vector.tensor_copy(picked[i][:], dm[m][:].indirect(src[:, s0 // 16 : (s0 + n) // 16]))
+
+        pairs = {}
+
+        def add_pairs(i, eng):
+            m, s0, n = SUM_PIECES[i]
+            g = picked[i][:].rearrange("p (x j) -> p x j", j=K)
+            pairs[i] = keep.tile([P, n // K, 2], F32, name="pairs%d" % i)
+            eng.tensor_tensor(pairs[i][:], g[:, :, 0:2], g[:, :, 2:4], ALU.add)
+
+        def add_last(i, eng):
+            m, s0, n = SUM_PIECES[i]
+            res = keep.tile([P, n // K], F32, name="res%d" % i)
+            eng.tensor_tensor(res[:], pairs[i][:, :, 0], pairs[i][:, :, 1], ALU.add)
+            nc.sync.dma_start(out[m * P : (m + 1) * P, s0 // K : (s0 + n) // K], res[:])
+
+        def reduce_piece(i):
+            m, s0, n = SUM_PIECES[i]
+            res = keep.tile([P, n // K], F32, name="res%d" % i)
+            nc.vector.tensor_reduce(res[:], picked[i][:].rearrange("p (x j) -> p x j", j=K), mybir.AxisListType.X, ALU.add)
+            nc.sync.dma_start(out[m * P : (m + 1) * P, s0 // K : (s0 + n) // K], res[:])
+
+        last = len(SUM_PIECES) - 1
+        if SUM_ENGINE == "v":
+            for i in range(last + 1):
+                pick(i)
+                if i >= 2:
+                    add_last(i - 2, nc.vector)
+                if i >= 1 and i - 1 < last - 1:
+                    add_pairs(i - 1, nc.vector)
+            reduce_piece(last - 1)
+            reduce_piece(last)
+        else:
+            for i in range(last + 1):
+                pick(i)
+                if i < last:
+                    add_pairs(i, nc.gpsimd)
+                    add_last(i, nc.gpsimd)
+            reduce_piece(last)

@@ -21,8 +21,7 @@ PACK = 4
 N_TILE = 512
 PAD = 32
 PIECES = [(0, 512), (512, 512), (1024, 512), (1536, 256), (1792, 128), (1920, 128)]
-SUM_PIECES = [(0, 0, 1024), (0, 1024, 1024), (1, 0, 1024), (1, 1024, 512), (1, 1536, 256), (1, 1792, 256)]
-SUM_ENGINE = "v"
+SUM_PIECES = [(0, 0, 512), (0, 512, 512), (0, 1024, 512), (0, 1536, 512), (1, 0, 512), (1, 512, 512), (1, 1024, 256), (1, 1280, 512), (1, 1792, 256)]
 
 
 def tile_attend_gmp_sig_kernel(tc, dyT, hE, w_words, w_scales, offs, offs2, out):
@@ -38,8 +37,8 @@ def tile_attend_gmp_sig_kernel(tc, dyT, hE, w_words, w_scales, offs, offs2, out)
         u = [keep.tile([P, PACK, N_TILE], F32, name="u%d" % c) for c in range(4)]
         w_codes = keep.tile([P, D], U32, name="w_codes", align_bytes=64)
         w_plane = keep.tile([P, D], U8, name="w_plane", align_bytes=64)
-        codes = [keep.tile([P, N_TILE], U32, name="codes%d" % c, align_bytes=64) for c in range(4)]
-        planes = [keep.tile([P, N_TILE], U8, name="planes%d" % c, align_bytes=64) for c in range(4)]
+        codes = keep.tile([P, E], U32, name="codes", align_bytes=64)
+        plane = keep.tile([P, E], U8, name="plane", align_bytes=64)
         dm = [keep.tile([P, E], F32, name="dm%d" % m) for m in range(2)]
 
         dy_rows = dyT.rearrange("(p t) x -> t p x", t=PACK)
@@ -87,34 +86,42 @@ def tile_attend_gmp_sig_kernel(tc, dyT, hE, w_words, w_scales, offs, offs2, out)
             if i == len(PIECES) - 1:
                 nc.vector.tensor_scalar(grouped[i][:], prod[i][:].rearrange("p t e -> p e t"), -1.0, None, ALU.mult)
             else:
-                nc.scalar.activation(grouped[i][:], prod[i][:].rearrange("p t e -> p e t"), COPY, scale=-1.0)
+                nc.scalar.activation(
+                    grouped[i][:].rearrange("p (c i) t -> p c t i", i=4),
+                    prod[i][:].rearrange("p t (c i) -> p c t i", i=4),
+                    COPY,
+                    scale=-1.0,
+                )
 
         def quantise(i):
             e0, n = PIECES[i]
-            c, c0 = divmod(e0, N_TILE)
             nc.vector.quantize_mx(
-                out=codes[c][:, c0 : c0 + n].bitcast(E5M2X4),
-                scales=planes[c][:, c0 : c0 + n],
+                out=codes[:, e0 : e0 + n].bitcast(E5M2X4),
+                scales=plane[:, e0 : e0 + n],
                 in_=grouped[i][:].rearrange("p e t -> p (e t)"),
             )
 
-        def multiply(c):
+        def multiply(m, e0, keep0, keep1, on_vector):
+            acc = psum.tile([P, N_TILE], F32, name="acc%d" % (banks.pop(0)))
+            nc.tensor.matmul_mx(
+                out=acc[:],
+                lhsT=w_codes[:, m * P : (m + 1) * P].bitcast(E4M3X4),
+                lhsT_scale=w_plane[:, m * P : (m + 1) * P],
+                rhs=codes[:, e0 : e0 + N_TILE].bitcast(E5M2X4),
+                rhs_scale=plane[:, e0 : e0 + N_TILE],
+                start=True,
+                stop=True,
+            )
+            if on_vector:
+                nc.vector.tensor_copy(dm[m][:, keep0:keep1], acc[:, keep0 - e0 : keep1 - e0])
+            else:
+                nc.scalar.copy(dm[m][:, keep0:keep1], acc[:, keep0 - e0 : keep1 - e0])
+
+        def multiply_chunk(c):
             for m in range(2):
-                acc = psum.tile([P, N_TILE], F32, name="acc%d_%d" % (c, m))
-                nc.tensor.matmul_mx(
-                    out=acc[:],
-                    lhsT=w_codes[:, m * P : (m + 1) * P].bitcast(E4M3X4),
-                    lhsT_scale=w_plane[:, m * P : (m + 1) * P],
-                    rhs=codes[c][:].bitcast(E5M2X4),
-                    rhs_scale=planes[c][:],
-                    start=True,
-                    stop=True,
-                )
-                cols = dm[m][:, c * N_TILE : (c + 1) * N_TILE]
-                if c == 3 and m == 0:
-                    nc.vector.tensor_copy(cols, acc[:])
-                else:
-                    nc.scalar.copy(cols, acc[:])
+                multiply(m, c * N_TILE, c * N_TILE, (c + 1) * N_TILE, False)
+
+        banks = [0, 1, 2, 3, 4, 5, 6, 7, 0]
 
         slope(0, 0, 1)
         for t in range(PACK):
@@ -124,18 +131,37 @@ def tile_attend_gmp_sig_kernel(tc, dyT, hE, w_words, w_scales, offs, offs2, out)
                 slope(1, 0, PACK)
             gather(0, t)
         round_piece(0)
-        for i in range(1, len(PIECES)):
-            for t in range(PACK):
-                gather(i, t)
-                if t == 1 and i < 3:
-                    slope(i + 1, 0, PACK)
-                if t == (3 if i == len(PIECES) - 1 else 2):
-                    quantise(i - 1)
-                    if i - 1 < 3:
-                        multiply(i - 1)
-            round_piece(i)
-        quantise(len(PIECES) - 1)
-        multiply(3)
+        for t in range(PACK):
+            gather(1, t)
+            if t == 1:
+                slope(2, 0, PACK)
+            if t == 2:
+                quantise(0)
+                multiply_chunk(0)
+        round_piece(1)
+        for t in range(PACK):
+            gather(2, t)
+        round_piece(2)
+        slope(3, 0, PACK)
+        quantise(1)
+        multiply_chunk(1)
+        for t in range(PACK):
+            gather(3, t)
+        round_piece(3)
+        quantise(2)
+        for t in range(PACK):
+            gather(4, t)
+        round_piece(4)
+        multiply_chunk(2)
+        quantise(3)
+        for t in range(PACK):
+            gather(5, t)
+        quantise(4)
+        round_piece(5)
+        multiply(0, 1408, 1536, 1920, False)
+        quantise(5)
+        multiply(0, 1536, 1920, 2048, True)
+        multiply(1, 1536, 1536, 2048, False)
 
         picked = {}
 
@@ -165,19 +191,11 @@ def tile_attend_gmp_sig_kernel(tc, dyT, hE, w_words, w_scales, offs, offs2, out)
             nc.sync.dma_start(out[m * P : (m + 1) * P, s0 // K : (s0 + n) // K], res[:])
 
         last = len(SUM_PIECES) - 1
-        if SUM_ENGINE == "v":
-            for i in range(last + 1):
-                pick(i)
-                if i >= 2:
-                    add_last(i - 2, nc.vector)
-                if i >= 1 and i - 1 < last - 1:
-                    add_pairs(i - 1, nc.vector)
-            reduce_piece(last - 1)
-            reduce_piece(last)
-        else:
-            for i in range(last + 1):
-                pick(i)
-                if i < last:
-                    add_pairs(i, nc.gpsimd)
-                    add_last(i, nc.gpsimd)
-            reduce_piece(last)
+        for i in range(last + 1):
+            pick(i)
+            if i < last - 1:
+                add_pairs(i, nc.gpsimd)
+                add_last(i, nc.gpsimd)
+        add_pairs(last - 1, nc.vector)
+        reduce_piece(last)
+        add_last(last - 1, nc.vector)

@@ -19,9 +19,9 @@ COPY = mybir.ActivationFunctionType.Copy
 P = 128
 PACK = 4
 N_TILE = 512
-PAD = 32
-PIECES = [(0, 512), (512, 512), (1024, 512), (1536, 256), (1792, 128), (1920, 128)]
-SUM_PIECES = [(0, 0, 512), (0, 512, 512), (0, 1024, 512), (0, 1536, 512), (1, 0, 512), (1, 512, 512), (1, 1024, 256), (1, 1280, 512), (1, 1792, 256)]
+LOADS = [(0, 512), (512, 1024), (1024, 1536), (1536, 2048)]
+PIECES = [(0, 512), (512, 1024), (1024, 1536), (1536, 1792), (1792, 1920), (1920, 2048)]
+WINDOW = 512 + 32
 
 
 def tile_attend_gmp_sig_kernel(tc, dyT, hE, w_words, w_scales, offs, offs2, out):
@@ -32,9 +32,17 @@ def tile_attend_gmp_sig_kernel(tc, dyT, hE, w_words, w_scales, offs, offs2, out)
 
         dst = keep.tile([P, E // 16], U16, name="dst")
         src = keep.tile([P, E // 16], U16, name="src")
-        dy = [keep.tile([P, V + PAD], F32, name="dy%d" % t) for t in range(PACK)]
-        h = [keep.tile([P, PACK, N_TILE], F32, name="h%d" % c) for c in range(4)]
-        u = [keep.tile([P, PACK, N_TILE], F32, name="u%d" % c) for c in range(4)]
+        dy = [keep.tile([P, WINDOW], F32, name="dy%d" % t) for t in range(PACK)]
+        h = {e0: keep.tile([P, PACK, e1 - e0], F32, name="h%d" % e0) for e0, e1 in LOADS}
+        u = {e0: keep.tile([P, PACK, e1 - e0], F32, name="u%d" % e0) for e0, e1 in LOADS}
+        prod = {e0: keep.tile([P, PACK, e1 - e0], F32, name="prod%d" % e0) for e0, e1 in PIECES}
+
+        def cut(tiles, t0, t1, e0, e1):
+            base = max(b for b in tiles if b <= e0)
+            return tiles[base][:, t0:t1, e0 - base : e1 - base]
+
+        grouped = keep.tile([P, E, PACK], BF16, name="grouped", align_bytes=64)
+        grouped_last = keep.tile([P, 128, PACK], BF16, name="grouped_last", align_bytes=64)
         w_codes = keep.tile([P, D], U32, name="w_codes", align_bytes=64)
         w_plane = keep.tile([P, D], U8, name="w_plane", align_bytes=64)
         codes = keep.tile([P, E], U32, name="codes", align_bytes=64)
@@ -48,60 +56,62 @@ def tile_attend_gmp_sig_kernel(tc, dyT, hE, w_words, w_scales, offs, offs2, out)
             nc.gpsimd.memset(dy[t][:, V:], 0.0)
         nc.gpsimd.memset(w_plane[:].bitcast(I32), 0)
 
-        for t in range(PACK):
-            nc.sync.dma_start(h[0][:, t, :], h_rows[:, t, 0:N_TILE])
-            if t == 0:
-                nc.sync.dma_start(dst[:], offs)
+        def load_h(t0, t1, e0, e1):
+            nc.sync.dma_start(cut(h, t0, t1, e0, e1), h_rows[:, t0:t1, e0:e1])
+
+        def load_dy(t):
             nc.sync.dma_start(dy[t][:, :V], dy_rows[t])
-        for c in range(1, 4):
-            nc.sync.dma_start(h[c][:], h_rows[:, :, c * N_TILE : (c + 1) * N_TILE])
+
+        load_h(0, 1, 0, 512)
+        load_h(1, 2, 0, 512)
+        nc.sync.dma_start(dst[:], offs)
+        load_dy(0)
+        load_h(2, 3, 0, 512)
+        load_dy(1)
+        load_h(3, 4, 0, 512)
+        load_dy(2)
+        load_h(0, PACK, 512, 1024)
+        load_dy(3)
+        load_h(0, PACK, 1024, 1536)
+        load_h(0, PACK, 1536, 2048)
         nc.sync.dma_start(w_codes[:].bitcast(I32), w_words[0].rearrange("p d r -> p (d r)").bitcast(I32))
         for q in range(4):
             nc.sync.dma_start(w_plane[32 * q : 32 * q + 4, :].bitcast(I32), w_scales[0, 4 * q : 4 * q + 4, :].bitcast(I32))
         nc.sync.dma_start(src[:], offs2)
 
-        def slope(c, t0, t1):
+        def slope(t0, t1, e0, e1):
             nc.vector.scalar_tensor_tensor(
-                u[c][:, t0:t1, :], h[c][:, t0:t1, :], 1.0, h[c][:, t0:t1, :], ALU.subtract, ALU.mult
+                cut(u, t0, t1, e0, e1), cut(h, t0, t1, e0, e1), 1.0, cut(h, t0, t1, e0, e1), ALU.subtract, ALU.mult
             )
 
-        prod = {}
-        grouped = {}
-
-        def gather(i, t):
-            e0, n = PIECES[i]
-            c, c0 = divmod(e0, N_TILE)
-            if t == 0:
-                prod[i] = keep.tile([P, PACK, n], F32, name="prod%d" % i)
+        def gather(t, e0, e1):
             nc.vector.tensor_tensor(
-                prod[i][:, t, :],
-                dy[t][:].indirect(dst[:, e0 // 16 : (e0 + n) // 16]),
-                u[c][:, t, c0 : c0 + n],
+                cut(prod, t, t + 1, e0, e1)[:, 0, :],
+                dy[t][:].indirect(dst[:, e0 // 16 : e1 // 16]),
+                cut(u, t, t + 1, e0, e1)[:, 0, :],
                 ALU.mult,
             )
 
-        def round_piece(i):
-            e0, n = PIECES[i]
-            grouped[i] = keep.tile([P, n, PACK], BF16, name="grouped%d" % i, align_bytes=64)
-            if i == len(PIECES) - 1:
-                nc.vector.tensor_scalar(grouped[i][:], prod[i][:].rearrange("p t e -> p e t"), -1.0, None, ALU.mult)
-            else:
-                nc.scalar.activation(
-                    grouped[i][:].rearrange("p (c i) t -> p c t i", i=4),
-                    prod[i][:].rearrange("p t (c i) -> p c t i", i=4),
-                    COPY,
-                    scale=-1.0,
-                )
+        def gather_all(e0, e1):
+            for t in range(PACK):
+                gather(t, e0, e1)
 
-        def quantise(i):
-            e0, n = PIECES[i]
-            nc.vector.quantize_mx(
-                out=codes[:, e0 : e0 + n].bitcast(E5M2X4),
-                scales=plane[:, e0 : e0 + n],
-                in_=grouped[i][:].rearrange("p e t -> p (e t)"),
+        def round_on_scalar(e0, e1):
+            nc.scalar.activation(
+                grouped[:, e0:e1, :].rearrange("p (c i) t -> p c t i", i=4),
+                cut(prod, 0, PACK, e0, e1).rearrange("p t (c i) -> p c t i", i=4),
+                COPY,
+                scale=-1.0,
             )
 
-        def multiply(m, e0, keep0, keep1, on_vector):
+        def quantise(e0, e1, values):
+            nc.vector.quantize_mx(
+                out=codes[:, e0:e1].bitcast(E5M2X4),
+                scales=plane[:, e0:e1],
+                in_=values.rearrange("p e t -> p (e t)"),
+            )
+
+        def multiply(m, e0, keep0, keep1):
             acc = psum.tile([P, N_TILE], F32, name="acc%d" % (banks.pop(0)))
             nc.tensor.matmul_mx(
                 out=acc[:],
@@ -112,90 +122,64 @@ def tile_attend_gmp_sig_kernel(tc, dyT, hE, w_words, w_scales, offs, offs2, out)
                 start=True,
                 stop=True,
             )
-            if on_vector:
-                nc.vector.tensor_copy(dm[m][:, keep0:keep1], acc[:, keep0 - e0 : keep1 - e0])
-            else:
-                nc.scalar.copy(dm[m][:, keep0:keep1], acc[:, keep0 - e0 : keep1 - e0])
+            nc.scalar.copy(dm[m][:, keep0:keep1], acc[:, keep0 - e0 : keep1 - e0])
 
         def multiply_chunk(c):
             for m in range(2):
-                multiply(m, c * N_TILE, c * N_TILE, (c + 1) * N_TILE, False)
+                multiply(m, c * N_TILE, c * N_TILE, (c + 1) * N_TILE)
 
-        banks = [0, 1, 2, 3, 4, 5, 6, 7, 0]
+        banks = [0, 1, 2, 3, 4, 5, 6, 7]
 
-        slope(0, 0, 1)
+        def finish(e0, e1):
+            round_on_scalar(e0, e1)
+            quantise(e0, e1, grouped[:, e0:e1, :])
+
+        slope(0, 1, 0, 512)
         for t in range(PACK):
             if t + 1 < PACK:
-                slope(0, t + 1, t + 2)
+                slope(t + 1, t + 2, 0, 512)
             else:
-                slope(1, 0, PACK)
-            gather(0, t)
-        round_piece(0)
+                slope(0, PACK, 512, 1024)
+            gather(t, 0, 512)
+        finish(0, 512)
         for t in range(PACK):
-            gather(1, t)
+            gather(t, 512, 1024)
             if t == 1:
-                slope(2, 0, PACK)
-            if t == 2:
-                quantise(0)
-                multiply_chunk(0)
-        round_piece(1)
-        for t in range(PACK):
-            gather(2, t)
-        round_piece(2)
-        slope(3, 0, PACK)
-        quantise(1)
+                slope(0, PACK, 1024, 1536)
+        finish(512, 1024)
+        multiply_chunk(0)
+        gather_all(1024, 1536)
+        finish(1024, 1536)
         multiply_chunk(1)
-        for t in range(PACK):
-            gather(3, t)
-        round_piece(3)
-        quantise(2)
-        for t in range(PACK):
-            gather(4, t)
-        round_piece(4)
+        slope(0, 2, 1536, 2048)
+        slope(2, PACK, 1536, 2048)
+        gather_all(1536, 1792)
+        finish(1536, 1792)
+        gather_all(1792, 1920)
+        finish(1792, 1920)
         multiply_chunk(2)
-        quantise(3)
-        for t in range(PACK):
-            gather(5, t)
-        quantise(4)
-        round_piece(5)
-        multiply(0, 1408, 1536, 1920, False)
-        quantise(5)
-        multiply(0, 1536, 1920, 2048, True)
-        multiply(1, 1536, 1536, 2048, False)
+        gather_all(1920, 2048)
+        nc.vector.tensor_scalar(grouped_last[:], prod[1920][:].rearrange("p t e -> p e t"), -1.0, None, ALU.mult)
+        quantise(1920, 2048, grouped_last[:])
+        multiply_chunk(3)
 
-        picked = {}
+        def pick(m, s0, s1):
+            picked = keep.tile([P, s1 - s0], F32, name="picked%d_%d" % (m, s0))
+            nc.vector.tensor_copy(picked[:], dm[m][:].indirect(src[:, s0 // 16 : s1 // 16]))
+            return picked[:].rearrange("p (x j) -> p x j", j=K)
 
-        def pick(i):
-            m, s0, n = SUM_PIECES[i]
-            picked[i] = keep.tile([P, n], F32, name="picked%d" % i)
-            nc.vector.tensor_copy(picked[i][:], dm[m][:].indirect(src[:, s0 // 16 : (s0 + n) // 16]))
-
-        pairs = {}
-
-        def add_pairs(i, eng):
-            m, s0, n = SUM_PIECES[i]
-            g = picked[i][:].rearrange("p (x j) -> p x j", j=K)
-            pairs[i] = keep.tile([P, n // K, 2], F32, name="pairs%d" % i)
-            eng.tensor_tensor(pairs[i][:], g[:, :, 0:2], g[:, :, 2:4], ALU.add)
-
-        def add_last(i, eng):
-            m, s0, n = SUM_PIECES[i]
-            res = keep.tile([P, n // K], F32, name="res%d" % i)
-            eng.tensor_tensor(res[:], pairs[i][:, :, 0], pairs[i][:, :, 1], ALU.add)
-            nc.sync.dma_start(out[m * P : (m + 1) * P, s0 // K : (s0 + n) // K], res[:])
-
-        def reduce_piece(i):
-            m, s0, n = SUM_PIECES[i]
-            res = keep.tile([P, n // K], F32, name="res%d" % i)
-            nc.vector.tensor_reduce(res[:], picked[i][:].rearrange("p (x j) -> p x j", j=K), mybir.AxisListType.X, ALU.add)
-            nc.sync.dma_start(out[m * P : (m + 1) * P, s0 // K : (s0 + n) // K], res[:])
-
-        last = len(SUM_PIECES) - 1
-        for i in range(last + 1):
-            pick(i)
-            if i < last - 1:
-                add_pairs(i, nc.gpsimd)
-                add_last(i, nc.gpsimd)
-        add_pairs(last - 1, nc.vector)
-        reduce_piece(last)
-        add_last(last - 1, nc.vector)
+        for m, s0, s1 in [(0, 0, 1024), (0, 1024, 2048), (1, 0, 1024), (1, 1024, 1536)]:
+            nodes = (s1 - s0) // K
+            pairs = keep.tile([P, nodes, 2], F32, name="pairs%d_%d" % (m, s0))
+            for a in range(s0, s1, 512):
+                g = pick(m, a, a + 512)
+                x0 = (a - s0) // K
+                nc.gpsimd.tensor_tensor(pairs[:, x0 : x0 + 128, :], g[:, :, 0:2], g[:, :, 2:4], ALU.add)
+            res = keep.tile([P, nodes], F32, name="res%d_%d" % (m, s0))
+            nc.gpsimd.tensor_tensor(res[:], pairs[:, :, 0], pairs[:, :, 1], ALU.add)
+            nc.sync.dma_start(out[m * P : (m + 1) * P, s0 // K : s1 // K], res[:])
+        tail = keep.tile([P, 128], F32, name="tail")
+        last = [pick(1, 1536, 1792), pick(1, 1792, 2048)]
+        for i in range(2):
+            nc.vector.tensor_reduce(tail[:, 64 * i : 64 * (i + 1)], last[i], mybir.AxisListType.X, ALU.add)
+        nc.sync.dma_start(out[P : 2 * P, V - 128 : V], tail[:])

@@ -18,10 +18,15 @@ COPY = mybir.ActivationFunctionType.Copy
 
 P = 128
 PACK = 4
-N_TILE = 512
-LOADS = [(0, 512), (512, 1024), (1024, 1536), (1536, 2048)]
-PIECES = [(0, 512), (512, 1024), (1024, 1536), (1536, 1792), (1792, 1920), (1920, 2048)]
-WINDOW = 512 + 32
+PER_COLUMN = 16
+CHUNK = 512
+CHUNKS = [(e0, e0 + CHUNK) for e0 in range(0, E, CHUNK)]
+PIECES = CHUNKS[:-1] + [(1536, 1792), (1792, 1920), (1920, 2048)]
+DY_WINDOW = V + 32
+RUN = 4
+PICK = 512
+GPSIMD_SUMS = [(0, 0, 1024), (0, 1024, 2048), (1, 0, 1024), (1, 1024, 1536)]
+VECTOR_SUMS = [(1536, 1792), (1792, 2048)]
 
 
 def tile_attend_gmp_sig_kernel(tc, dyT, hE, w_words, w_scales, offs, offs2, out):
@@ -30,156 +35,154 @@ def tile_attend_gmp_sig_kernel(tc, dyT, hE, w_words, w_scales, offs, offs2, out)
         keep = ctx.enter_context(tc.tile_pool(name="keep", bufs=1))
         psum = ctx.enter_context(tc.psum_pool(name="psum", bufs=1))
 
-        dst = keep.tile([P, E // 16], U16, name="dst")
-        src = keep.tile([P, E // 16], U16, name="src")
-        dy = [keep.tile([P, WINDOW], F32, name="dy%d" % t) for t in range(PACK)]
-        h = {e0: keep.tile([P, PACK, e1 - e0], F32, name="h%d" % e0) for e0, e1 in LOADS}
-        u = {e0: keep.tile([P, PACK, e1 - e0], F32, name="u%d" % e0) for e0, e1 in LOADS}
-        prod = {e0: keep.tile([P, PACK, e1 - e0], F32, name="prod%d" % e0) for e0, e1 in PIECES}
+        dst = keep.tile([P, E // PER_COLUMN], U16, name="dst")
+        src = keep.tile([P, E // PER_COLUMN], U16, name="src")
+        dy = [keep.tile([P, DY_WINDOW], F32, name="dy%d" % t) for t in range(PACK)]
+        h = {e0: keep.tile([P, PACK, e1 - e0], F32, name="h%d" % e0) for e0, e1 in CHUNKS}
+        neg_slope = {e0: keep.tile([P, PACK, e1 - e0], F32, name="neg_slope%d" % e0) for e0, e1 in CHUNKS}
+        neg_dz = {e0: keep.tile([P, PACK, e1 - e0], F32, name="neg_dz%d" % e0) for e0, e1 in PIECES}
+        last_e0, last_e1 = PIECES[-1]
+        grouped = keep.tile([P, E, PACK], BF16, name="grouped", align_bytes=64)
+        grouped_last = keep.tile([P, last_e1 - last_e0, PACK], BF16, name="grouped_last", align_bytes=64)
+        w_codes = keep.tile([P, D], U32, name="w_codes", align_bytes=64)
+        w_scale = keep.tile([P, D], U8, name="w_scale", align_bytes=64)
+        dz_codes = keep.tile([P, E], U32, name="dz_codes", align_bytes=64)
+        dz_scale = keep.tile([P, E], U8, name="dz_scale", align_bytes=64)
+        dm = [keep.tile([P, E], F32, name="dm%d" % half) for half in range(D // P)]
 
         def cut(tiles, t0, t1, e0, e1):
-            base = max(b for b in tiles if b <= e0)
+            base = max(first for first in tiles if first <= e0)
             return tiles[base][:, t0:t1, e0 - base : e1 - base]
-
-        grouped = keep.tile([P, E, PACK], BF16, name="grouped", align_bytes=64)
-        grouped_last = keep.tile([P, 128, PACK], BF16, name="grouped_last", align_bytes=64)
-        w_codes = keep.tile([P, D], U32, name="w_codes", align_bytes=64)
-        w_plane = keep.tile([P, D], U8, name="w_plane", align_bytes=64)
-        codes = keep.tile([P, E], U32, name="codes", align_bytes=64)
-        plane = keep.tile([P, E], U8, name="plane", align_bytes=64)
-        dm = [keep.tile([P, E], F32, name="dm%d" % m) for m in range(2)]
 
         dy_rows = dyT.rearrange("(p t) x -> t p x", t=PACK)
         h_rows = hE.rearrange("(p t) e -> p t e", t=PACK)
 
         for t in range(PACK):
             nc.gpsimd.memset(dy[t][:, V:], 0.0)
-        nc.gpsimd.memset(w_plane[:].bitcast(I32), 0)
+        nc.gpsimd.memset(w_scale[:].bitcast(I32), 0)
 
-        def load_h(t0, t1, e0, e1):
+        def load_h(t0, t1, chunk):
+            e0, e1 = CHUNKS[chunk]
             nc.sync.dma_start(cut(h, t0, t1, e0, e1), h_rows[:, t0:t1, e0:e1])
 
-        def load_dy(t):
+        load_h(0, 1, 0)
+        for t in range(PACK):
+            if t + 1 < PACK:
+                load_h(t + 1, t + 2, 0)
+            else:
+                load_h(0, 2, 1)
+            if t == 0:
+                nc.sync.dma_start(dst[:], offs)
             nc.sync.dma_start(dy[t][:, :V], dy_rows[t])
-
-        load_h(0, 1, 0, 512)
-        load_h(1, 2, 0, 512)
-        nc.sync.dma_start(dst[:], offs)
-        load_dy(0)
-        load_h(2, 3, 0, 512)
-        load_dy(1)
-        load_h(3, 4, 0, 512)
-        load_dy(2)
-        load_h(0, PACK, 512, 1024)
-        load_dy(3)
-        load_h(0, PACK, 1024, 1536)
-        load_h(0, PACK, 1536, 2048)
+        load_h(2, PACK, 1)
+        load_h(0, PACK, 2)
+        load_h(0, PACK, 3)
         nc.sync.dma_start(w_codes[:].bitcast(I32), w_words[0].rearrange("p d r -> p (d r)").bitcast(I32))
         for q in range(4):
-            nc.sync.dma_start(w_plane[32 * q : 32 * q + 4, :].bitcast(I32), w_scales[0, 4 * q : 4 * q + 4, :].bitcast(I32))
+            nc.sync.dma_start(
+                w_scale[32 * q : 32 * q + 4, :].bitcast(I32), w_scales[0, 4 * q : 4 * q + 4, :].bitcast(I32)
+            )
         nc.sync.dma_start(src[:], offs2)
 
-        def slope(t0, t1, e0, e1):
-            nc.vector.scalar_tensor_tensor(
-                cut(u, t0, t1, e0, e1), cut(h, t0, t1, e0, e1), 1.0, cut(h, t0, t1, e0, e1), ALU.subtract, ALU.mult
-            )
+        def slope(t0, t1, chunk):
+            e0, e1 = CHUNKS[chunk]
+            saved = cut(h, t0, t1, e0, e1)
+            nc.vector.scalar_tensor_tensor(cut(neg_slope, t0, t1, e0, e1), saved, 1.0, saved, ALU.subtract, ALU.mult)
 
         def gather(t, e0, e1):
             nc.vector.tensor_tensor(
-                cut(prod, t, t + 1, e0, e1)[:, 0, :],
-                dy[t][:].indirect(dst[:, e0 // 16 : e1 // 16]),
-                cut(u, t, t + 1, e0, e1)[:, 0, :],
+                cut(neg_dz, t, t + 1, e0, e1)[:, 0, :],
+                dy[t][:].indirect(dst[:, e0 // PER_COLUMN : e1 // PER_COLUMN]),
+                cut(neg_slope, t, t + 1, e0, e1)[:, 0, :],
                 ALU.mult,
             )
 
-        def gather_all(e0, e1):
+        def gather_piece(e0, e1):
             for t in range(PACK):
                 gather(t, e0, e1)
 
-        def round_on_scalar(e0, e1):
-            nc.scalar.activation(
-                grouped[:, e0:e1, :].rearrange("p (c i) t -> p c t i", i=4),
-                cut(prod, 0, PACK, e0, e1).rearrange("p t (c i) -> p c t i", i=4),
-                COPY,
-                scale=-1.0,
-            )
-
         def quantise(e0, e1, values):
             nc.vector.quantize_mx(
-                out=codes[:, e0:e1].bitcast(E5M2X4),
-                scales=plane[:, e0:e1],
+                out=dz_codes[:, e0:e1].bitcast(E5M2X4),
+                scales=dz_scale[:, e0:e1],
                 in_=values.rearrange("p e t -> p (e t)"),
             )
 
-        def multiply(m, e0, keep0, keep1):
-            acc = psum.tile([P, N_TILE], F32, name="acc%d" % (banks.pop(0)))
-            nc.tensor.matmul_mx(
-                out=acc[:],
-                lhsT=w_codes[:, m * P : (m + 1) * P].bitcast(E4M3X4),
-                lhsT_scale=w_plane[:, m * P : (m + 1) * P],
-                rhs=codes[:, e0 : e0 + N_TILE].bitcast(E5M2X4),
-                rhs_scale=plane[:, e0 : e0 + N_TILE],
-                start=True,
-                stop=True,
+        def round_and_quantise(e0, e1):
+            nc.scalar.activation(
+                grouped[:, e0:e1, :].rearrange("p (c i) t -> p c t i", i=RUN),
+                cut(neg_dz, 0, PACK, e0, e1).rearrange("p t (c i) -> p c t i", i=RUN),
+                COPY,
+                scale=-1.0,
             )
-            nc.scalar.copy(dm[m][:, keep0:keep1], acc[:, keep0 - e0 : keep1 - e0])
-
-        def multiply_chunk(c):
-            for m in range(2):
-                multiply(m, c * N_TILE, c * N_TILE, (c + 1) * N_TILE)
-
-        banks = [0, 1, 2, 3, 4, 5, 6, 7]
-
-        def finish(e0, e1):
-            round_on_scalar(e0, e1)
             quantise(e0, e1, grouped[:, e0:e1, :])
 
-        slope(0, 1, 0, 512)
+        def multiply(chunk):
+            e0, e1 = CHUNKS[chunk]
+            for half in range(D // P):
+                d_cols = slice(half * P, (half + 1) * P)
+                acc = psum.tile([P, CHUNK], F32, name="acc%d" % (chunk * (D // P) + half))
+                nc.tensor.matmul_mx(
+                    out=acc[:],
+                    lhsT=w_codes[:, d_cols].bitcast(E4M3X4),
+                    lhsT_scale=w_scale[:, d_cols],
+                    rhs=dz_codes[:, e0:e1].bitcast(E5M2X4),
+                    rhs_scale=dz_scale[:, e0:e1],
+                    start=True,
+                    stop=True,
+                )
+                nc.scalar.copy(dm[half][:, e0:e1], acc[:])
+
+        slope(0, 1, 0)
         for t in range(PACK):
             if t + 1 < PACK:
-                slope(t + 1, t + 2, 0, 512)
+                slope(t + 1, t + 2, 0)
             else:
-                slope(0, PACK, 512, 1024)
-            gather(t, 0, 512)
-        finish(0, 512)
+                slope(0, 2, 1)
+            gather(t, *PIECES[0])
+        round_and_quantise(*PIECES[0])
+        slope(2, PACK, 1)
         for t in range(PACK):
-            gather(t, 512, 1024)
+            gather(t, *PIECES[1])
             if t == 1:
-                slope(0, PACK, 1024, 1536)
-        finish(512, 1024)
-        multiply_chunk(0)
-        gather_all(1024, 1536)
-        finish(1024, 1536)
-        multiply_chunk(1)
-        slope(0, 2, 1536, 2048)
-        slope(2, PACK, 1536, 2048)
-        gather_all(1536, 1792)
-        finish(1536, 1792)
-        gather_all(1792, 1920)
-        finish(1792, 1920)
-        multiply_chunk(2)
-        gather_all(1920, 2048)
-        nc.vector.tensor_scalar(grouped_last[:], prod[1920][:].rearrange("p t e -> p e t"), -1.0, None, ALU.mult)
-        quantise(1920, 2048, grouped_last[:])
-        multiply_chunk(3)
+                slope(0, PACK, 2)
+        round_and_quantise(*PIECES[1])
+        multiply(0)
+        gather_piece(*PIECES[2])
+        round_and_quantise(*PIECES[2])
+        multiply(1)
+        slope(0, 2, 3)
+        slope(2, PACK, 3)
+        for e0, e1 in PIECES[3:5]:
+            gather_piece(e0, e1)
+            round_and_quantise(e0, e1)
+        multiply(2)
+        gather_piece(last_e0, last_e1)
+        nc.vector.tensor_scalar(grouped_last[:], neg_dz[last_e0][:].rearrange("p t e -> p e t"), -1.0, None, ALU.mult)
+        quantise(last_e0, last_e1, grouped_last[:])
+        multiply(3)
 
-        def pick(m, s0, s1):
-            picked = keep.tile([P, s1 - s0], F32, name="picked%d_%d" % (m, s0))
-            nc.vector.tensor_copy(picked[:], dm[m][:].indirect(src[:, s0 // 16 : s1 // 16]))
+        def pick(half, s0, s1):
+            picked = keep.tile([P, s1 - s0], F32, name="picked%d_%d" % (half, s0))
+            nc.vector.tensor_copy(picked[:], dm[half][:].indirect(src[:, s0 // PER_COLUMN : s1 // PER_COLUMN]))
             return picked[:].rearrange("p (x j) -> p x j", j=K)
 
-        for m, s0, s1 in [(0, 0, 1024), (0, 1024, 2048), (1, 0, 1024), (1, 1024, 1536)]:
+        for half, s0, s1 in GPSIMD_SUMS:
             nodes = (s1 - s0) // K
-            pairs = keep.tile([P, nodes, 2], F32, name="pairs%d_%d" % (m, s0))
-            for a in range(s0, s1, 512):
-                g = pick(m, a, a + 512)
-                x0 = (a - s0) // K
-                nc.gpsimd.tensor_tensor(pairs[:, x0 : x0 + 128, :], g[:, :, 0:2], g[:, :, 2:4], ALU.add)
-            res = keep.tile([P, nodes], F32, name="res%d_%d" % (m, s0))
-            nc.gpsimd.tensor_tensor(res[:], pairs[:, :, 0], pairs[:, :, 1], ALU.add)
-            nc.sync.dma_start(out[m * P : (m + 1) * P, s0 // K : s1 // K], res[:])
-        tail = keep.tile([P, 128], F32, name="tail")
-        last = [pick(1, 1536, 1792), pick(1, 1792, 2048)]
-        for i in range(2):
-            nc.vector.tensor_reduce(tail[:, 64 * i : 64 * (i + 1)], last[i], mybir.AxisListType.X, ALU.add)
-        nc.sync.dma_start(out[P : 2 * P, V - 128 : V], tail[:])
+            pairs = keep.tile([P, nodes, 2], F32, name="pairs%d_%d" % (half, s0))
+            for first in range(s0, s1, PICK):
+                picked = pick(half, first, first + PICK)
+                x0 = (first - s0) // K
+                nc.gpsimd.tensor_tensor(pairs[:, x0 : x0 + PICK // K, :], picked[:, :, 0:2], picked[:, :, 2:4], ALU.add)
+            sums = keep.tile([P, nodes], F32, name="sums%d_%d" % (half, s0))
+            nc.gpsimd.tensor_tensor(sums[:], pairs[:, :, 0], pairs[:, :, 1], ALU.add)
+            nc.sync.dma_start(out[half * P : (half + 1) * P, s0 // K : s1 // K], sums[:])
+
+        tail_x0 = VECTOR_SUMS[0][0] // K
+        tail_sums = keep.tile([P, V - tail_x0], F32, name="tail_sums")
+        tail_picked = [pick(1, s0, s1) for s0, s1 in VECTOR_SUMS]
+        for (s0, s1), picked in zip(VECTOR_SUMS, tail_picked):
+            nc.vector.tensor_reduce(
+                tail_sums[:, s0 // K - tail_x0 : s1 // K - tail_x0], picked, mybir.AxisListType.X, ALU.add
+            )
+        nc.sync.dma_start(out[P : 2 * P, tail_x0:V], tail_sums[:])

@@ -1,6 +1,7 @@
 from contextlib import ExitStack
 
 import concourse.mybir as mybir
+from concourse.masks import make_identity
 
 V, K, E, D, DV = 512, 4, 2048, 256, 512
 FLOPS = 2 * DV * D * E
@@ -19,11 +20,18 @@ COPY = mybir.ActivationFunctionType.Copy
 P = 128
 PACK = 4
 PER_COLUMN = 16
-CHUNK = 512
-CHUNKS = [(e0, e0 + CHUNK) for e0 in range(0, E, CHUNK)]
-PIECES = CHUNKS[:-1] + [(1536, 1792), (1792, 1920), (1920, 2048)]
-DY_WINDOW = V + 32
+BANK = 512
+BANKS = 8
+HEAD = 128
+MAIN = 1408
+SIDE = [(1408, 1664), (1664, 1920)]
+LAST = (1920, 2048)
+BLOCKS = (MAIN - HEAD) // P
+DY_WINDOW = MAIN + 32
 RUN = 4
+LOADS = [[128, 384, 768, 1408], [128, 768, 1408], [128, 1408], [128, 1408]]
+GATHERS = [[0, 128, 384, 768, 1408], [0, 768, 1408], [0, 1408], [0, 1152, 1408]]
+ORDER = [0, 1, 2, 3, 4, 5, 6, 8, 7, 9]
 PICK = 512
 GPSIMD_SUMS = [(0, 0, 1024), (0, 1024, 2048), (1, 0, 1024), (1, 1024, 1536)]
 VECTOR_SUMS = [(1536, 1792), (1792, 2048)]
@@ -35,48 +43,48 @@ def tile_attend_gmp_sig_kernel(tc, dyT, hE, w_words, w_scales, offs, offs2, out)
         keep = ctx.enter_context(tc.tile_pool(name="keep", bufs=1))
         psum = ctx.enter_context(tc.psum_pool(name="psum", bufs=1))
 
+        side0, side1 = SIDE[0][0], SIDE[-1][1]
+        last0, last1 = LAST
         dst = keep.tile([P, E // PER_COLUMN], U16, name="dst")
         src = keep.tile([P, E // PER_COLUMN], U16, name="src")
         dy = [keep.tile([P, DY_WINDOW], F32, name="dy%d" % t) for t in range(PACK)]
-        h = {e0: keep.tile([P, PACK, e1 - e0], F32, name="h%d" % e0) for e0, e1 in CHUNKS}
-        neg_slope = {e0: keep.tile([P, PACK, e1 - e0], F32, name="neg_slope%d" % e0) for e0, e1 in CHUNKS}
-        neg_dz = {e0: keep.tile([P, PACK, e1 - e0], F32, name="neg_dz%d" % e0) for e0, e1 in PIECES}
-        last_e0, last_e1 = PIECES[-1]
-        grouped = keep.tile([P, E, PACK], BF16, name="grouped", align_bytes=64)
-        grouped_last = keep.tile([P, last_e1 - last_e0, PACK], BF16, name="grouped_last", align_bytes=64)
+        ident = keep.tile([P, P], F32, name="ident")
+        h_head = keep.tile([P, PACK, HEAD], F32, name="h_head")
+        factor = [keep.tile([P, MAIN], F32, name="factor%d" % t, tag="factor%d" % t) for t in range(PACK)]
+        h_side = keep.tile([P, PACK, side1 - side0], F32, name="h_side")
+        h_last = keep.tile([P, PACK, last1 - last0], F32, name="h_last")
+        ident_first = keep.tile([P, P], F32, name="ident_first", tag="rest")
+        rest_turned = keep.tile([P, PACK * BLOCKS * P], F32, name="rest_turned", tag="turned", align_bytes=64)
+        product = keep.tile([P, PACK, MAIN], F32, name="product", tag="product", align_bytes=64)
+        grouped = keep.tile([P, last0, PACK], BF16, name="grouped", align_bytes=64)
         w_codes = keep.tile([P, D], U32, name="w_codes", align_bytes=64)
         w_scale = keep.tile([P, D], U8, name="w_scale", align_bytes=64)
         dz_codes = keep.tile([P, E], U32, name="dz_codes", align_bytes=64)
         dz_scale = keep.tile([P, E], U8, name="dz_scale", align_bytes=64)
         dm = [keep.tile([P, E], F32, name="dm%d" % half) for half in range(D // P)]
-
-        def cut(tiles, t0, t1, e0, e1):
-            base = max(first for first in tiles if first <= e0)
-            return tiles[base][:, t0:t1, e0 - base : e1 - base]
+        bank = [psum.tile([P, BANK], F32, name="bank%d" % b) for b in range(BANKS)]
 
         dy_rows = dyT.rearrange("(p t) x -> t p x", t=PACK)
         h_rows = hE.rearrange("(p t) e -> p t e", t=PACK)
 
-        for t in range(PACK):
+        nc.gpsimd.memset(dy[0][:, V:], 0.0)
+        make_identity(nc, ident_first[:])
+        make_identity(nc, ident[:])
+        for t in range(1, PACK):
             nc.gpsimd.memset(dy[t][:, V:], 0.0)
         nc.gpsimd.memset(w_scale[:].bitcast(I32), 0)
 
-        def load_h(t0, t1, chunk):
-            e0, e1 = CHUNKS[chunk]
-            nc.sync.dma_start(cut(h, t0, t1, e0, e1), h_rows[:, t0:t1, e0:e1])
-
-        load_h(0, 1, 0)
+        nc.sync.dma_start(h_head[:], h_rows[:, :, :HEAD])
+        nc.sync.dma_start(dst[:], offs)
         for t in range(PACK):
-            if t + 1 < PACK:
-                load_h(t + 1, t + 2, 0)
-            else:
-                load_h(0, 2, 1)
-            if t == 0:
-                nc.sync.dma_start(dst[:], offs)
-            nc.sync.dma_start(dy[t][:, :V], dy_rows[t])
-        load_h(2, PACK, 1)
-        load_h(0, PACK, 2)
-        load_h(0, PACK, 3)
+            if t < 2:
+                nc.sync.dma_start(dy[t][:, :V], dy_rows[t])
+            for e0, e1 in zip(LOADS[t], LOADS[t][1:]):
+                nc.sync.dma_start(factor[t][:, e0:e1], h_rows[:, t, e0:e1])
+            if t >= 2:
+                nc.sync.dma_start(dy[t][:, :V], dy_rows[t])
+        nc.sync.dma_start(h_side[:], h_rows[:, :, side0:side1])
+        nc.sync.dma_start(h_last[:], h_rows[:, :, last0:last1])
         nc.sync.dma_start(w_codes[:].bitcast(I32), w_words[0].rearrange("p d r -> p (d r)").bitcast(I32))
         for q in range(4):
             nc.sync.dma_start(
@@ -84,22 +92,16 @@ def tile_attend_gmp_sig_kernel(tc, dyT, hE, w_words, w_scales, offs, offs2, out)
             )
         nc.sync.dma_start(src[:], offs2)
 
-        def slope(t0, t1, chunk):
-            e0, e1 = CHUNKS[chunk]
-            saved = cut(h, t0, t1, e0, e1)
-            nc.vector.scalar_tensor_tensor(cut(neg_slope, t0, t1, e0, e1), saved, 1.0, saved, ALU.subtract, ALU.mult)
-
-        def gather(t, e0, e1):
+        def gather(target, t, e0, e1, plain):
             nc.vector.tensor_tensor(
-                cut(neg_dz, t, t + 1, e0, e1)[:, 0, :],
-                dy[t][:].indirect(dst[:, e0 // PER_COLUMN : e1 // PER_COLUMN]),
-                cut(neg_slope, t, t + 1, e0, e1)[:, 0, :],
-                ALU.mult,
+                target, dy[t][:].indirect(dst[:, e0 // PER_COLUMN : e1 // PER_COLUMN]), plain, ALU.mult
             )
 
-        def gather_piece(e0, e1):
-            for t in range(PACK):
-                gather(t, e0, e1)
+        def as_runs_out(values):
+            return values.rearrange("p (c i) t -> p c t i", i=RUN)
+
+        def as_runs_in(values):
+            return values.rearrange("p t (c i) -> p c t i", i=RUN)
 
         def quantise(e0, e1, values):
             nc.vector.quantize_mx(
@@ -108,59 +110,104 @@ def tile_attend_gmp_sig_kernel(tc, dyT, hE, w_words, w_scales, offs, offs2, out)
                 in_=values.rearrange("p e t -> p (e t)"),
             )
 
-        def round_and_quantise(e0, e1):
-            nc.scalar.activation(
-                grouped[:, e0:e1, :].rearrange("p (c i) t -> p c t i", i=RUN),
-                cut(neg_dz, 0, PACK, e0, e1).rearrange("p t (c i) -> p c t i", i=RUN),
-                COPY,
-                scale=-1.0,
+        def multiply(half, e0, acc, new0):
+            d_cols = slice(half * P, (half + 1) * P)
+            nc.tensor.matmul_mx(
+                out=acc[:],
+                lhsT=w_codes[:, d_cols].bitcast(E4M3X4),
+                lhsT_scale=w_scale[:, d_cols],
+                rhs=dz_codes[:, e0 : e0 + BANK].bitcast(E5M2X4),
+                rhs_scale=dz_scale[:, e0 : e0 + BANK],
+                start=True,
+                stop=True,
             )
-            quantise(e0, e1, grouped[:, e0:e1, :])
+            nc.scalar.copy(dm[half][:, new0 : e0 + BANK], acc[:, new0 - e0 :])
 
-        def multiply(chunk):
-            e0, e1 = CHUNKS[chunk]
-            for half in range(D // P):
-                d_cols = slice(half * P, (half + 1) * P)
-                acc = psum.tile([P, CHUNK], F32, name="acc%d" % (chunk * (D // P) + half))
-                nc.tensor.matmul_mx(
-                    out=acc[:],
-                    lhsT=w_codes[:, d_cols].bitcast(E4M3X4),
-                    lhsT_scale=w_scale[:, d_cols],
-                    rhs=dz_codes[:, e0:e1].bitcast(E5M2X4),
-                    rhs_scale=dz_scale[:, e0:e1],
-                    start=True,
-                    stop=True,
-                )
-                nc.scalar.copy(dm[half][:, e0:e1], acc[:])
+        for t in range(PACK):
+            nc.vector.scalar_tensor_tensor(
+                factor[t][:, :HEAD], h_head[:, t, :], 1.0, h_head[:, t, :], ALU.subtract, ALU.mult
+            )
+        for t in range(PACK):
+            for e0, e1 in zip(GATHERS[t], GATHERS[t][1:]):
+                gather(product[:, t, e0:e1], t, e0, e1, factor[t][:, e0:e1])
 
-        slope(0, 1, 0)
+        home = {k: bank[place % BANKS] for place, k in enumerate(ORDER)}
+        staging = bank[BANKS - 2 :]
+        early = ORDER[: BANKS - 2]
+
+        def turn_back(t, k):
+            i = t * BLOCKS + k
+            nc.tensor.transpose(home[k][:, t * P : (t + 1) * P], rest_turned[:, i * P : (i + 1) * P], ident[:])
+
+        groups = PACK * BLOCKS // 4
+        for g in range(groups + 1):
+            if g < groups:
+                stage = staging[g % 2]
+                for slot in range(4):
+                    t, k = divmod(4 * g + slot, BLOCKS)
+                    e0 = HEAD + k * P
+                    nc.tensor.transpose(stage[:, slot * P : (slot + 1) * P], factor[t][:, e0 : e0 + P], ident_first[:])
+                nc.scalar.activation(rest_turned[:, g * BANK : (g + 1) * BANK], stage[:], COPY, bias=1.0, scale=-1.0)
+            if g > 0:
+                for slot in range(4):
+                    t, k = divmod(4 * (g - 1) + slot, BLOCKS)
+                    if k in early:
+                        turn_back(t, k)
+        for k in ORDER[BANKS - 2 : BANKS]:
+            for t in range(PACK):
+                turn_back(t, k)
+
+        rest = keep.tile([P, PACK * (last1 - side0)], F32, name="rest", tag="rest")
+        rest_side = rest[:, : PACK * (side1 - side0)].rearrange("p (t e) -> p t e", t=PACK)
+        rest_last = rest[:, PACK * (side1 - side0) :].rearrange("p (t e) -> p t e", t=PACK)
+        nc.scalar.activation(rest_side, h_side[:], COPY, bias=1.0, scale=-1.0)
+        nc.scalar.activation(rest_last, h_last[:], COPY, bias=1.0, scale=-1.0)
+        slope = keep.tile([P, PACK, side1 - side0], F32, name="slope", tag="factor%d" % (PACK - 1))
+        nc.gpsimd.tensor_tensor(slope[:], h_side[:], rest_side, ALU.mult)
+
+        for place, k in enumerate(ORDER):
+            e0 = HEAD + k * P
+            nc.vector.tensor_tensor(
+                as_runs_out(grouped[:, e0 : e0 + P, :]),
+                as_runs_in(product[:, :, e0 : e0 + P]),
+                as_runs_in(home[k][:].rearrange("p (t e) -> p t e", t=PACK)),
+                ALU.mult,
+            )
+            if place + BANKS < BLOCKS:
+                for t in range(PACK):
+                    turn_back(t, ORDER[place + BANKS])
+
+        grouped_head = keep.tile([P, HEAD, PACK], BF16, name="grouped_head", tag="turned", align_bytes=64)
+        nc.scalar.activation(as_runs_out(grouped_head[:]), as_runs_in(product[:, :, :HEAD]), COPY, scale=-1.0)
+        quantise(128, 1152, grouped[:, 128:1152, :])
+        quantise(0, HEAD, grouped_head[:])
+        multiply(0, 0, bank[2], 0)
+        multiply(0, 512, bank[3], 512)
+        multiply(1, 0, bank[4], 0)
+        multiply(1, 512, bank[5], 512)
+
+        late = keep.tile([P, PACK * (side1 - side0)], F32, name="late", tag="product", align_bytes=64)
+        for e0, e1 in SIDE:
+            dz = late[:, PACK * (e0 - side0) : PACK * (e1 - side0)].rearrange("p (t e) -> p t e", t=PACK)
+            for t in range(PACK):
+                gather(dz[:, t, :], t, e0, e1, slope[:, t, e0 - side0 : e1 - side0])
+            nc.scalar.activation(as_runs_out(grouped[:, e0:e1, :]), as_runs_in(dz), COPY)
+        quantise(1152, 1664, grouped[:, 1152:1664, :])
+        multiply(0, 1024, bank[6], 1024)
+        product_last = late[:, : PACK * (last1 - last0)].rearrange("p (t e) -> p t e", t=PACK)
         for t in range(PACK):
-            if t + 1 < PACK:
-                slope(t + 1, t + 2, 0)
-            else:
-                slope(0, 2, 1)
-            gather(t, *PIECES[0])
-        round_and_quantise(*PIECES[0])
-        slope(2, PACK, 1)
-        for t in range(PACK):
-            gather(t, *PIECES[1])
-            if t == 1:
-                slope(0, PACK, 2)
-        round_and_quantise(*PIECES[1])
-        multiply(0)
-        gather_piece(*PIECES[2])
-        round_and_quantise(*PIECES[2])
-        multiply(1)
-        slope(0, 2, 3)
-        slope(2, PACK, 3)
-        for e0, e1 in PIECES[3:5]:
-            gather_piece(e0, e1)
-            round_and_quantise(e0, e1)
-        multiply(2)
-        gather_piece(last_e0, last_e1)
-        nc.vector.tensor_scalar(grouped_last[:], neg_dz[last_e0][:].rearrange("p t e -> p e t"), -1.0, None, ALU.mult)
-        quantise(last_e0, last_e1, grouped_last[:])
-        multiply(3)
+            gather(product_last[:, t, :], t, last0, last1, h_last[:, t, :])
+        quantise(1664, 1920, grouped[:, 1664:1920, :])
+        multiply(0, 1408, bank[0], 1536)
+        second = PACK * (SIDE[1][0] - side0)
+        grouped_last = late[:, second : second + 2 * (last1 - last0)].bitcast(BF16).rearrange("p (e t) -> p e t", t=PACK)
+        nc.vector.tensor_tensor(
+            as_runs_out(grouped_last), as_runs_in(product_last), as_runs_in(rest_last), ALU.mult
+        )
+        quantise(last0, last1, grouped_last)
+        multiply(0, 1536, bank[1], 1920)
+        multiply(1, 1024, bank[7], 1024)
+        multiply(1, 1536, bank[2], 1536)
 
         def pick(half, s0, s1):
             picked = keep.tile([P, s1 - s0], F32, name="picked%d_%d" % (half, s0))

@@ -29,7 +29,8 @@ LAST = (1920, 2048)
 BLOCKS = (MAIN - HEAD) // P
 DY_WINDOW = MAIN + 32
 RUN = 4
-LOADS = [[128, 384, 768, 1408], [128, 768, 1408], [128, 1408], [128, 1408]]
+LOADS = [[128, 384, 768, 1408], [128, 768, 1408], [128, 1408], [128, 1152, 1408]]
+SPLIT = 1152
 GATHERS = [[0, 128, 384, 768, 1408], [0, 768, 1408], [0, 1408], [0, 1152, 1408]]
 ORDER = [0, 1, 2, 3, 4, 5, 6, 8, 7, 9]
 PICK = 512
@@ -50,9 +51,16 @@ def tile_attend_gmp_sig_kernel(tc, dyT, hE, w_words, w_scales, offs, offs2, out)
         dy = [keep.tile([P, DY_WINDOW], F32, name="dy%d" % t) for t in range(PACK)]
         ident = keep.tile([P, P], F32, name="ident")
         h_head = keep.tile([P, PACK, HEAD], F32, name="h_head")
-        factor = [keep.tile([P, MAIN], F32, name="factor%d" % t, tag="factor%d" % t) for t in range(PACK)]
-        h_side = keep.tile([P, PACK, side1 - side0], F32, name="h_side")
-        h_last = keep.tile([P, PACK, last1 - last0], F32, name="h_last")
+        front = [keep.tile([P, MAIN], F32, name="front%d" % t) for t in range(PACK - 1)]
+        front.append(keep.tile([P, SPLIT], F32, name="front_last", tag="gate"))
+        back_last = keep.tile([P, MAIN - SPLIT], F32, name="back_last")
+
+        def factor(t, e0, e1):
+            if t == PACK - 1 and e0 >= SPLIT:
+                return back_last[:, e0 - SPLIT : e1 - SPLIT]
+            return front[t][:, e0:e1]
+
+        h_side = keep.tile([P, PACK, E - side0], F32, name="h_side")
         ident_first = keep.tile([P, P], F32, name="ident_first", tag="rest")
         rest_turned = keep.tile([P, PACK * BLOCKS * P], F32, name="rest_turned", tag="turned", align_bytes=64)
         product = keep.tile([P, PACK, MAIN], F32, name="product", tag="product", align_bytes=64)
@@ -80,11 +88,12 @@ def tile_attend_gmp_sig_kernel(tc, dyT, hE, w_words, w_scales, offs, offs2, out)
             if t < 2:
                 nc.sync.dma_start(dy[t][:, :V], dy_rows[t])
             for e0, e1 in zip(LOADS[t], LOADS[t][1:]):
-                nc.sync.dma_start(factor[t][:, e0:e1], h_rows[:, t, e0:e1])
-            if t >= 2:
+                nc.sync.dma_start(factor(t, e0, e1), h_rows[:, t, e0:e1])
+            if t == 2:
                 nc.sync.dma_start(dy[t][:, :V], dy_rows[t])
-        nc.sync.dma_start(h_side[:], h_rows[:, :, side0:side1])
-        nc.sync.dma_start(h_last[:], h_rows[:, :, last0:last1])
+        nc.sync.dma_start(h_side[:, :2, :], h_rows[:, :2, side0:])
+        nc.sync.dma_start(dy[3][:, :V], dy_rows[3])
+        nc.sync.dma_start(h_side[:, 2:, :], h_rows[:, 2:, side0:])
         nc.sync.dma_start(w_codes[:].bitcast(I32), w_words[0].rearrange("p d r -> p (d r)").bitcast(I32))
         for q in range(4):
             nc.sync.dma_start(
@@ -97,11 +106,11 @@ def tile_attend_gmp_sig_kernel(tc, dyT, hE, w_words, w_scales, offs, offs2, out)
                 target, dy[t][:].indirect(dst[:, e0 // PER_COLUMN : e1 // PER_COLUMN]), plain, ALU.mult
             )
 
-        def as_runs_out(values):
-            return values.rearrange("p (c i) t -> p c t i", i=RUN)
+        def as_runs_out(values, run=RUN):
+            return values.rearrange("p (c i) t -> p c t i", i=run)
 
-        def as_runs_in(values):
-            return values.rearrange("p t (c i) -> p c t i", i=RUN)
+        def as_runs_in(values, run=RUN):
+            return values.rearrange("p t (c i) -> p c t i", i=run)
 
         def quantise(e0, e1, values):
             nc.vector.quantize_mx(
@@ -125,11 +134,11 @@ def tile_attend_gmp_sig_kernel(tc, dyT, hE, w_words, w_scales, offs, offs2, out)
 
         for t in range(PACK):
             nc.vector.scalar_tensor_tensor(
-                factor[t][:, :HEAD], h_head[:, t, :], 1.0, h_head[:, t, :], ALU.subtract, ALU.mult
+                factor(t, 0, HEAD), h_head[:, t, :], 1.0, h_head[:, t, :], ALU.subtract, ALU.mult
             )
         for t in range(PACK):
             for e0, e1 in zip(GATHERS[t], GATHERS[t][1:]):
-                gather(product[:, t, e0:e1], t, e0, e1, factor[t][:, e0:e1])
+                gather(product[:, t, e0:e1], t, e0, e1, factor(t, e0, e1))
 
         home = {k: bank[place % BANKS] for place, k in enumerate(ORDER)}
         staging = bank[BANKS - 2 :]
@@ -146,7 +155,7 @@ def tile_attend_gmp_sig_kernel(tc, dyT, hE, w_words, w_scales, offs, offs2, out)
                 for slot in range(4):
                     t, k = divmod(4 * g + slot, BLOCKS)
                     e0 = HEAD + k * P
-                    nc.tensor.transpose(stage[:, slot * P : (slot + 1) * P], factor[t][:, e0 : e0 + P], ident_first[:])
+                    nc.tensor.transpose(stage[:, slot * P : (slot + 1) * P], factor(t, e0, e0 + P), ident_first[:])
                 nc.scalar.activation(rest_turned[:, g * BANK : (g + 1) * BANK], stage[:], COPY, bias=1.0, scale=-1.0)
             if g > 0:
                 for slot in range(4):
@@ -157,20 +166,18 @@ def tile_attend_gmp_sig_kernel(tc, dyT, hE, w_words, w_scales, offs, offs2, out)
             for t in range(PACK):
                 turn_back(t, k)
 
-        rest = keep.tile([P, PACK * (last1 - side0)], F32, name="rest", tag="rest")
-        rest_side = rest[:, : PACK * (side1 - side0)].rearrange("p (t e) -> p t e", t=PACK)
-        rest_last = rest[:, PACK * (side1 - side0) :].rearrange("p (t e) -> p t e", t=PACK)
-        nc.scalar.activation(rest_side, h_side[:], COPY, bias=1.0, scale=-1.0)
-        nc.scalar.activation(rest_last, h_last[:], COPY, bias=1.0, scale=-1.0)
-        slope = keep.tile([P, PACK, side1 - side0], F32, name="slope", tag="factor%d" % (PACK - 1))
-        nc.gpsimd.tensor_tensor(slope[:], h_side[:], rest_side, ALU.mult)
+        rest_side = keep.tile([P, PACK, E - side0], F32, name="rest_side", tag="rest")
+        for t0 in (0, 2):
+            nc.scalar.activation(rest_side[:, t0 : t0 + 2, :], h_side[:, t0 : t0 + 2, :], COPY, bias=1.0, scale=-1.0)
+        slope = keep.tile([P, PACK, E - side0], F32, name="slope", tag="gate")
+        nc.gpsimd.tensor_tensor(slope[:], h_side[:], rest_side[:], ALU.mult)
 
         for place, k in enumerate(ORDER):
             e0 = HEAD + k * P
             nc.vector.tensor_tensor(
-                as_runs_out(grouped[:, e0 : e0 + P, :]),
-                as_runs_in(product[:, :, e0 : e0 + P]),
-                as_runs_in(home[k][:].rearrange("p (t e) -> p t e", t=PACK)),
+                as_runs_out(grouped[:, e0 : e0 + P, :], 2),
+                as_runs_in(product[:, :, e0 : e0 + P], 2),
+                as_runs_in(home[k][:].rearrange("p (t e) -> p t e", t=PACK), 2),
                 ALU.mult,
             )
             if place + BANKS < BLOCKS:
@@ -196,14 +203,12 @@ def tile_attend_gmp_sig_kernel(tc, dyT, hE, w_words, w_scales, offs, offs2, out)
         multiply(0, 1024, bank[6], 1024)
         product_last = late[:, : PACK * (last1 - last0)].rearrange("p (t e) -> p t e", t=PACK)
         for t in range(PACK):
-            gather(product_last[:, t, :], t, last0, last1, h_last[:, t, :])
+            gather(product_last[:, t, :], t, last0, last1, slope[:, t, last0 - side0 :])
         quantise(1664, 1920, grouped[:, 1664:1920, :])
         multiply(0, 1408, bank[0], 1536)
         second = PACK * (SIDE[1][0] - side0)
         grouped_last = late[:, second : second + 2 * (last1 - last0)].bitcast(BF16).rearrange("p (e t) -> p e t", t=PACK)
-        nc.vector.tensor_tensor(
-            as_runs_out(grouped_last), as_runs_in(product_last), as_runs_in(rest_last), ALU.mult
-        )
+        nc.vector.tensor_copy(as_runs_out(grouped_last, 2), as_runs_in(product_last, 2))
         quantise(last0, last1, grouped_last)
         multiply(0, 1536, bank[1], 1920)
         multiply(1, 1024, bank[7], 1024)

@@ -61,7 +61,7 @@ def tile_attend_gmp_sig_kernel(tc, dyT, hE, w_words, w_scales, offs, offs2, out)
             return front[t][:, e0:e1]
 
         h_side = keep.tile([P, PACK, E - side0], F32, name="h_side")
-        ident_first = keep.tile([P, P], F32, name="ident_first", tag="rest")
+        ident_first = [keep.tile([P, P], F32, name="ident_first%d" % n, tag="rest%d" % n) for n in range(2)]
         rest_turned = keep.tile([P, PACK * BLOCKS * P], F32, name="rest_turned", tag="turned", align_bytes=64)
         product = keep.tile([P, PACK, MAIN], F32, name="product", tag="product", align_bytes=64)
         grouped = keep.tile([P, last0, PACK], BF16, name="grouped", align_bytes=64)
@@ -75,10 +75,12 @@ def tile_attend_gmp_sig_kernel(tc, dyT, hE, w_words, w_scales, offs, offs2, out)
         dy_rows = dyT.rearrange("(p t) x -> t p x", t=PACK)
         h_rows = hE.rearrange("(p t) e -> p t e", t=PACK)
 
-        nc.gpsimd.memset(dy[0][:, V:], 0.0)
-        make_identity(nc, ident_first[:])
+        for t in range(2):
+            nc.vector.memset(dy[t][:, V:], 0.0)
+        make_identity(nc, ident_first[0][:])
+        make_identity(nc, ident_first[1][:])
         make_identity(nc, ident[:])
-        for t in range(1, PACK):
+        for t in range(2, PACK):
             nc.gpsimd.memset(dy[t][:, V:], 0.0)
         nc.gpsimd.memset(w_scale[:].bitcast(I32), 0)
 
@@ -91,7 +93,7 @@ def tile_attend_gmp_sig_kernel(tc, dyT, hE, w_words, w_scales, offs, offs2, out)
                 nc.sync.dma_start(factor(t, e0, e1), h_rows[:, t, e0:e1])
             if t == 2:
                 nc.sync.dma_start(dy[t][:, :V], dy_rows[t])
-        nc.sync.dma_start(h_side[:, :2, :], h_rows[:, :2, side0:])
+                nc.sync.dma_start(h_side[:, :2, :], h_rows[:, :2, side0:])
         nc.sync.dma_start(dy[3][:, :V], dy_rows[3])
         nc.sync.dma_start(h_side[:, 2:, :], h_rows[:, 2:, side0:])
         nc.sync.dma_start(w_codes[:].bitcast(I32), w_words[0].rearrange("p d r -> p (d r)").bitcast(I32))
@@ -141,36 +143,32 @@ def tile_attend_gmp_sig_kernel(tc, dyT, hE, w_words, w_scales, offs, offs2, out)
                 gather(product[:, t, e0:e1], t, e0, e1, factor(t, e0, e1))
 
         home = {k: bank[place % BANKS] for place, k in enumerate(ORDER)}
-        staging = bank[BANKS - 2 :]
-        early = ORDER[: BANKS - 2]
+        staging = bank[BANKS // 2 :]
 
         def turn_back(t, k):
             i = t * BLOCKS + k
             nc.tensor.transpose(home[k][:, t * P : (t + 1) * P], rest_turned[:, i * P : (i + 1) * P], ident[:])
 
         groups = PACK * BLOCKS // 4
-        for g in range(groups + 1):
-            if g < groups:
-                stage = staging[g % 2]
+        first_groups = (PACK - 1) * BLOCKS // 4
+        rest_side = []
+        for n, (g0, g1) in enumerate([(0, first_groups), (first_groups, groups)]):
+            for g in range(g0, g1):
+                stage = staging[g % len(staging)]
                 for slot in range(4):
                     t, k = divmod(4 * g + slot, BLOCKS)
                     e0 = HEAD + k * P
-                    nc.tensor.transpose(stage[:, slot * P : (slot + 1) * P], factor(t, e0, e0 + P), ident_first[:])
+                    nc.tensor.transpose(stage[:, slot * P : (slot + 1) * P], factor(t, e0, e0 + P), ident_first[n][:])
                 nc.scalar.activation(rest_turned[:, g * BANK : (g + 1) * BANK], stage[:], COPY, bias=1.0, scale=-1.0)
-            if g > 0:
-                for slot in range(4):
-                    t, k = divmod(4 * (g - 1) + slot, BLOCKS)
-                    if k in early:
-                        turn_back(t, k)
-        for k in ORDER[BANKS - 2 : BANKS]:
+            rest_side.append(keep.tile([P, 2, E - side0], F32, name="rest_side%d" % n, tag="rest%d" % n))
+            nc.scalar.activation(rest_side[n][:], h_side[:, 2 * n : 2 * n + 2, :], COPY, bias=1.0, scale=-1.0)
+        for k in ORDER[:BANKS]:
             for t in range(PACK):
                 turn_back(t, k)
 
-        rest_side = keep.tile([P, PACK, E - side0], F32, name="rest_side", tag="rest")
-        for t0 in (0, 2):
-            nc.scalar.activation(rest_side[:, t0 : t0 + 2, :], h_side[:, t0 : t0 + 2, :], COPY, bias=1.0, scale=-1.0)
         slope = keep.tile([P, PACK, E - side0], F32, name="slope", tag="gate")
-        nc.gpsimd.tensor_tensor(slope[:], h_side[:], rest_side[:], ALU.mult)
+        for n in range(2):
+            nc.gpsimd.tensor_tensor(slope[:, 2 * n : 2 * n + 2, :], h_side[:, 2 * n : 2 * n + 2, :], rest_side[n][:], ALU.mult)
 
         for place, k in enumerate(ORDER):
             e0 = HEAD + k * P

@@ -52,16 +52,17 @@ def tile_attend_gmp_sig_kernel(tc, dyT, hE, w_words, w_scales, offs, offs2, out)
         ident = keep.tile([P, P], F32, name="ident")
         h_head = keep.tile([P, PACK, HEAD], F32, name="h_head")
         front = [keep.tile([P, MAIN], F32, name="front%d" % t) for t in range(PACK - 1)]
-        front.append(keep.tile([P, SPLIT], F32, name="front_last", tag="gate"))
-        back_last = keep.tile([P, MAIN - SPLIT], F32, name="back_last")
+        front.append(keep.tile([P, SPLIT], F32, name="front_last"))
+        back_last = keep.tile([P, MAIN - SPLIT], F32, name="back_last", tag="gate")
 
         def factor(t, e0, e1):
             if t == PACK - 1 and e0 >= SPLIT:
                 return back_last[:, e0 - SPLIT : e1 - SPLIT]
             return front[t][:, e0:e1]
 
-        h_side = keep.tile([P, PACK, E - side0], F32, name="h_side")
-        ident_first = [keep.tile([P, P], F32, name="ident_first%d" % n, tag="rest%d" % n) for n in range(2)]
+        h_side = keep.tile([P, PACK, side1 - side0], F32, name="h_side")
+        h_last = keep.tile([P, PACK, last1 - last0], F32, name="h_last")
+        ident_first = keep.tile([P, P], F32, name="ident_first", tag="rest")
         rest_turned = keep.tile([P, PACK * BLOCKS * P], F32, name="rest_turned", tag="turned", align_bytes=64)
         product = keep.tile([P, PACK, MAIN], F32, name="product", tag="product", align_bytes=64)
         grouped = keep.tile([P, last0, PACK], BF16, name="grouped", align_bytes=64)
@@ -77,8 +78,7 @@ def tile_attend_gmp_sig_kernel(tc, dyT, hE, w_words, w_scales, offs, offs2, out)
 
         for t in range(2):
             nc.vector.memset(dy[t][:, V:], 0.0)
-        make_identity(nc, ident_first[0][:])
-        make_identity(nc, ident_first[1][:])
+        make_identity(nc, ident_first[:])
         make_identity(nc, ident[:])
         for t in range(2, PACK):
             nc.gpsimd.memset(dy[t][:, V:], 0.0)
@@ -93,9 +93,10 @@ def tile_attend_gmp_sig_kernel(tc, dyT, hE, w_words, w_scales, offs, offs2, out)
                 nc.sync.dma_start(factor(t, e0, e1), h_rows[:, t, e0:e1])
             if t == 2:
                 nc.sync.dma_start(dy[t][:, :V], dy_rows[t])
-                nc.sync.dma_start(h_side[:, :2, :], h_rows[:, :2, side0:])
+        nc.sync.dma_start(h_side[:, :2, :], h_rows[:, :2, side0:side1])
         nc.sync.dma_start(dy[3][:, :V], dy_rows[3])
-        nc.sync.dma_start(h_side[:, 2:, :], h_rows[:, 2:, side0:])
+        nc.sync.dma_start(h_side[:, 2:, :], h_rows[:, 2:, side0:side1])
+        nc.sync.dma_start(h_last[:], h_rows[:, :, last0:last1])
         nc.sync.dma_start(w_codes[:].bitcast(I32), w_words[0].rearrange("p d r -> p (d r)").bitcast(I32))
         for q in range(4):
             nc.sync.dma_start(
@@ -150,32 +151,31 @@ def tile_attend_gmp_sig_kernel(tc, dyT, hE, w_words, w_scales, offs, offs2, out)
             nc.tensor.transpose(home[k][:, t * P : (t + 1) * P], rest_turned[:, i * P : (i + 1) * P], ident[:])
 
         groups = PACK * BLOCKS // 4
-        first_groups = (PACK - 1) * BLOCKS // 4
-        rest_side = []
-        for n, (g0, g1) in enumerate([(0, first_groups), (first_groups, groups)]):
-            for g in range(g0, g1):
-                stage = staging[g % len(staging)]
-                for slot in range(4):
-                    t, k = divmod(4 * g + slot, BLOCKS)
-                    e0 = HEAD + k * P
-                    nc.tensor.transpose(stage[:, slot * P : (slot + 1) * P], factor(t, e0, e0 + P), ident_first[n][:])
-                nc.scalar.activation(rest_turned[:, g * BANK : (g + 1) * BANK], stage[:], COPY, bias=1.0, scale=-1.0)
-            rest_side.append(keep.tile([P, 2, E - side0], F32, name="rest_side%d" % n, tag="rest%d" % n))
-            nc.scalar.activation(rest_side[n][:], h_side[:, 2 * n : 2 * n + 2, :], COPY, bias=1.0, scale=-1.0)
+        for g in range(groups):
+            stage = staging[g % len(staging)]
+            for slot in range(4):
+                t, k = divmod(4 * g + slot, BLOCKS)
+                e0 = HEAD + k * P
+                nc.tensor.transpose(stage[:, slot * P : (slot + 1) * P], factor(t, e0, e0 + P), ident_first[:])
+            nc.scalar.activation(rest_turned[:, g * BANK : (g + 1) * BANK], stage[:], COPY, bias=1.0, scale=-1.0)
+        rest = keep.tile([P, PACK + 1, side1 - side0], F32, name="rest", tag="rest")
+        for t0 in (0, 2):
+            nc.scalar.activation(rest[:, t0 : t0 + 2, :], h_side[:, t0 : t0 + 2, :], COPY, bias=1.0, scale=-1.0)
+        rest_last = rest[:, PACK, :].rearrange("p (t e) -> p t e", t=PACK)
+        nc.scalar.activation(rest_last, h_last[:], COPY, bias=1.0, scale=-1.0)
         for k in ORDER[:BANKS]:
             for t in range(PACK):
                 turn_back(t, k)
 
-        slope = keep.tile([P, PACK, E - side0], F32, name="slope", tag="gate")
-        for n in range(2):
-            nc.gpsimd.tensor_tensor(slope[:, 2 * n : 2 * n + 2, :], h_side[:, 2 * n : 2 * n + 2, :], rest_side[n][:], ALU.mult)
+        slope = keep.tile([P, PACK, side1 - side0], F32, name="slope", tag="gate")
+        nc.gpsimd.tensor_tensor(slope[:], h_side[:], rest[:, :PACK, :], ALU.mult)
 
         for place, k in enumerate(ORDER):
             e0 = HEAD + k * P
             nc.vector.tensor_tensor(
-                as_runs_out(grouped[:, e0 : e0 + P, :], 2),
-                as_runs_in(product[:, :, e0 : e0 + P], 2),
-                as_runs_in(home[k][:].rearrange("p (t e) -> p t e", t=PACK), 2),
+                as_runs_out(grouped[:, e0 : e0 + P, :]),
+                as_runs_in(product[:, :, e0 : e0 + P]),
+                as_runs_in(home[k][:].rearrange("p (t e) -> p t e", t=PACK)),
                 ALU.mult,
             )
             if place + BANKS < BLOCKS:
@@ -201,12 +201,12 @@ def tile_attend_gmp_sig_kernel(tc, dyT, hE, w_words, w_scales, offs, offs2, out)
         multiply(0, 1024, bank[6], 1024)
         product_last = late[:, : PACK * (last1 - last0)].rearrange("p (t e) -> p t e", t=PACK)
         for t in range(PACK):
-            gather(product_last[:, t, :], t, last0, last1, slope[:, t, last0 - side0 :])
+            gather(product_last[:, t, :], t, last0, last1, h_last[:, t, :])
         quantise(1664, 1920, grouped[:, 1664:1920, :])
         multiply(0, 1408, bank[0], 1536)
         second = PACK * (SIDE[1][0] - side0)
         grouped_last = late[:, second : second + 2 * (last1 - last0)].bitcast(BF16).rearrange("p (e t) -> p e t", t=PACK)
-        nc.vector.tensor_copy(as_runs_out(grouped_last, 2), as_runs_in(product_last, 2))
+        nc.vector.tensor_tensor(as_runs_out(grouped_last), as_runs_in(product_last), as_runs_in(rest_last), ALU.mult)
         quantise(last0, last1, grouped_last)
         multiply(0, 1536, bank[1], 1920)
         multiply(1, 1024, bank[7], 1024)

@@ -34,8 +34,8 @@ SPLIT = 1152
 GATHERS = [[0, 128, 384, 768, 1408], [0, 768, 1408], [0, 1408], [0, 1152, 1408]]
 ORDER = [0, 1, 2, 3, 4, 5, 6, 8, 7, 9]
 PICK = 512
-GPSIMD_SUMS = [(0, 0, 1024), (0, 1024, 2048), (1, 0, 1024), (1, 1024, 1536)]
-VECTOR_SUMS = [(1536, 1792), (1792, 2048)]
+GPSIMD_SUMS = [(0, 0, 1024), (0, 1024, 2048), (1, 0, 1024), (1, 1024, 1280)]
+VECTOR_SUMS = [(1280, 1792), (1792, 2048)]
 
 
 def tile_attend_gmp_sig_kernel(tc, dyT, hE, w_words, w_scales, offs, offs2, out):
@@ -221,9 +221,10 @@ def tile_attend_gmp_sig_kernel(tc, dyT, hE, w_words, w_scales, offs, offs2, out)
             nodes = (s1 - s0) // K
             pairs = keep.tile([P, nodes, 2], F32, name="pairs%d_%d" % (half, s0))
             for first in range(s0, s1, PICK):
-                picked = pick(half, first, first + PICK)
+                end = min(first + PICK, s1)
+                picked = pick(half, first, end)
                 x0 = (first - s0) // K
-                nc.gpsimd.tensor_tensor(pairs[:, x0 : x0 + PICK // K, :], picked[:, :, 0:2], picked[:, :, 2:4], ALU.add)
+                nc.gpsimd.tensor_tensor(pairs[:, x0 : (end - s0) // K, :], picked[:, :, 0:2], picked[:, :, 2:4], ALU.add)
             sums = keep.tile([P, nodes], F32, name="sums%d_%d" % (half, s0))
             nc.gpsimd.tensor_tensor(sums[:], pairs[:, :, 0], pairs[:, :, 1], ALU.add)
             nc.sync.dma_start(out[half * P : (half + 1) * P, s0 // K : s1 // K], sums[:])

@@ -22,17 +22,13 @@ PACK = 4
 PER_COLUMN = 16
 BANK = 512
 BANKS = 8
-HEAD = 128
 MAIN = 1408
-SIDE = [(1408, 1664), (1664, 1920)]
-LAST = (1920, 2048)
-BLOCKS = (MAIN - HEAD) // P
-DY_WINDOW = MAIN + 32
+BLOCKS = MAIN // P
+SIDE = [(MAIN, 1792), (1792, E)]
+PIECES = [0, 512, 1024, 1536, E]
+SPARE = 32
 RUN = 4
-LOADS = [[128, 384, 768, 1408], [128, 768, 1408], [128, 1408], [128, 1152, 1408]]
-SPLIT = 1152
-GATHERS = [[0, 128, 384, 768, 1408], [0, 768, 1408], [0, 1408], [0, 1152, 1408]]
-ORDER = [0, 1, 2, 3, 4, 5, 6, 8, 7, 9]
+GATHERS = [[0, 128, 448, 1152, E], [0, 1024, E], [0, E], [0, MAIN, E]]
 PICK = 512
 GPSIMD_SUMS = [(0, 0, 1024), (0, 1024, 2048), (1, 0, 1024), (1, 1024, 1280)]
 VECTOR_SUMS = [(1280, 1792), (1792, 2048)]
@@ -44,59 +40,37 @@ def tile_attend_gmp_sig_kernel(tc, dyT, hE, w_words, w_scales, offs, offs2, out)
         keep = ctx.enter_context(tc.tile_pool(name="keep", bufs=1))
         psum = ctx.enter_context(tc.psum_pool(name="psum", bufs=1))
 
-        side0, side1 = SIDE[0][0], SIDE[-1][1]
-        last0, last1 = LAST
         dst = keep.tile([P, E // PER_COLUMN], U16, name="dst")
         src = keep.tile([P, E // PER_COLUMN], U16, name="src")
-        dy = [keep.tile([P, DY_WINDOW], F32, name="dy%d" % t) for t in range(PACK)]
+        longest = [max(e1 - e0 for e0, e1 in zip(cuts, cuts[1:])) for cuts in GATHERS]
+        dy = [keep.tile([P, longest[t] + SPARE], F32, name="dy%d" % t) for t in range(PACK)]
         ident = keep.tile([P, P], F32, name="ident")
-        h_head = keep.tile([P, PACK, HEAD], F32, name="h_head")
-        front = [keep.tile([P, MAIN], F32, name="front%d" % t) for t in range(PACK - 1)]
-        front.append(keep.tile([P, SPLIT], F32, name="front_last"))
-        back_last = keep.tile([P, MAIN - SPLIT], F32, name="back_last", tag="gate")
-
-        def factor(t, e0, e1):
-            if t == PACK - 1 and e0 >= SPLIT:
-                return back_last[:, e0 - SPLIT : e1 - SPLIT]
-            return front[t][:, e0:e1]
-
-        h_side = keep.tile([P, PACK, side1 - side0], F32, name="h_side")
-        h_last = keep.tile([P, PACK, last1 - last0], F32, name="h_last")
-        ident_first = keep.tile([P, P], F32, name="ident_first", tag="rest")
-        rest_turned = keep.tile([P, PACK * BLOCKS * P], F32, name="rest_turned", tag="turned", align_bytes=64)
-        product = keep.tile([P, PACK, MAIN], F32, name="product", tag="product", align_bytes=64)
-        grouped = keep.tile([P, last0, PACK], BF16, name="grouped", align_bytes=64)
+        h = [keep.tile([P, E], F32, name="h%d" % t) for t in range(PACK)]
+        rest_turned = keep.tile([P, PACK * BLOCKS * P], F32, name="rest_turned")
+        rest = keep.tile([P, PACK, E - MAIN], F32, name="rest")
+        product = keep.tile([P, PACK, E], F32, name="product", tag="product", align_bytes=64)
+        grouped = keep.tile([P, E, PACK], BF16, name="grouped", align_bytes=64)
         w_codes = keep.tile([P, D], U32, name="w_codes", align_bytes=64)
         w_scale = keep.tile([P, D], U8, name="w_scale", align_bytes=64)
-        dz_codes = keep.tile([P, E], U32, name="dz_codes", align_bytes=64)
         dz_scale = keep.tile([P, E], U8, name="dz_scale", align_bytes=64)
         dm = [keep.tile([P, E], F32, name="dm%d" % half) for half in range(D // P)]
         bank = [psum.tile([P, BANK], F32, name="bank%d" % b) for b in range(BANKS)]
 
         dy_rows = dyT.rearrange("(p t) x -> t p x", t=PACK)
-        h_rows = hE.rearrange("(p t) e -> p t e", t=PACK)
+        h_rows = hE.rearrange("(p t) e -> t p e", t=PACK)
 
         for t in range(2):
             nc.vector.memset(dy[t][:, V:], 0.0)
-        make_identity(nc, ident_first[:])
         make_identity(nc, ident[:])
         for t in range(2, PACK):
             nc.gpsimd.memset(dy[t][:, V:], 0.0)
         nc.gpsimd.memset(w_scale[:].bitcast(I32), 0)
 
-        nc.sync.dma_start(h_head[:], h_rows[:, :, :HEAD])
         nc.sync.dma_start(dst[:], offs)
         for t in range(PACK):
-            if t < 2:
-                nc.sync.dma_start(dy[t][:, :V], dy_rows[t])
-            for e0, e1 in zip(LOADS[t], LOADS[t][1:]):
-                nc.sync.dma_start(factor(t, e0, e1), h_rows[:, t, e0:e1])
-            if t == 2:
-                nc.sync.dma_start(dy[t][:, :V], dy_rows[t])
-        nc.sync.dma_start(h_side[:, :2, :], h_rows[:, :2, side0:side1])
-        nc.sync.dma_start(dy[3][:, :V], dy_rows[3])
-        nc.sync.dma_start(h_side[:, 2:, :], h_rows[:, 2:, side0:side1])
-        nc.sync.dma_start(h_last[:], h_rows[:, :, last0:last1])
+            nc.sync.dma_start(dy[t][:, :V], dy_rows[t])
+            for e0, e1 in zip(GATHERS[t], GATHERS[t][1:]):
+                nc.sync.dma_start(h[t][:, e0:e1], h_rows[t][:, e0:e1])
         nc.sync.dma_start(w_codes[:].bitcast(I32), w_words[0].rearrange("p d r -> p (d r)").bitcast(I32))
         for q in range(4):
             nc.sync.dma_start(
@@ -104,25 +78,59 @@ def tile_attend_gmp_sig_kernel(tc, dyT, hE, w_words, w_scales, offs, offs2, out)
             )
         nc.sync.dma_start(src[:], offs2)
 
-        def gather(target, t, e0, e1, plain):
+        def as_runs_out(values):
+            return values.rearrange("p (c i) t -> p c t i", i=RUN)
+
+        def as_runs_in(values):
+            return values.rearrange("p t (c i) -> p c t i", i=RUN)
+
+        for t in range(PACK):
+            for e0, e1 in zip(GATHERS[t], GATHERS[t][1:]):
+                nc.vector.tensor_tensor(
+                    product[:, t, e0:e1],
+                    dy[t][:].indirect(dst[:, e0 // PER_COLUMN : e1 // PER_COLUMN]),
+                    h[t][:, e0:e1],
+                    ALU.mult,
+                )
+
+        staging = bank[BANKS // 2 :]
+
+        def turn_back(k):
+            for t in range(PACK):
+                i = t * BLOCKS + k
+                nc.tensor.transpose(
+                    bank[k % BANKS][:, t * P : (t + 1) * P], rest_turned[:, i * P : (i + 1) * P], ident[:]
+                )
+
+        for g in range(PACK * BLOCKS // 4):
+            stage = staging[g % len(staging)]
+            for slot in range(4):
+                t, k = divmod(4 * g + slot, BLOCKS)
+                nc.tensor.transpose(stage[:, slot * P : (slot + 1) * P], h[t][:, k * P : (k + 1) * P], ident[:])
+            nc.scalar.activation(rest_turned[:, g * BANK : (g + 1) * BANK], stage[:], COPY, bias=1.0, scale=-1.0)
+        for t in range(PACK):
+            nc.scalar.activation(rest[:, t, :], h[t][:, MAIN:], COPY, bias=1.0, scale=-1.0)
+        for k in range(BANKS):
+            turn_back(k)
+
+        for e0, e1 in SIDE:
+            late = keep.tile([P, PACK, e1 - e0], F32, name="late%d" % e0)
+            nc.gpsimd.tensor_tensor(late[:], product[:, :, e0:e1], rest[:, :, e0 - MAIN : e1 - MAIN], ALU.mult)
+            nc.scalar.activation(as_runs_out(grouped[:, e0:e1, :]), as_runs_in(late[:]), COPY)
+        for k in range(BLOCKS):
+            e0 = k * P
             nc.vector.tensor_tensor(
-                target, dy[t][:].indirect(dst[:, e0 // PER_COLUMN : e1 // PER_COLUMN]), plain, ALU.mult
+                as_runs_out(grouped[:, e0 : e0 + P, :]),
+                as_runs_in(product[:, :, e0 : e0 + P]),
+                as_runs_in(bank[k % BANKS][:].rearrange("p (t e) -> p t e", t=PACK)),
+                ALU.mult,
             )
+            if k + BANKS < BLOCKS:
+                turn_back(k + BANKS)
 
-        def as_runs_out(values, run=RUN):
-            return values.rearrange("p (c i) t -> p c t i", i=run)
+        dz_codes = keep.tile([P, E], U32, name="dz_codes", tag="product", align_bytes=64)
 
-        def as_runs_in(values, run=RUN):
-            return values.rearrange("p t (c i) -> p c t i", i=run)
-
-        def quantise(e0, e1, values):
-            nc.vector.quantize_mx(
-                out=dz_codes[:, e0:e1].bitcast(E5M2X4),
-                scales=dz_scale[:, e0:e1],
-                in_=values.rearrange("p e t -> p (e t)"),
-            )
-
-        def multiply(half, e0, acc, new0):
+        def multiply(half, e0, acc):
             d_cols = slice(half * P, (half + 1) * P)
             nc.tensor.matmul_mx(
                 out=acc[:],
@@ -133,84 +141,23 @@ def tile_attend_gmp_sig_kernel(tc, dyT, hE, w_words, w_scales, offs, offs2, out)
                 start=True,
                 stop=True,
             )
-            nc.scalar.copy(dm[half][:, new0 : e0 + BANK], acc[:, new0 - e0 :])
 
-        for t in range(PACK):
-            nc.vector.scalar_tensor_tensor(
-                factor(t, 0, HEAD), h_head[:, t, :], 1.0, h_head[:, t, :], ALU.subtract, ALU.mult
+        for c, (e0, e1) in enumerate(zip(PIECES, PIECES[1:])):
+            nc.vector.quantize_mx(
+                out=dz_codes[:, e0:e1].bitcast(E5M2X4),
+                scales=dz_scale[:, e0:e1],
+                in_=grouped[:, e0:e1, :].rearrange("p e t -> p (e t)"),
             )
-        for t in range(PACK):
-            for e0, e1 in zip(GATHERS[t], GATHERS[t][1:]):
-                gather(product[:, t, e0:e1], t, e0, e1, factor(t, e0, e1))
-
-        home = {k: bank[place % BANKS] for place, k in enumerate(ORDER)}
-        staging = bank[BANKS // 2 :]
-
-        def turn_back(t, k):
-            i = t * BLOCKS + k
-            nc.tensor.transpose(home[k][:, t * P : (t + 1) * P], rest_turned[:, i * P : (i + 1) * P], ident[:])
-
-        groups = PACK * BLOCKS // 4
-        for g in range(groups):
-            stage = staging[g % len(staging)]
-            for slot in range(4):
-                t, k = divmod(4 * g + slot, BLOCKS)
-                e0 = HEAD + k * P
-                nc.tensor.transpose(stage[:, slot * P : (slot + 1) * P], factor(t, e0, e0 + P), ident_first[:])
-            nc.scalar.activation(rest_turned[:, g * BANK : (g + 1) * BANK], stage[:], COPY, bias=1.0, scale=-1.0)
-        rest = keep.tile([P, PACK + 1, side1 - side0], F32, name="rest", tag="rest")
-        for t0 in (0, 2):
-            nc.scalar.activation(rest[:, t0 : t0 + 2, :], h_side[:, t0 : t0 + 2, :], COPY, bias=1.0, scale=-1.0)
-        rest_last = rest[:, PACK, :].rearrange("p (t e) -> p t e", t=PACK)
-        nc.scalar.activation(rest_last, h_last[:], COPY, bias=1.0, scale=-1.0)
-        for k in ORDER[:BANKS]:
-            for t in range(PACK):
-                turn_back(t, k)
-
-        slope = keep.tile([P, PACK, side1 - side0], F32, name="slope", tag="gate")
-        nc.gpsimd.tensor_tensor(slope[:], h_side[:], rest[:, :PACK, :], ALU.mult)
-
-        for place, k in enumerate(ORDER):
-            e0 = HEAD + k * P
-            nc.vector.tensor_tensor(
-                as_runs_out(grouped[:, e0 : e0 + P, :]),
-                as_runs_in(product[:, :, e0 : e0 + P]),
-                as_runs_in(home[k][:].rearrange("p (t e) -> p t e", t=PACK)),
-                ALU.mult,
-            )
-            if place + BANKS < BLOCKS:
-                for t in range(PACK):
-                    turn_back(t, ORDER[place + BANKS])
-
-        grouped_head = keep.tile([P, HEAD, PACK], BF16, name="grouped_head", tag="turned", align_bytes=64)
-        nc.scalar.activation(as_runs_out(grouped_head[:]), as_runs_in(product[:, :, :HEAD]), COPY, scale=-1.0)
-        quantise(128, 1152, grouped[:, 128:1152, :])
-        quantise(0, HEAD, grouped_head[:])
-        multiply(0, 0, bank[2], 0)
-        multiply(0, 512, bank[3], 512)
-        multiply(1, 0, bank[4], 0)
-        multiply(1, 512, bank[5], 512)
-
-        late = keep.tile([P, PACK * (side1 - side0)], F32, name="late", tag="product", align_bytes=64)
-        for e0, e1 in SIDE:
-            dz = late[:, PACK * (e0 - side0) : PACK * (e1 - side0)].rearrange("p (t e) -> p t e", t=PACK)
-            for t in range(PACK):
-                gather(dz[:, t, :], t, e0, e1, slope[:, t, e0 - side0 : e1 - side0])
-            nc.scalar.activation(as_runs_out(grouped[:, e0:e1, :]), as_runs_in(dz), COPY)
-        quantise(1152, 1664, grouped[:, 1152:1664, :])
-        multiply(0, 1024, bank[6], 1024)
-        product_last = late[:, : PACK * (last1 - last0)].rearrange("p (t e) -> p t e", t=PACK)
-        for t in range(PACK):
-            gather(product_last[:, t, :], t, last0, last1, h_last[:, t, :])
-        quantise(1664, 1920, grouped[:, 1664:1920, :])
-        multiply(0, 1408, bank[0], 1536)
-        second = PACK * (SIDE[1][0] - side0)
-        grouped_last = late[:, second : second + 2 * (last1 - last0)].bitcast(BF16).rearrange("p (e t) -> p e t", t=PACK)
-        nc.vector.tensor_tensor(as_runs_out(grouped_last), as_runs_in(product_last), as_runs_in(rest_last), ALU.mult)
-        quantise(last0, last1, grouped_last)
-        multiply(0, 1536, bank[1], 1920)
-        multiply(1, 1024, bank[7], 1024)
-        multiply(1, 1536, bank[2], 1536)
+            acc = bank[3 + c]
+            multiply(0, e1 - BANK, acc)
+            if e1 < E:
+                nc.scalar.copy(dm[0][:, e0:e1], acc[:, BANK - (e1 - e0) :])
+            else:
+                nc.vector.tensor_copy(dm[0][:, e0:e1], acc[:, BANK - (e1 - e0) :])
+        for c in range(E // BANK):
+            acc = bank[6 + c % 2]
+            multiply(1, c * BANK, acc)
+            nc.scalar.copy(dm[1][:, c * BANK : (c + 1) * BANK], acc[:])
 
         def pick(half, s0, s1):
             picked = keep.tile([P, s1 - s0], F32, name="picked%d_%d" % (half, s0))

@@ -16,19 +16,22 @@ E4M3X4 = mybir.dt.float8_e4m3fn_x4
 E5M2X4 = mybir.dt.float8_e5m2_x4
 ALU = mybir.AluOpType
 COPY = mybir.ActivationFunctionType.Copy
+SQUARE = mybir.ActivationFunctionType.Square
 
 P = 128
 PACK = 4
 PER_COLUMN = 16
 BANK = 512
 BANKS = 8
-MAIN = 1408
-BLOCKS = MAIN // P
-SIDE = [(MAIN, 1792), (1792, E)]
-PIECES = [0, 512, 1024, 1536, E]
+FRONT = 1024
+BLOCKS = (E - FRONT) // P
+SIDE = [(0, 512), (512, 768), (768, FRONT)]
+AFTER_BLOCK = {0: 4, 512: 6}
+PIECES = [1024, 0, 1536, 512]
 SPARE = 32
 RUN = 4
-GATHERS = [[0, 128, 448, 1152, E], [0, 1024, E], [0, E], [0, MAIN, E]]
+GATHERS = [[0, 128, 384, FRONT], [0, 512, FRONT], [0, FRONT], [0, FRONT]]
+BACK_LOAD = 256
 PICK = 512
 GPSIMD_SUMS = [(0, 0, 1024), (0, 1024, 2048), (1, 0, 1024), (1, 1024, 1280)]
 VECTOR_SUMS = [(1280, 1792), (1792, 2048)]
@@ -42,14 +45,14 @@ def tile_attend_gmp_sig_kernel(tc, dyT, hE, w_words, w_scales, offs, offs2, out)
 
         dst = keep.tile([P, E // PER_COLUMN], U16, name="dst")
         src = keep.tile([P, E // PER_COLUMN], U16, name="src")
-        longest = [max(e1 - e0 for e0, e1 in zip(cuts, cuts[1:])) for cuts in GATHERS]
-        dy = [keep.tile([P, longest[t] + SPARE], F32, name="dy%d" % t) for t in range(PACK)]
+        dy = [keep.tile([P, max(FRONT, E - FRONT) + SPARE], F32, name="dy%d" % t) for t in range(PACK)]
         ident = keep.tile([P, P], F32, name="ident")
-        h = [keep.tile([P, E], F32, name="h%d" % t) for t in range(PACK)]
-        rest_turned = keep.tile([P, PACK * BLOCKS * P], F32, name="rest_turned")
-        rest = keep.tile([P, PACK, E - MAIN], F32, name="rest")
-        product = keep.tile([P, PACK, E], F32, name="product", tag="product", align_bytes=64)
-        grouped = keep.tile([P, E, PACK], BF16, name="grouped", align_bytes=64)
+        h_front = [keep.tile([P, FRONT], F32, name="h_front%d" % t) for t in range(PACK - 1)]
+        h_front.append(keep.tile([P, FRONT], F32, name="h_front_last", tag="looked_up", align_bytes=64))
+        h_back = [keep.tile([P, PACK, BACK_LOAD], F32, name="h_back%d" % e0) for e0 in range(FRONT, E, BACK_LOAD)]
+        rest = keep.tile([P, PACK, FRONT], F32, name="rest")
+        product = keep.tile([P, PACK, FRONT], F32, name="product")
+        grouped = {e0: keep.tile([P, BANK, PACK], BF16, name="grouped%d" % e0, align_bytes=64) for e0 in range(FRONT, E, BANK)}
         w_codes = keep.tile([P, D], U32, name="w_codes", align_bytes=64)
         w_scale = keep.tile([P, D], U8, name="w_scale", align_bytes=64)
         dz_scale = keep.tile([P, E], U8, name="dz_scale", align_bytes=64)
@@ -57,7 +60,7 @@ def tile_attend_gmp_sig_kernel(tc, dyT, hE, w_words, w_scales, offs, offs2, out)
         bank = [psum.tile([P, BANK], F32, name="bank%d" % b) for b in range(BANKS)]
 
         dy_rows = dyT.rearrange("(p t) x -> t p x", t=PACK)
-        h_rows = hE.rearrange("(p t) e -> t p e", t=PACK)
+        h_rows = hE.rearrange("(p t) e -> p t e", t=PACK)
 
         for t in range(2):
             nc.vector.memset(dy[t][:, V:], 0.0)
@@ -70,7 +73,9 @@ def tile_attend_gmp_sig_kernel(tc, dyT, hE, w_words, w_scales, offs, offs2, out)
         for t in range(PACK):
             nc.sync.dma_start(dy[t][:, :V], dy_rows[t])
             for e0, e1 in zip(GATHERS[t], GATHERS[t][1:]):
-                nc.sync.dma_start(h[t][:, e0:e1], h_rows[t][:, e0:e1])
+                nc.sync.dma_start(h_front[t][:, e0:e1], h_rows[:, t, e0:e1])
+        for i, e0 in enumerate(range(FRONT, E, BACK_LOAD)):
+            nc.sync.dma_start(h_back[i][:], h_rows[:, :, e0 : e0 + BACK_LOAD])
         nc.sync.dma_start(w_codes[:].bitcast(I32), w_words[0].rearrange("p d r -> p (d r)").bitcast(I32))
         for q in range(4):
             nc.sync.dma_start(
@@ -89,46 +94,59 @@ def tile_attend_gmp_sig_kernel(tc, dyT, hE, w_words, w_scales, offs, offs2, out)
                 nc.vector.tensor_tensor(
                     product[:, t, e0:e1],
                     dy[t][:].indirect(dst[:, e0 // PER_COLUMN : e1 // PER_COLUMN]),
-                    h[t][:, e0:e1],
+                    h_front[t][:, e0:e1],
                     ALU.mult,
                 )
 
-        staging = bank[BANKS // 2 :]
-
-        def turn_back(k):
-            for t in range(PACK):
-                i = t * BLOCKS + k
-                nc.tensor.transpose(
-                    bank[k % BANKS][:, t * P : (t + 1) * P], rest_turned[:, i * P : (i + 1) * P], ident[:]
-                )
-
-        for g in range(PACK * BLOCKS // 4):
-            stage = staging[g % len(staging)]
-            for slot in range(4):
-                t, k = divmod(4 * g + slot, BLOCKS)
-                nc.tensor.transpose(stage[:, slot * P : (slot + 1) * P], h[t][:, k * P : (k + 1) * P], ident[:])
-            nc.scalar.activation(rest_turned[:, g * BANK : (g + 1) * BANK], stage[:], COPY, bias=1.0, scale=-1.0)
         for t in range(PACK):
-            nc.scalar.activation(rest[:, t, :], h[t][:, MAIN:], COPY, bias=1.0, scale=-1.0)
-        for k in range(BANKS):
-            turn_back(k)
+            nc.scalar.activation(rest[:, t, :], h_front[t][:], COPY, bias=-1.0, scale=1.0)
+        looked_up = keep.tile([P, PACK, E - FRONT], F32, name="looked_up", tag="looked_up", align_bytes=64)
+        for t in range(PACK):
+            nc.vector.tensor_copy(looked_up[:, t, :], dy[t][:].indirect(dst[:, FRONT // PER_COLUMN :]))
+
+        def turn(k):
+            load, e0 = divmod(k * P, BACK_LOAD)
+            for t in range(PACK):
+                nc.tensor.transpose(bank[k][:, t * P : (t + 1) * P], h_back[load][:, t, e0 : e0 + P], ident[:])
+            square = keep.tile([P, BANK], F32, name="square%d" % k)
+            negative = keep.tile([P, BANK], F32, name="negative%d" % k, tag="negative%d" % k, align_bytes=64)
+            nc.scalar.activation(square[:], bank[k][:], SQUARE)
+            nc.scalar.activation(negative[:], bank[k][:], COPY, scale=-1.0)
+            return square, negative
+
+        def turn_back(k, terms):
+            for t in range(PACK):
+                cols = slice(t * P, (t + 1) * P)
+                for i, term in enumerate(terms):
+                    nc.tensor.matmul(bank[k][:, cols], term[:, cols], ident[:], start=i == 0, stop=i == 1, is_transpose=True)
+
+        terms = [turn(0)]
+        for k in range(BLOCKS):
+            if k + 1 < BLOCKS:
+                terms.append(turn(k + 1))
+            turn_back(k, terms[k])
+
+        for e0, k in AFTER_BLOCK.items():
+            grouped[e0] = keep.tile([P, BANK, PACK], BF16, name="grouped%d" % e0, tag="negative%d" % k, align_bytes=64)
+
+        def grouped_at(e0, e1):
+            first = e0 - e0 % BANK
+            return grouped[first][:, e0 - first : e1 - first, :]
 
         for e0, e1 in SIDE:
             late = keep.tile([P, PACK, e1 - e0], F32, name="late%d" % e0)
-            nc.gpsimd.tensor_tensor(late[:], product[:, :, e0:e1], rest[:, :, e0 - MAIN : e1 - MAIN], ALU.mult)
-            nc.scalar.activation(as_runs_out(grouped[:, e0:e1, :]), as_runs_in(late[:]), COPY)
+            nc.gpsimd.tensor_tensor(late[:], product[:, :, e0:e1], rest[:, :, e0:e1], ALU.mult)
+            nc.scalar.activation(as_runs_out(grouped_at(e0, e1)), as_runs_in(late[:]), COPY)
         for k in range(BLOCKS):
             e0 = k * P
             nc.vector.tensor_tensor(
-                as_runs_out(grouped[:, e0 : e0 + P, :]),
-                as_runs_in(product[:, :, e0 : e0 + P]),
-                as_runs_in(bank[k % BANKS][:].rearrange("p (t e) -> p t e", t=PACK)),
+                as_runs_out(grouped_at(FRONT + e0, FRONT + e0 + P)),
+                as_runs_in(looked_up[:, :, e0 : e0 + P]),
+                as_runs_in(bank[k][:].rearrange("p (t e) -> p t e", t=PACK)),
                 ALU.mult,
             )
-            if k + BANKS < BLOCKS:
-                turn_back(k + BANKS)
 
-        dz_codes = keep.tile([P, E], U32, name="dz_codes", tag="product", align_bytes=64)
+        dz_codes = keep.tile([P, E], U32, name="dz_codes", tag="looked_up", align_bytes=64)
 
         def multiply(half, e0, acc):
             d_cols = slice(half * P, (half + 1) * P)
@@ -142,22 +160,23 @@ def tile_attend_gmp_sig_kernel(tc, dyT, hE, w_words, w_scales, offs, offs2, out)
                 stop=True,
             )
 
-        for c, (e0, e1) in enumerate(zip(PIECES, PIECES[1:])):
+        for c, e0 in enumerate(PIECES):
+            e1 = e0 + BANK
             nc.vector.quantize_mx(
                 out=dz_codes[:, e0:e1].bitcast(E5M2X4),
                 scales=dz_scale[:, e0:e1],
-                in_=grouped[:, e0:e1, :].rearrange("p e t -> p (e t)"),
+                in_=grouped[e0][:].rearrange("p e t -> p (e t)"),
             )
-            acc = bank[3 + c]
-            multiply(0, e1 - BANK, acc)
-            if e1 < E:
-                nc.scalar.copy(dm[0][:, e0:e1], acc[:, BANK - (e1 - e0) :])
+            acc = bank[c]
+            multiply(0, e0, acc)
+            if c + 1 < len(PIECES):
+                nc.scalar.activation(dm[0][:, e0:e1], acc[:], COPY, scale=-1.0)
             else:
-                nc.vector.tensor_copy(dm[0][:, e0:e1], acc[:, BANK - (e1 - e0) :])
-        for c in range(E // BANK):
-            acc = bank[6 + c % 2]
-            multiply(1, c * BANK, acc)
-            nc.scalar.copy(dm[1][:, c * BANK : (c + 1) * BANK], acc[:])
+                nc.vector.tensor_scalar(dm[0][:, e0:e1], acc[:], -1.0, None, ALU.mult)
+        for c, e0 in enumerate(PIECES):
+            acc = bank[2 + c % 2]
+            multiply(1, e0, acc)
+            nc.scalar.activation(dm[1][:, e0 : e0 + BANK], acc[:], COPY, scale=-1.0)
 
         def pick(half, s0, s1):
             picked = keep.tile([P, s1 - s0], F32, name="picked%d_%d" % (half, s0))

@@ -26,11 +26,12 @@ BANKS = 8
 FRONT = 1024
 BLOCKS = (E - FRONT) // P
 SIDE = [(0, 512), (512, 768), (768, FRONT)]
-AFTER_BLOCK = {0: 4, 512: 6}
+AFTER_BLOCK = {0: 6, 512: 7}
+BACK = E - FRONT
+HELD = 5
 PIECES = [1024, 0, 1536, 512]
 SPARE = 32
 RUN = 4
-GATHERS = [[0, 128, 384, FRONT], [0, 512, FRONT], [0, FRONT], [0, FRONT]]
 BACK_LOAD = 256
 PICK = 512
 GPSIMD_SUMS = [(0, 0, 1024), (0, 1024, 2048), (1, 0, 1024), (1, 1024, 1280)]
@@ -48,7 +49,9 @@ def tile_attend_gmp_sig_kernel(tc, dyT, hE, w_words, w_scales, offs, offs2, out)
         dy = [keep.tile([P, max(FRONT, E - FRONT) + SPARE], F32, name="dy%d" % t) for t in range(PACK)]
         ident = keep.tile([P, P], F32, name="ident")
         h_front = [keep.tile([P, FRONT], F32, name="h_front%d" % t) for t in range(PACK - 1)]
-        h_front.append(keep.tile([P, FRONT], F32, name="h_front_last", tag="looked_up", align_bytes=64))
+        looked_up = keep.tile([P, PACK * BACK], F32, name="looked_up")
+        h_front = [tile[:] for tile in h_front] + [looked_up[:, 3 * BACK // 2 : 3 * BACK // 2 + FRONT]]
+        dz_codes = keep.tile([P, E], U32, name="dz_codes", align_bytes=64)
         h_back = [keep.tile([P, PACK, BACK_LOAD], F32, name="h_back%d" % e0) for e0 in range(FRONT, E, BACK_LOAD)]
         rest = keep.tile([P, PACK, FRONT], F32, name="rest")
         product = keep.tile([P, PACK, FRONT], F32, name="product")
@@ -70,12 +73,22 @@ def tile_attend_gmp_sig_kernel(tc, dyT, hE, w_words, w_scales, offs, offs2, out)
         nc.gpsimd.memset(w_scale[:].bitcast(I32), 0)
 
         nc.sync.dma_start(dst[:], offs)
-        for t in range(PACK):
-            nc.sync.dma_start(dy[t][:, :V], dy_rows[t])
-            for e0, e1 in zip(GATHERS[t], GATHERS[t][1:]):
-                nc.sync.dma_start(h_front[t][:, e0:e1], h_rows[:, t, e0:e1])
-        for i, e0 in enumerate(range(FRONT, E, BACK_LOAD)):
-            nc.sync.dma_start(h_back[i][:], h_rows[:, :, e0 : e0 + BACK_LOAD])
+
+        def load_back(i):
+            nc.sync.dma_start(h_back[i][:], h_rows[:, :, FRONT + i * BACK_LOAD : FRONT + (i + 1) * BACK_LOAD])
+
+        nc.sync.dma_start(dy[0][:, :V], dy_rows[0])
+        load_back(0)
+        nc.sync.dma_start(h_front[0], h_rows[:, 0, :FRONT])
+        nc.sync.dma_start(dy[1][:, :V], dy_rows[1])
+        nc.sync.dma_start(h_front[1], h_rows[:, 1, :FRONT])
+        load_back(1)
+        nc.sync.dma_start(dy[2][:, :V], dy_rows[2])
+        nc.sync.dma_start(h_front[2], h_rows[:, 2, :FRONT])
+        nc.sync.dma_start(h_front[3], h_rows[:, 3, :FRONT])
+        nc.sync.dma_start(dy[3][:, :V], dy_rows[3])
+        load_back(2)
+        load_back(3)
         nc.sync.dma_start(w_codes[:].bitcast(I32), w_words[0].rearrange("p d r -> p (d r)").bitcast(I32))
         for q in range(4):
             nc.sync.dma_start(
@@ -89,30 +102,32 @@ def tile_attend_gmp_sig_kernel(tc, dyT, hE, w_words, w_scales, offs, offs2, out)
         def as_runs_in(values):
             return values.rearrange("p t (c i) -> p c t i", i=RUN)
 
-        for t in range(PACK):
-            for e0, e1 in zip(GATHERS[t], GATHERS[t][1:]):
-                nc.vector.tensor_tensor(
-                    product[:, t, e0:e1],
-                    dy[t][:].indirect(dst[:, e0 // PER_COLUMN : e1 // PER_COLUMN]),
-                    h_front[t][:, e0:e1],
-                    ALU.mult,
-                )
+        def look_up(t, e0, e1):
+            offsets = dst[:, (FRONT + e0) // PER_COLUMN : (FRONT + e1) // PER_COLUMN]
+            nc.vector.tensor_copy(looked_up[:, t * BACK + e0 : t * BACK + e1], dy[t][:].indirect(offsets))
 
+        look_up(0, 0, BACK)
         for t in range(PACK):
-            nc.scalar.activation(rest[:, t, :], h_front[t][:], COPY, bias=-1.0, scale=1.0)
-        looked_up = keep.tile([P, PACK, E - FRONT], F32, name="looked_up", tag="looked_up", align_bytes=64)
-        for t in range(PACK):
-            nc.vector.tensor_copy(looked_up[:, t, :], dy[t][:].indirect(dst[:, FRONT // PER_COLUMN :]))
+            nc.vector.tensor_tensor(
+                product[:, t, :], dy[t][:].indirect(dst[:, : FRONT // PER_COLUMN]), h_front[t], ALU.mult
+            )
+            nc.scalar.activation(rest[:, t, :], h_front[t], COPY, bias=-1.0, scale=1.0)
+        look_up(3, 0, BACK)
+        look_up(1, 0, BACK)
+        look_up(2, 0, BACK // 2)
 
         def turn(k):
             load, e0 = divmod(k * P, BACK_LOAD)
             for t in range(PACK):
                 nc.tensor.transpose(bank[k][:, t * P : (t + 1) * P], h_back[load][:, t, e0 : e0 + P], ident[:])
             square = keep.tile([P, BANK], F32, name="square%d" % k)
-            negative = keep.tile([P, BANK], F32, name="negative%d" % k, tag="negative%d" % k, align_bytes=64)
+            if k == HELD:
+                negative = looked_up[:, 5 * BACK // 2 : 5 * BACK // 2 + BANK]
+            else:
+                negative = keep.tile([P, BANK], F32, name="negative%d" % k, tag="negative%d" % k, align_bytes=64)[:]
             nc.scalar.activation(square[:], bank[k][:], SQUARE)
-            nc.scalar.activation(negative[:], bank[k][:], COPY, scale=-1.0)
-            return square, negative
+            nc.scalar.activation(negative, bank[k][:], COPY, scale=-1.0)
+            return square[:], negative
 
         def turn_back(k, terms):
             for t in range(PACK):
@@ -125,6 +140,8 @@ def tile_attend_gmp_sig_kernel(tc, dyT, hE, w_words, w_scales, offs, offs2, out)
             if k + 1 < BLOCKS:
                 terms.append(turn(k + 1))
             turn_back(k, terms[k])
+        look_up(2, BACK // 2, BACK)
+        looked_up_sets = looked_up[:].rearrange("p (t e) -> p t e", t=PACK)
 
         for e0, k in AFTER_BLOCK.items():
             grouped[e0] = keep.tile([P, BANK, PACK], BF16, name="grouped%d" % e0, tag="negative%d" % k, align_bytes=64)
@@ -141,12 +158,10 @@ def tile_attend_gmp_sig_kernel(tc, dyT, hE, w_words, w_scales, offs, offs2, out)
             e0 = k * P
             nc.vector.tensor_tensor(
                 as_runs_out(grouped_at(FRONT + e0, FRONT + e0 + P)),
-                as_runs_in(looked_up[:, :, e0 : e0 + P]),
+                as_runs_in(looked_up_sets[:, :, e0 : e0 + P]),
                 as_runs_in(bank[k][:].rearrange("p (t e) -> p t e", t=PACK)),
                 ALU.mult,
             )
-
-        dz_codes = keep.tile([P, E], U32, name="dz_codes", tag="looked_up", align_bytes=64)
 
         def multiply(half, e0, acc):
             d_cols = slice(half * P, (half + 1) * P)

@@ -24,18 +24,24 @@ PER_COLUMN = 16
 BANK = 512
 BANKS = 8
 FRONT = 1024
-BLOCKS = (E - FRONT) // P
-SIDE = [(0, 512), (512, 768), (768, FRONT)]
-AFTER_BLOCK = {0: 6, 512: 7}
 BACK = E - FRONT
+BLOCKS = BACK // P
+SIDE = [(0, 512), (512, 768), (768, FRONT)]
 HELD = 5
 PIECES = [1024, 0, 1536, 512]
 SPARE = 32
 RUN = 4
-BACK_LOAD = 256
-PICK = 512
-GPSIMD_SUMS = [(0, 0, 1024), (0, 1024, 2048), (1, 0, 1024), (1, 1024, 1280)]
-VECTOR_SUMS = [(1280, 1792), (1792, 2048)]
+BACK_LOADS = [0, 256, 384, 640, 896, BACK]
+SUMS = [
+    (0, 0, 1024, "gpsimd"),
+    (0, 1024, 2048, "tensor"),
+    (1, 0, 512, "gpsimd"),
+    (1, 512, 1024, "tensor"),
+    (1, 1024, 1408, "gpsimd"),
+    (1, 1408, 1792, "vector"),
+    (1, 1792, 2048, "vector"),
+]
+STORES = [(0, 0, 512), (1, 0, 128), (1, 128, 256), (1, 256, 352), (1, 352, 512)]
 
 
 def tile_attend_gmp_sig_kernel(tc, dyT, hE, w_words, w_scales, offs, offs2, out):
@@ -50,12 +56,12 @@ def tile_attend_gmp_sig_kernel(tc, dyT, hE, w_words, w_scales, offs, offs2, out)
         ident = keep.tile([P, P], F32, name="ident")
         h_front = [keep.tile([P, FRONT], F32, name="h_front%d" % t) for t in range(PACK - 1)]
         looked_up = keep.tile([P, PACK * BACK], F32, name="looked_up")
-        h_front = [tile[:] for tile in h_front] + [looked_up[:, 3 * BACK // 2 : 3 * BACK // 2 + FRONT]]
+        h_front = [tile[:] for tile in h_front] + [looked_up[:, 7 * BACK // 4 : 7 * BACK // 4 + FRONT]]
         dz_codes = keep.tile([P, E], U32, name="dz_codes", align_bytes=64)
-        h_back = [keep.tile([P, PACK, BACK_LOAD], F32, name="h_back%d" % e0) for e0 in range(FRONT, E, BACK_LOAD)]
+        back_loads = list(zip(BACK_LOADS, BACK_LOADS[1:]))
+        h_back = [keep.tile([P, PACK, e1 - e0], F32, name="h_back%d" % e0) for e0, e1 in back_loads]
         rest = keep.tile([P, PACK, FRONT], F32, name="rest")
         product = keep.tile([P, PACK, FRONT], F32, name="product")
-        grouped = {e0: keep.tile([P, BANK, PACK], BF16, name="grouped%d" % e0, align_bytes=64) for e0 in range(FRONT, E, BANK)}
         w_codes = keep.tile([P, D], U32, name="w_codes", align_bytes=64)
         w_scale = keep.tile([P, D], U8, name="w_scale", align_bytes=64)
         dz_scale = keep.tile([P, E], U8, name="dz_scale", align_bytes=64)
@@ -75,20 +81,21 @@ def tile_attend_gmp_sig_kernel(tc, dyT, hE, w_words, w_scales, offs, offs2, out)
         nc.sync.dma_start(dst[:], offs)
 
         def load_back(i):
-            nc.sync.dma_start(h_back[i][:], h_rows[:, :, FRONT + i * BACK_LOAD : FRONT + (i + 1) * BACK_LOAD])
+            e0, e1 = back_loads[i]
+            nc.sync.dma_start(h_back[i][:], h_rows[:, :, FRONT + e0 : FRONT + e1])
 
         nc.sync.dma_start(dy[0][:, :V], dy_rows[0])
-        load_back(0)
         nc.sync.dma_start(h_front[0], h_rows[:, 0, :FRONT])
+        load_back(0)
         nc.sync.dma_start(dy[1][:, :V], dy_rows[1])
         nc.sync.dma_start(h_front[1], h_rows[:, 1, :FRONT])
-        load_back(1)
         nc.sync.dma_start(dy[2][:, :V], dy_rows[2])
         nc.sync.dma_start(h_front[2], h_rows[:, 2, :FRONT])
+        load_back(1)
         nc.sync.dma_start(h_front[3], h_rows[:, 3, :FRONT])
         nc.sync.dma_start(dy[3][:, :V], dy_rows[3])
-        load_back(2)
-        load_back(3)
+        for i in range(2, len(back_loads)):
+            load_back(i)
         nc.sync.dma_start(w_codes[:].bitcast(I32), w_words[0].rearrange("p d r -> p (d r)").bitcast(I32))
         for q in range(4):
             nc.sync.dma_start(
@@ -115,16 +122,15 @@ def tile_attend_gmp_sig_kernel(tc, dyT, hE, w_words, w_scales, offs, offs2, out)
         look_up(3, 0, BACK)
         look_up(1, 0, BACK)
         look_up(2, 0, BACK // 2)
+        look_up(2, BACK // 2, BACK)
 
         def turn(k):
-            load, e0 = divmod(k * P, BACK_LOAD)
+            load = max(i for i, (first, end) in enumerate(back_loads) if first <= k * P)
+            e0 = k * P - back_loads[load][0]
             for t in range(PACK):
                 nc.tensor.transpose(bank[k][:, t * P : (t + 1) * P], h_back[load][:, t, e0 : e0 + P], ident[:])
-            square = keep.tile([P, BANK], F32, name="square%d" % k)
-            if k == HELD:
-                negative = looked_up[:, 5 * BACK // 2 : 5 * BACK // 2 + BANK]
-            else:
-                negative = keep.tile([P, BANK], F32, name="negative%d" % k, tag="negative%d" % k, align_bytes=64)[:]
+            square = keep.tile([P, BANK], F32, name="square%d" % k, tag="square%d" % k, align_bytes=64)
+            negative = keep.tile([P, BANK], F32, name="negative%d" % k, tag="negative%d" % k, align_bytes=64)[:]
             nc.scalar.activation(square[:], bank[k][:], SQUARE)
             nc.scalar.activation(negative, bank[k][:], COPY, scale=-1.0)
             return square[:], negative
@@ -140,11 +146,13 @@ def tile_attend_gmp_sig_kernel(tc, dyT, hE, w_words, w_scales, offs, offs2, out)
             if k + 1 < BLOCKS:
                 terms.append(turn(k + 1))
             turn_back(k, terms[k])
-        look_up(2, BACK // 2, BACK)
         looked_up_sets = looked_up[:].rearrange("p (t e) -> p t e", t=PACK)
 
-        for e0, k in AFTER_BLOCK.items():
-            grouped[e0] = keep.tile([P, BANK, PACK], BF16, name="grouped%d" % e0, tag="negative%d" % k, align_bytes=64)
+        homes = {0: "negative6", 512: "negative7", 1024: "negative%d" % HELD, 1536: "square%d" % HELD}
+        grouped = {
+            e0: keep.tile([P, BANK, PACK], BF16, name="grouped%d" % e0, tag=tag, align_bytes=64)
+            for e0, tag in homes.items()
+        }
 
         def grouped_at(e0, e1):
             first = e0 - e0 % BANK
@@ -198,23 +206,31 @@ def tile_attend_gmp_sig_kernel(tc, dyT, hE, w_words, w_scales, offs, offs2, out)
             nc.vector.tensor_copy(picked[:], dm[half][:].indirect(src[:, s0 // PER_COLUMN : s1 // PER_COLUMN]))
             return picked[:].rearrange("p (x j) -> p x j", j=K)
 
-        for half, s0, s1 in GPSIMD_SUMS:
-            nodes = (s1 - s0) // K
-            pairs = keep.tile([P, nodes, 2], F32, name="pairs%d_%d" % (half, s0))
-            for first in range(s0, s1, PICK):
-                end = min(first + PICK, s1)
-                picked = pick(half, first, end)
-                x0 = (first - s0) // K
-                nc.gpsimd.tensor_tensor(pairs[:, x0 : (end - s0) // K, :], picked[:, :, 0:2], picked[:, :, 2:4], ALU.add)
-            sums = keep.tile([P, nodes], F32, name="sums%d_%d" % (half, s0))
-            nc.gpsimd.tensor_tensor(sums[:], pairs[:, :, 0], pairs[:, :, 1], ALU.add)
-            nc.sync.dma_start(out[half * P : (half + 1) * P, s0 // K : s1 // K], sums[:])
-
-        tail_x0 = VECTOR_SUMS[0][0] // K
-        tail_sums = keep.tile([P, V - tail_x0], F32, name="tail_sums")
-        tail_picked = [pick(1, s0, s1) for s0, s1 in VECTOR_SUMS]
-        for (s0, s1), picked in zip(VECTOR_SUMS, tail_picked):
-            nc.vector.tensor_reduce(
-                tail_sums[:, s0 // K - tail_x0 : s1 // K - tail_x0], picked, mybir.AxisListType.X, ALU.add
-            )
-        nc.sync.dma_start(out[P : 2 * P, tail_x0:V], tail_sums[:])
+        sums = [keep.tile([P, V], F32, name="sums%d" % half) for half in range(D // P)]
+        waiting = []
+        turns = 0
+        for half, s0, s1, adder in SUMS:
+            picked = pick(half, s0, s1)
+            x0, x1 = s0 // K, s1 // K
+            if adder == "gpsimd":
+                pairs = keep.tile([P, x1 - x0, 2], F32, name="pairs%d_%d" % (half, s0))
+                nc.gpsimd.tensor_tensor(pairs[:], picked[:, :, 0:2], picked[:, :, 2:4], ALU.add)
+                nc.gpsimd.tensor_tensor(sums[half][:, x0:x1], pairs[:, :, 0], pairs[:, :, 1], ALU.add)
+            elif adder == "tensor":
+                for x in range(0, x1 - x0, P):
+                    across, back = bank[3 - turns % 2], bank[4 + turns % 2]
+                    for j in range(K):
+                        nc.tensor.matmul(
+                            across[:, :P], picked[:, x : x + P, j], ident[:], start=j == 0, stop=j == K - 1, is_transpose=True
+                        )
+                    turned = keep.tile([P, P], F32, name="turned%d" % turns)
+                    nc.scalar.copy(turned[:], across[:, :P])
+                    nc.tensor.transpose(back[:, :P], turned[:], ident[:])
+                    nc.scalar.copy(sums[half][:, x0 + x : x0 + x + P], back[:, :P])
+                    turns = turns + 1
+            else:
+                waiting.append((half, x0, x1, picked))
+        for half, x0, x1, picked in waiting:
+            nc.vector.tensor_reduce(sums[half][:, x0:x1], picked, mybir.AxisListType.X, ALU.add)
+        for half, x0, x1 in STORES:
+            nc.sync.dma_start(out[half * P : (half + 1) * P, x0:x1], sums[half][:, x0:x1])

@@ -28,7 +28,6 @@ BACK = E - FRONT
 BLOCKS = BACK // P
 SIDE = [(0, 512), (512, 768), (768, FRONT)]
 HELD = 5
-PIECES = [1024, 0, 1536, 512]
 SPARE = 32
 RUN = 4
 BACK_LOADS = [0, 256, 384, 640, 896, BACK]
@@ -162,7 +161,8 @@ def tile_attend_gmp_sig_kernel(tc, dyT, hE, w_words, w_scales, offs, offs2, out)
             late = keep.tile([P, PACK, e1 - e0], F32, name="late%d" % e0)
             nc.gpsimd.tensor_tensor(late[:], product[:, :, e0:e1], rest[:, :, e0:e1], ALU.mult)
             nc.scalar.activation(as_runs_out(grouped_at(e0, e1)), as_runs_in(late[:]), COPY)
-        for k in range(BLOCKS):
+
+        def finish_block(k):
             e0 = k * P
             nc.vector.tensor_tensor(
                 as_runs_out(grouped_at(FRONT + e0, FRONT + e0 + P)),
@@ -183,21 +183,30 @@ def tile_attend_gmp_sig_kernel(tc, dyT, hE, w_words, w_scales, offs, offs2, out)
                 stop=True,
             )
 
-        for c, e0 in enumerate(PIECES):
-            e1 = e0 + BANK
+        def quantise(c, e0, e1):
             nc.vector.quantize_mx(
                 out=dz_codes[:, e0:e1].bitcast(E5M2X4),
                 scales=dz_scale[:, e0:e1],
-                in_=grouped[e0][:].rearrange("p e t -> p (e t)"),
+                in_=grouped_at(e0, e1).rearrange("p e t -> p (e t)"),
             )
             acc = bank[c]
-            multiply(0, e0, acc)
-            if c + 1 < len(PIECES):
-                nc.scalar.activation(dm[0][:, e0:e1], acc[:], COPY, scale=-1.0)
+            multiply(0, e1 - BANK, acc)
+            if e1 < E:
+                nc.scalar.activation(dm[0][:, e0:e1], acc[:, BANK - (e1 - e0) :], COPY, scale=-1.0)
             else:
-                nc.vector.tensor_scalar(dm[0][:, e0:e1], acc[:], -1.0, None, ALU.mult)
-        for c, e0 in enumerate(PIECES):
-            acc = bank[2 + c % 2]
+                nc.vector.tensor_scalar(dm[0][:, e0:e1], acc[:, BANK - (e1 - e0) :], -1.0, None, ALU.mult)
+
+        for k in range(BLOCKS - 2):
+            finish_block(k)
+        quantise(0, 1024, 1536)
+        finish_block(BLOCKS - 2)
+        quantise(1, 1536, 1792)
+        quantise(2, 0, 512)
+        finish_block(BLOCKS - 1)
+        quantise(3, 512, 1024)
+        quantise(4, 1792, E)
+        for c, e0 in enumerate(range(0, E, BANK)):
+            acc = bank[3 + c % 2]
             multiply(1, e0, acc)
             nc.scalar.activation(dm[1][:, e0 : e0 + BANK], acc[:], COPY, scale=-1.0)
 
@@ -218,7 +227,7 @@ def tile_attend_gmp_sig_kernel(tc, dyT, hE, w_words, w_scales, offs, offs2, out)
                 nc.gpsimd.tensor_tensor(sums[half][:, x0:x1], pairs[:, :, 0], pairs[:, :, 1], ALU.add)
             elif adder == "tensor":
                 for x in range(0, x1 - x0, P):
-                    across, back = bank[3 - turns % 2], bank[4 + turns % 2]
+                    across, back = bank[4 - turns % 2], bank[5 + turns % 2]
                     for j in range(K):
                         nc.tensor.matmul(
                             across[:, :P], picked[:, x : x + P, j], ident[:], start=j == 0, stop=j == K - 1, is_transpose=True

@@ -23,14 +23,11 @@ PACK = 4
 PER_COLUMN = 16
 BANK = 512
 BANKS = 8
-FRONT = 1024
-BACK = E - FRONT
-BLOCKS = BACK // P
-SIDE = [(0, 512), (512, 768), (768, FRONT)]
-HELD = 5
+A, B, C = 1024, 512, 512
+HELPED = 768
 SPARE = 32
 RUN = 4
-BACK_LOADS = [0, 256, 384, 640, 896, BACK]
+LAP = 32
 SUMS = [
     (0, 0, 1024, "gpsimd"),
     (0, 1024, 2048, "tensor"),
@@ -51,21 +48,59 @@ def tile_attend_gmp_sig_kernel(tc, dyT, hE, w_words, w_scales, offs, offs2, out)
 
         dst = keep.tile([P, E // PER_COLUMN], U16, name="dst")
         src = keep.tile([P, E // PER_COLUMN], U16, name="src")
-        dy = [keep.tile([P, max(FRONT, E - FRONT) + SPARE], F32, name="dy%d" % t) for t in range(PACK)]
+        dy = [keep.tile([P, A + SPARE], F32, name="dy%d" % t) for t in range(PACK)]
         ident = keep.tile([P, P], F32, name="ident")
-        h_front = [keep.tile([P, FRONT], F32, name="h_front%d" % t) for t in range(PACK - 1)]
-        looked_up = keep.tile([P, PACK * BACK], F32, name="looked_up")
-        h_front = [tile[:] for tile in h_front] + [looked_up[:, 7 * BACK // 4 : 7 * BACK // 4 + FRONT]]
+        quarter = keep.tile([P, P], F32, name="quarter")
+        h_c = [keep.tile([P, 2 * C], F32, name="h_c%d" % i, align_bytes=64) for i in range(2)]
         dz_codes = keep.tile([P, E], U32, name="dz_codes", align_bytes=64)
-        back_loads = list(zip(BACK_LOADS, BACK_LOADS[1:]))
-        h_back = [keep.tile([P, PACK, e1 - e0], F32, name="h_back%d" % e0) for e0, e1 in back_loads]
-        rest = keep.tile([P, PACK, FRONT], F32, name="rest")
-        product = keep.tile([P, PACK, FRONT], F32, name="product")
         w_codes = keep.tile([P, D], U32, name="w_codes", align_bytes=64)
         w_scale = keep.tile([P, D], U8, name="w_scale", align_bytes=64)
         dz_scale = keep.tile([P, E], U8, name="dz_scale", align_bytes=64)
         dm = [keep.tile([P, E], F32, name="dm%d" % half) for half in range(D // P)]
         bank = [psum.tile([P, BANK], F32, name="bank%d" % b) for b in range(BANKS)]
+
+        def fresh(name, columns):
+            return keep.tile([P, columns], F32, name=name, align_bytes=64)[:]
+
+        piece = A // 2
+        square2_at = 3 * B + A - LAP
+        step = A + square2_at + HELPED - LAP
+        work = fresh("work", piece + PACK * step + A)
+        rows = work[:, piece : piece + PACK * step]
+        product_a = rows.rearrange("p (t x) -> p t x", t=PACK)[:, :, :A]
+        between = rows[:, A:step]
+        ahead = rows[:, 2 * step + A :]
+        behind = work[:, piece + 3 * step + A :]
+        looked_up = ahead[:, : PACK * B].rearrange("p (t e) -> p t e", t=PACK)
+        h_a0 = [fresh("h_a0_%d" % i, piece) for i in range(2)]
+        squares_b = fresh("squares_b", PACK * BANK)
+        slope3_at = P * 2 - LAP
+        slope_c_at = slope3_at + A - LAP
+        square3_at = slope_c_at + 2 * C
+        h2_at = square3_at + A - LAP
+        h_a = [None, fresh("h_a1", A), behind[:, h2_at : h2_at + A], fresh("h_a3", A)]
+        h_b_homes = [fresh("h_b%d" % i, 2 * B) for i in range(2)]
+        h_b = [home.rearrange("p (t e) -> p t e", t=PACK) for home in h_b_homes]
+        square_a0 = [fresh("square_a0", piece), ahead[:, 2 * B + LAP : 2 * B + LAP + piece]]
+        square_a = [
+            None,
+            ahead[:, 3 * B : 3 * B + A],
+            ahead[:, square2_at : square2_at + A],
+            behind[:, square3_at : square3_at + A],
+        ]
+        square_c = [h_a[2], h_b_homes[0]]
+        slope_a0 = [fresh("slope_a0", piece), between[:, :piece]]
+        slope_a = [
+            None,
+            between[:, piece - LAP : piece - LAP + A],
+            between[:, piece + HELPED - 2 * LAP : piece + HELPED + A - 2 * LAP],
+            behind[:, slope3_at : slope3_at + A],
+        ]
+        around_c = fresh("around_c", C // 2 + PACK * C)
+        slope_c = [behind[:, slope_c_at : slope_c_at + 2 * C], around_c[:, : 2 * C]]
+        grouped_b = work[:, 2 * piece + 3 * step : 2 * piece + 3 * step + 2 * B]
+        grouped_b = grouped_b.bitcast(BF16).rearrange("p (e t) -> p e t", t=PACK)
+        product_c = around_c[:, C // 2 :].rearrange("p (t e) -> p t e", t=PACK)
 
         dy_rows = dyT.rearrange("(p t) x -> t p x", t=PACK)
         h_rows = hE.rearrange("(p t) e -> p t e", t=PACK)
@@ -75,26 +110,23 @@ def tile_attend_gmp_sig_kernel(tc, dyT, hE, w_words, w_scales, offs, offs2, out)
         make_identity(nc, ident[:])
         for t in range(2, PACK):
             nc.gpsimd.memset(dy[t][:, V:], 0.0)
+        nc.gpsimd.memset(quarter[:], -0.25)
         nc.gpsimd.memset(w_scale[:].bitcast(I32), 0)
 
         nc.sync.dma_start(dst[:], offs)
-
-        def load_back(i):
-            e0, e1 = back_loads[i]
-            nc.sync.dma_start(h_back[i][:], h_rows[:, :, FRONT + e0 : FRONT + e1])
-
         nc.sync.dma_start(dy[0][:, :V], dy_rows[0])
-        nc.sync.dma_start(h_front[0], h_rows[:, 0, :FRONT])
-        load_back(0)
+        nc.sync.dma_start(h_a0[0], h_rows[:, 0, : A // 2])
         nc.sync.dma_start(dy[1][:, :V], dy_rows[1])
-        nc.sync.dma_start(h_front[1], h_rows[:, 1, :FRONT])
+        nc.sync.dma_start(h_a0[1], h_rows[:, 0, A // 2 : A])
+        nc.sync.dma_start(h_a[1], h_rows[:, 1, :A])
         nc.sync.dma_start(dy[2][:, :V], dy_rows[2])
-        nc.sync.dma_start(h_front[2], h_rows[:, 2, :FRONT])
-        load_back(1)
-        nc.sync.dma_start(h_front[3], h_rows[:, 3, :FRONT])
+        nc.sync.dma_start(h_a[2], h_rows[:, 2, :A])
         nc.sync.dma_start(dy[3][:, :V], dy_rows[3])
-        for i in range(2, len(back_loads)):
-            load_back(i)
+        nc.sync.dma_start(h_a[3], h_rows[:, 3, :A])
+        for i in (1, 0):
+            nc.sync.dma_start(h_b[i], h_rows[:, :, A + i * B // 2 : A + (i + 1) * B // 2])
+        for i in range(2):
+            nc.sync.dma_start(h_c[i][:].rearrange("p (t e) -> p t e", t=2), h_rows[:, 2 * i : 2 * i + 2, A + B :])
         nc.sync.dma_start(w_codes[:].bitcast(I32), w_words[0].rearrange("p d r -> p (d r)").bitcast(I32))
         for q in range(4):
             nc.sync.dma_start(
@@ -108,68 +140,72 @@ def tile_attend_gmp_sig_kernel(tc, dyT, hE, w_words, w_scales, offs, offs2, out)
         def as_runs_in(values):
             return values.rearrange("p t (c i) -> p c t i", i=RUN)
 
-        def look_up(t, e0, e1):
-            offsets = dst[:, (FRONT + e0) // PER_COLUMN : (FRONT + e1) // PER_COLUMN]
-            nc.vector.tensor_copy(looked_up[:, t * BACK + e0 : t * BACK + e1], dy[t][:].indirect(offsets))
+        def columns(t, e0, e1):
+            return dy[t][:].indirect(dst[:, e0 // PER_COLUMN : e1 // PER_COLUMN])
 
-        look_up(0, 0, BACK)
-        for t in range(PACK):
-            nc.vector.tensor_tensor(
-                product[:, t, :], dy[t][:].indirect(dst[:, : FRONT // PER_COLUMN]), h_front[t], ALU.mult
-            )
-            nc.scalar.activation(rest[:, t, :], h_front[t], COPY, bias=-1.0, scale=1.0)
-        look_up(3, 0, BACK)
-        look_up(1, 0, BACK)
-        look_up(2, 0, BACK // 2)
-        look_up(2, BACK // 2, BACK)
+        def centred_square(square, h):
+            nc.scalar.activation(square, h, SQUARE, bias=-0.5, scale=1.0)
+            return square
 
-        def turn(k):
-            load = max(i for i, (first, end) in enumerate(back_loads) if first <= k * P)
-            e0 = k * P - back_loads[load][0]
+        def lower_on_scalar(slope, square):
+            nc.scalar.activation(slope, square, COPY, bias=-0.25, scale=1.0)
+
+        def lower_on_gpsimd(slope, square):
+            nc.gpsimd.tensor_scalar(slope, square, 1.0, -0.25, ALU.mult, ALU.add)
+
+        def copy_b(t):
+            nc.vector.tensor_copy(looked_up[:, t, :], columns(t, A, A + B))
+
+        def multiply_a(t, e0, e1):
+            nc.vector.tensor_tensor(product_a[:, t, e0:e1], columns(t, e0, e1), slope_a[t][:, e0:e1], ALU.mult)
+
+        def shared_slope(t, copied):
+            square = centred_square(square_a[t], h_a[t])
+            lower_on_scalar(slope_a[t][:, HELPED:], square[:, HELPED:])
+            copy_b(copied)
+            lower_on_gpsimd(slope_a[t][:, :HELPED], square[:, :HELPED])
+            multiply_a(t, HELPED, A)
+            multiply_a(t, 0, HELPED)
+
+        copy_b(0)
+        copy_b(1)
+        for i in range(2):
+            lower_on_scalar(slope_a0[i], centred_square(square_a0[i], h_a0[i]))
+            e0, e1 = i * A // 2, (i + 1) * A // 2
+            nc.vector.tensor_tensor(product_a[:, 0, e0:e1], columns(0, e0, e1), slope_a0[i], ALU.mult)
+        shared_slope(1, 2)
+        shared_slope(2, 3)
+        lower_on_scalar(slope_a[3], centred_square(square_a[3], h_a[3]))
+        multiply_a(3, 0, A)
+
+        order = [2, 3, 0, 1]
+        for k in order:
             for t in range(PACK):
-                nc.tensor.transpose(bank[k][:, t * P : (t + 1) * P], h_back[load][:, t, e0 : e0 + P], ident[:])
-            square = keep.tile([P, BANK], F32, name="square%d" % k, tag="square%d" % k, align_bytes=64)
-            negative = keep.tile([P, BANK], F32, name="negative%d" % k, tag="negative%d" % k, align_bytes=64)[:]
-            nc.scalar.activation(square[:], bank[k][:], SQUARE)
-            nc.scalar.activation(negative, bank[k][:], COPY, scale=-1.0)
-            return square[:], negative
-
-        def turn_back(k, terms):
+                e0 = k % 2 * P
+                nc.tensor.transpose(bank[k][:, t * P : (t + 1) * P], h_b[k // 2][:, t, e0 : e0 + P], ident[:])
+        for place, k in enumerate(order):
+            square = centred_square(squares_b[:, place * BANK : (place + 1) * BANK], bank[k][:])
             for t in range(PACK):
                 cols = slice(t * P, (t + 1) * P)
-                for i, term in enumerate(terms):
-                    nc.tensor.matmul(bank[k][:, cols], term[:, cols], ident[:], start=i == 0, stop=i == 1, is_transpose=True)
-
-        terms = [turn(0)]
-        for k in range(BLOCKS):
-            if k + 1 < BLOCKS:
-                terms.append(turn(k + 1))
-            turn_back(k, terms[k])
-        looked_up_sets = looked_up[:].rearrange("p (t e) -> p t e", t=PACK)
-
-        homes = {0: "negative6", 512: "negative7", 1024: "negative%d" % HELD, 1536: "square%d" % HELD}
-        grouped = {
-            e0: keep.tile([P, BANK, PACK], BF16, name="grouped%d" % e0, tag=tag, align_bytes=64)
-            for e0, tag in homes.items()
-        }
-
-        def grouped_at(e0, e1):
-            first = e0 - e0 % BANK
-            return grouped[first][:, e0 - first : e1 - first, :]
-
-        for e0, e1 in SIDE:
-            late = keep.tile([P, PACK, e1 - e0], F32, name="late%d" % e0)
-            nc.gpsimd.tensor_tensor(late[:], product[:, :, e0:e1], rest[:, :, e0:e1], ALU.mult)
-            nc.scalar.activation(as_runs_out(grouped_at(e0, e1)), as_runs_in(late[:]), COPY)
+                nc.tensor.matmul(bank[k][:, cols], quarter[:], ident[:], start=True, stop=False, is_transpose=True)
+                nc.tensor.matmul(bank[k][:, cols], square[:, cols], ident[:], start=False, stop=True, is_transpose=True)
 
         def finish_block(k):
             e0 = k * P
             nc.vector.tensor_tensor(
-                as_runs_out(grouped_at(FRONT + e0, FRONT + e0 + P)),
-                as_runs_in(looked_up_sets[:, :, e0 : e0 + P]),
+                as_runs_out(grouped_b[:, e0 : e0 + P, :]),
+                as_runs_in(looked_up[:, :, e0 : e0 + P]),
                 as_runs_in(bank[k][:].rearrange("p (t e) -> p t e", t=PACK)),
                 ALU.mult,
             )
+
+        def multiply_c(t):
+            nc.vector.tensor_tensor(product_c[:, t, :], columns(t, A + B, E), slope_c[t // 2][:, t % 2 * C : (t % 2 + 1) * C], ALU.mult)
+
+        def rounded(home, values):
+            grouped = home.bitcast(BF16).rearrange("p (e t) -> p e t", t=PACK)
+            nc.scalar.activation(as_runs_out(grouped), as_runs_in(values), COPY)
+            return grouped
 
         def multiply(half, e0, acc):
             d_cols = slice(half * P, (half + 1) * P)
@@ -183,32 +219,53 @@ def tile_attend_gmp_sig_kernel(tc, dyT, hE, w_words, w_scales, offs, offs2, out)
                 stop=True,
             )
 
-        def quantise(c, e0, e1):
+        def quantise(grouped, e0):
+            e1 = e0 + grouped.shape[1]
             nc.vector.quantize_mx(
                 out=dz_codes[:, e0:e1].bitcast(E5M2X4),
                 scales=dz_scale[:, e0:e1],
-                in_=grouped_at(e0, e1).rearrange("p e t -> p (e t)"),
+                in_=grouped.rearrange("p e t -> p (e t)"),
             )
-            acc = bank[c]
-            multiply(0, e1 - BANK, acc)
-            if e1 < E:
-                nc.scalar.activation(dm[0][:, e0:e1], acc[:, BANK - (e1 - e0) :], COPY, scale=-1.0)
-            else:
-                nc.vector.tensor_scalar(dm[0][:, e0:e1], acc[:, BANK - (e1 - e0) :], -1.0, None, ALU.mult)
 
-        for k in range(BLOCKS - 2):
-            finish_block(k)
-        quantise(0, 1024, 1536)
-        finish_block(BLOCKS - 2)
-        quantise(1, 1536, 1792)
-        quantise(2, 0, 512)
-        finish_block(BLOCKS - 1)
-        quantise(3, 512, 1024)
-        quantise(4, 1792, E)
-        for c, e0 in enumerate(range(0, E, BANK)):
-            acc = bank[3 + c % 2]
-            multiply(1, e0, acc)
-            nc.scalar.activation(dm[1][:, e0 : e0 + BANK], acc[:], COPY, scale=-1.0)
+        def first_half(e0, e1, acc):
+            multiply(0, e1 - BANK, acc)
+            return dm[0][:, e0:e1], acc[:, BANK - (e1 - e0) :]
+
+        def empty_on_scalar(columns_of_dm, acc):
+            nc.scalar.activation(columns_of_dm, acc, COPY, scale=-1.0)
+
+        def empty_on_vector(columns_of_dm, acc):
+            nc.vector.tensor_scalar(columns_of_dm, acc, -1.0, None, ALU.mult)
+
+        for i in range(2):
+            centred_square(square_c[i], h_c[i][:])
+        lower_on_scalar(slope_c[1], square_c[1])
+        finish_block(2)
+        finish_block(3)
+        lower_on_gpsimd(slope_c[0], square_c[0])
+        for t in (2, 3, 0, 1):
+            multiply_c(t)
+        pieces = []
+        for i, home in enumerate((square_c[1], work[:, : 2 * piece])):
+            quantise(rounded(home, product_a[:, :, i * BANK : (i + 1) * BANK]), i * BANK)
+            pieces.append(first_half(i * BANK, (i + 1) * BANK, bank[4 + 2 * i]))
+            multiply(1, i * BANK, bank[5 + 2 * i])
+        finish_block(0)
+        finish_block(1)
+        grouped_c = [rounded(fresh("grouped_c%d" % i, C), product_c[:, :, i * C // 2 : (i + 1) * C // 2]) for i in range(2)]
+        quantise(grouped_c[0], A + B)
+        quantise(grouped_b, A)
+        quantise(grouped_c[1], A + B + C // 2)
+        pieces.append(first_half(A, A + B, bank[2]))
+        pieces.append(first_half(A + B, A + B + C // 2, bank[3]))
+        last = first_half(A + B + C // 2, E, bank[0])
+        for piece in pieces:
+            empty_on_scalar(*piece)
+        empty_on_vector(*last)
+        multiply(1, 2 * BANK, bank[3])
+        multiply(1, 3 * BANK, bank[0])
+        for c, b in enumerate((5, 7, 3, 0)):
+            empty_on_scalar(dm[1][:, c * BANK : (c + 1) * BANK], bank[b][:])
 
         def pick(half, s0, s1):
             picked = keep.tile([P, s1 - s0], F32, name="picked%d_%d" % (half, s0))

@@ -24,7 +24,6 @@ PER_COLUMN = 16
 BANK = 512
 BANKS = 8
 A, B, C = 1024, 512, 512
-HELPED = 768
 SPARE = 32
 RUN = 4
 LAP = 32
@@ -63,44 +62,37 @@ def tile_attend_gmp_sig_kernel(tc, dyT, hE, w_words, w_scales, offs, offs2, out)
             return keep.tile([P, columns], F32, name=name, align_bytes=64)[:]
 
         piece = A // 2
-        square2_at = 3 * B + A - LAP
-        step = A + square2_at + HELPED - LAP
-        work = fresh("work", piece + PACK * step + A)
-        rows = work[:, piece : piece + PACK * step]
+        square2_at = PACK * B - LAP
+        h3_at = PACK * B + A
+        step = A + h3_at + A - LAP
+        rows = fresh("rows", PACK * step)
         product_a = rows.rearrange("p (t x) -> p t x", t=PACK)[:, :, :A]
-        between = rows[:, A:step]
+        gaps = [rows[:, t * step + A : (t + 1) * step] for t in range(PACK)]
         ahead = rows[:, 2 * step + A :]
-        behind = work[:, piece + 3 * step + A :]
+        grouped_b = rows[:, 3 * step + piece : 3 * step + piece + 2 * B]
+        grouped_b = grouped_b.bitcast(BF16).rearrange("p (e t) -> p e t", t=PACK)
         looked_up = ahead[:, : PACK * B].rearrange("p (t e) -> p t e", t=PACK)
-        h_a0 = [fresh("h_a0_%d" % i, piece) for i in range(2)]
-        squares_b = fresh("squares_b", PACK * BANK)
-        slope3_at = P * 2 - LAP
-        slope_c_at = slope3_at + A - LAP
-        square3_at = slope_c_at + 2 * C
-        h2_at = square3_at + A - LAP
-        h_a = [None, fresh("h_a1", A), behind[:, h2_at : h2_at + A], fresh("h_a3", A)]
-        h_b_homes = [fresh("h_b%d" % i, 2 * B) for i in range(2)]
+        grouped_a = gaps[3][:, B : B + 2 * A]
+        h_b_homes = [grouped_a[:, piece : piece + 2 * B], fresh("h_b1", 2 * B)]
         h_b = [home.rearrange("p (t e) -> p t e", t=PACK) for home in h_b_homes]
-        square_a0 = [fresh("square_a0", piece), ahead[:, 2 * B + LAP : 2 * B + LAP + piece]]
+        h_a0 = [gaps[0][:, piece - LAP : A - LAP], fresh("h_a0", piece)]
+        square_a0 = [fresh("square_a0", piece), gaps[0][:, :piece]]
+        h_a = [None, ahead[:, PACK * B : PACK * B + A], gaps[1][:, :A], ahead[:, h3_at : h3_at + A]]
         square_a = [
             None,
-            ahead[:, 3 * B : 3 * B + A],
+            gaps[0][:, A - 2 * LAP : 2 * A - 2 * LAP],
             ahead[:, square2_at : square2_at + A],
-            behind[:, square3_at : square3_at + A],
+            gaps[1][:, A - LAP : 2 * A - LAP],
         ]
-        square_c = [h_a[2], h_b_homes[0]]
-        slope_a0 = [fresh("slope_a0", piece), between[:, :piece]]
-        slope_a = [
-            None,
-            between[:, piece - LAP : piece - LAP + A],
-            between[:, piece + HELPED - 2 * LAP : piece + HELPED + A - 2 * LAP],
-            behind[:, slope3_at : slope3_at + A],
+        square_c = [fresh("square_c0", 2 * C), h_b_homes[0]]
+        around_c = fresh("around_c", A - LAP + PACK * C)
+        slope_a0 = [looked_up[:, 2, :], fresh("slope_a0", piece)]
+        slope_a = [None, fresh("slope_a1", A), around_c[:, :A], around_c[:, A - LAP : 2 * A - LAP]]
+        slope_c = [fresh("slope_c%d" % i, 2 * C) for i in range(2)]
+        product_c = around_c[:, A - LAP :].rearrange("p (t e) -> p t e", t=PACK)
+        square_b = [fresh("square_b0", BANK), fresh("square_b1", BANK)] + [
+            ahead[:, h3_at + i * BANK : h3_at + (i + 1) * BANK] for i in range(2)
         ]
-        around_c = fresh("around_c", C // 2 + PACK * C)
-        slope_c = [behind[:, slope_c_at : slope_c_at + 2 * C], around_c[:, : 2 * C]]
-        grouped_b = work[:, 2 * piece + 3 * step : 2 * piece + 3 * step + 2 * B]
-        grouped_b = grouped_b.bitcast(BF16).rearrange("p (e t) -> p e t", t=PACK)
-        product_c = around_c[:, C // 2 :].rearrange("p (t e) -> p t e", t=PACK)
 
         dy_rows = dyT.rearrange("(p t) x -> t p x", t=PACK)
         h_rows = hE.rearrange("(p t) e -> p t e", t=PACK)
@@ -121,8 +113,8 @@ def tile_attend_gmp_sig_kernel(tc, dyT, hE, w_words, w_scales, offs, offs2, out)
         nc.sync.dma_start(h_a[1], h_rows[:, 1, :A])
         nc.sync.dma_start(dy[2][:, :V], dy_rows[2])
         nc.sync.dma_start(h_a[2], h_rows[:, 2, :A])
-        nc.sync.dma_start(dy[3][:, :V], dy_rows[3])
         nc.sync.dma_start(h_a[3], h_rows[:, 3, :A])
+        nc.sync.dma_start(dy[3][:, :V], dy_rows[3])
         for i in (1, 0):
             nc.sync.dma_start(h_b[i], h_rows[:, :, A + i * B // 2 : A + (i + 1) * B // 2])
         for i in range(2):
@@ -159,36 +151,50 @@ def tile_attend_gmp_sig_kernel(tc, dyT, hE, w_words, w_scales, offs, offs2, out)
         def multiply_a(t, e0, e1):
             nc.vector.tensor_tensor(product_a[:, t, e0:e1], columns(t, e0, e1), slope_a[t][:, e0:e1], ALU.mult)
 
-        def shared_slope(t, copied):
-            square = centred_square(square_a[t], h_a[t])
-            lower_on_scalar(slope_a[t][:, HELPED:], square[:, HELPED:])
-            copy_b(copied)
-            lower_on_gpsimd(slope_a[t][:, :HELPED], square[:, :HELPED])
-            multiply_a(t, HELPED, A)
-            multiply_a(t, 0, HELPED)
-
         copy_b(0)
         copy_b(1)
-        for i in range(2):
-            lower_on_scalar(slope_a0[i], centred_square(square_a0[i], h_a0[i]))
-            e0, e1 = i * A // 2, (i + 1) * A // 2
+        def multiply_a0(i):
+            e0, e1 = i * piece, (i + 1) * piece
             nc.vector.tensor_tensor(product_a[:, 0, e0:e1], columns(0, e0, e1), slope_a0[i], ALU.mult)
-        shared_slope(1, 2)
-        shared_slope(2, 3)
-        lower_on_scalar(slope_a[3], centred_square(square_a[3], h_a[3]))
-        multiply_a(3, 0, A)
+
+        lower_on_scalar(slope_a0[0], centred_square(square_a0[0], h_a0[0]))
+        multiply_a0(0)
+        copy_b(2)
+        centred_square(square_a0[1], h_a0[1])
+        centred_square(square_a[1], h_a[1])
+        lower_on_scalar(slope_a0[1], square_a0[1])
+        multiply_a0(1)
+        for t in (1, 2):
+            centred_square(square_a[t + 1], h_a[t + 1])
+            lower_on_scalar(slope_a[t], square_a[t])
+            multiply_a(t, 0, A)
+        copy_b(3)
+
+        def turn(k):
+            across = bank[4 + k % 2]
+            for t in range(PACK):
+                e0 = k % 2 * P
+                nc.tensor.transpose(across[:, t * P : (t + 1) * P], h_b[k // 2][:, t, e0 : e0 + P], ident[:])
+            centred_square(square_b[k], across[:])
+
+        def turn_back(k):
+            for t in range(PACK):
+                cols = slice(t * P, (t + 1) * P)
+                nc.tensor.matmul(
+                    bank[k][:, cols], square_b[k][:, cols], ident[:], start=False, stop=t == PACK - 1, is_transpose=True
+                )
 
         order = [2, 3, 0, 1]
         for k in order:
             for t in range(PACK):
-                e0 = k % 2 * P
-                nc.tensor.transpose(bank[k][:, t * P : (t + 1) * P], h_b[k // 2][:, t, e0 : e0 + P], ident[:])
-        for place, k in enumerate(order):
-            square = centred_square(squares_b[:, place * BANK : (place + 1) * BANK], bank[k][:])
-            for t in range(PACK):
-                cols = slice(t * P, (t + 1) * P)
-                nc.tensor.matmul(bank[k][:, cols], quarter[:], ident[:], start=True, stop=False, is_transpose=True)
-                nc.tensor.matmul(bank[k][:, cols], square[:, cols], ident[:], start=False, stop=True, is_transpose=True)
+                nc.tensor.matmul(
+                    bank[k][:, t * P : (t + 1) * P], quarter[:], ident[:], start=t == 0, stop=False, is_transpose=True
+                )
+        for pair in (order[:2], order[2:]):
+            for k in pair:
+                turn(k)
+            for k in pair:
+                turn_back(k)
 
         def finish_block(k):
             e0 = k * P
@@ -237,16 +243,19 @@ def tile_attend_gmp_sig_kernel(tc, dyT, hE, w_words, w_scales, offs, offs2, out)
         def empty_on_vector(columns_of_dm, acc):
             nc.vector.tensor_scalar(columns_of_dm, acc, -1.0, None, ALU.mult)
 
-        for i in range(2):
-            centred_square(square_c[i], h_c[i][:])
-        lower_on_scalar(slope_c[1], square_c[1])
         finish_block(2)
         finish_block(3)
-        lower_on_gpsimd(slope_c[0], square_c[0])
-        for t in (2, 3, 0, 1):
+        lower_on_gpsimd(slope_a[3], square_a[3])
+        multiply_a(3, 0, A)
+        for i in range(2):
+            centred_square(square_c[i], h_c[i][:])
+        for i in range(2):
+            lower_on_scalar(slope_c[i], square_c[i])
+        for t in range(PACK):
             multiply_c(t)
+        quantise(grouped_b[:, B // 2 :, :], A + B // 2)
         pieces = []
-        for i, home in enumerate((square_c[1], work[:, : 2 * piece])):
+        for i, home in enumerate((grouped_a[:, :A], grouped_a[:, A:])):
             quantise(rounded(home, product_a[:, :, i * BANK : (i + 1) * BANK]), i * BANK)
             pieces.append(first_half(i * BANK, (i + 1) * BANK, bank[4 + 2 * i]))
             multiply(1, i * BANK, bank[5 + 2 * i])
@@ -254,17 +263,17 @@ def tile_attend_gmp_sig_kernel(tc, dyT, hE, w_words, w_scales, offs, offs2, out)
         finish_block(1)
         grouped_c = [rounded(fresh("grouped_c%d" % i, C), product_c[:, :, i * C // 2 : (i + 1) * C // 2]) for i in range(2)]
         quantise(grouped_c[0], A + B)
-        quantise(grouped_b, A)
+        quantise(grouped_b[:, : B // 2, :], A)
         quantise(grouped_c[1], A + B + C // 2)
-        pieces.append(first_half(A, A + B, bank[2]))
-        pieces.append(first_half(A + B, A + B + C // 2, bank[3]))
+        pieces.append(first_half(A + B // 2, A + B + C // 2, bank[2]))
+        pieces.append(first_half(A, A + B // 2, bank[3]))
         last = first_half(A + B + C // 2, E, bank[0])
         for piece in pieces:
             empty_on_scalar(*piece)
         empty_on_vector(*last)
-        multiply(1, 2 * BANK, bank[3])
-        multiply(1, 3 * BANK, bank[0])
-        for c, b in enumerate((5, 7, 3, 0)):
+        multiply(1, 3 * BANK, bank[3])
+        multiply(1, 2 * BANK, bank[0])
+        for c, b in enumerate((5, 7, 0, 3)):
             empty_on_scalar(dm[1][:, c * BANK : (c + 1) * BANK], bank[b][:])
 
         def pick(half, s0, s1):

@@ -50,7 +50,6 @@ def tile_attend_gmp_sig_kernel(tc, dyT, hE, w_words, w_scales, offs, offs2, out)
         dy = [keep.tile([P, A + SPARE], F32, name="dy%d" % t) for t in range(PACK)]
         ident = keep.tile([P, P], F32, name="ident")
         quarter = keep.tile([P, P], F32, name="quarter")
-        h_c = [keep.tile([P, 2 * C], F32, name="h_c%d" % i, align_bytes=64) for i in range(2)]
         dz_codes = keep.tile([P, E], U32, name="dz_codes", align_bytes=64)
         w_codes = keep.tile([P, D], U32, name="w_codes", align_bytes=64)
         w_scale = keep.tile([P, D], U8, name="w_scale", align_bytes=64)
@@ -63,7 +62,7 @@ def tile_attend_gmp_sig_kernel(tc, dyT, hE, w_words, w_scales, offs, offs2, out)
 
         piece = A // 2
         square2_at = PACK * B - LAP
-        h3_at = PACK * B + A
+        h3_at = PACK * B + 3 * A - 4 * LAP
         step = A + h3_at + A - LAP
         rows = fresh("rows", PACK * step)
         product_a = rows.rearrange("p (t x) -> p t x", t=PACK)[:, :, :A]
@@ -72,25 +71,29 @@ def tile_attend_gmp_sig_kernel(tc, dyT, hE, w_words, w_scales, offs, offs2, out)
         grouped_b = rows[:, 3 * step + piece : 3 * step + piece + 2 * B]
         grouped_b = grouped_b.bitcast(BF16).rearrange("p (e t) -> p e t", t=PACK)
         looked_up = ahead[:, : PACK * B].rearrange("p (t e) -> p t e", t=PACK)
+        spare = [gaps[0][:, i * A : (i + 1) * A] for i in range(5)] + [gaps[1][:, i * A : (i + 1) * A] for i in (2, 3)]
         grouped_a = gaps[3][:, B : B + 2 * A]
-        h_b_homes = [grouped_a[:, piece : piece + 2 * B], fresh("h_b1", 2 * B)]
+        h_b_homes = [grouped_a[:, piece : piece + 2 * B], spare[0]]
         h_b = [home.rearrange("p (t e) -> p t e", t=PACK) for home in h_b_homes]
-        h_a0 = [gaps[0][:, piece - LAP : A - LAP], fresh("h_a0", piece)]
-        square_a0 = [fresh("square_a0", piece), gaps[0][:, :piece]]
-        h_a = [None, ahead[:, PACK * B : PACK * B + A], gaps[1][:, :A], ahead[:, h3_at : h3_at + A]]
+        square0_at = square2_at + A - LAP
+        square1_at = square0_at + A - 2 * LAP
+        h_a0 = [ahead[:, square0_at + piece - LAP : square0_at + A - LAP], spare[1][:, :piece]]
+        square_a0 = [looked_up[:, 2, :], ahead[:, square0_at : square0_at + piece]]
+        h_a = [None, gaps[1][:, :A], gaps[1][:, A : 2 * A], ahead[:, h3_at : h3_at + A]]
         square_a = [
             None,
-            gaps[0][:, A - 2 * LAP : 2 * A - 2 * LAP],
+            ahead[:, square1_at : square1_at + A],
             ahead[:, square2_at : square2_at + A],
-            gaps[1][:, A - LAP : 2 * A - LAP],
+            ahead[:, square1_at : square1_at + A],
         ]
-        square_c = [fresh("square_c0", 2 * C), h_b_homes[0]]
-        around_c = fresh("around_c", A - LAP + PACK * C)
-        slope_a0 = [looked_up[:, 2, :], fresh("slope_a0", piece)]
-        slope_a = [None, fresh("slope_a1", A), around_c[:, :A], around_c[:, A - LAP : 2 * A - LAP]]
+        h_c = spare[5:]
+        square_c = [spare[2], h_b_homes[0]]
+        around_c = gaps[3][:, B + 2 * A : B + 4 * A - LAP]
+        slope_a0 = [spare[1][:, piece:], fresh("slope_a0", piece)]
+        slope_a = [None, spare[3], around_c[:, :A], around_c[:, A - LAP : 2 * A - LAP]]
         slope_c = [fresh("slope_c%d" % i, 2 * C) for i in range(2)]
-        product_c = around_c[:, A - LAP :].rearrange("p (t e) -> p t e", t=PACK)
-        square_b = [fresh("square_b0", BANK), fresh("square_b1", BANK)] + [
+        product_c = keep.tile([P, PACK, C], F32, name="product_c")
+        square_b = [spare[4][:, :BANK], spare[4][:, BANK:]] + [
             ahead[:, h3_at + i * BANK : h3_at + (i + 1) * BANK] for i in range(2)
         ]
 
@@ -118,7 +121,7 @@ def tile_attend_gmp_sig_kernel(tc, dyT, hE, w_words, w_scales, offs, offs2, out)
         for i in (1, 0):
             nc.sync.dma_start(h_b[i], h_rows[:, :, A + i * B // 2 : A + (i + 1) * B // 2])
         for i in range(2):
-            nc.sync.dma_start(h_c[i][:].rearrange("p (t e) -> p t e", t=2), h_rows[:, 2 * i : 2 * i + 2, A + B :])
+            nc.sync.dma_start(h_c[i].rearrange("p (t e) -> p t e", t=2), h_rows[:, 2 * i : 2 * i + 2, A + B :])
         nc.sync.dma_start(w_codes[:].bitcast(I32), w_words[0].rearrange("p d r -> p (d r)").bitcast(I32))
         for q in range(4):
             nc.sync.dma_start(
@@ -164,10 +167,13 @@ def tile_attend_gmp_sig_kernel(tc, dyT, hE, w_words, w_scales, offs, offs2, out)
         centred_square(square_a[1], h_a[1])
         lower_on_scalar(slope_a0[1], square_a0[1])
         multiply_a0(1)
-        for t in (1, 2):
-            centred_square(square_a[t + 1], h_a[t + 1])
-            lower_on_scalar(slope_a[t], square_a[t])
-            multiply_a(t, 0, A)
+        lower_on_scalar(slope_a[1], square_a[1])
+        multiply_a(1, 0, A)
+        centred_square(square_a[2], h_a[2])
+        centred_square(square_a[3][:, :piece], h_a[3][:, :piece])
+        lower_on_scalar(slope_a[2], square_a[2])
+        multiply_a(2, 0, A)
+        centred_square(square_a[3][:, piece:], h_a[3][:, piece:])
         copy_b(3)
 
         def turn(k):
@@ -248,7 +254,7 @@ def tile_attend_gmp_sig_kernel(tc, dyT, hE, w_words, w_scales, offs, offs2, out)
         lower_on_gpsimd(slope_a[3], square_a[3])
         multiply_a(3, 0, A)
         for i in range(2):
-            centred_square(square_c[i], h_c[i][:])
+            centred_square(square_c[i], h_c[i])
         for i in range(2):
             lower_on_scalar(slope_c[i], square_c[i])
         for t in range(PACK):

@@ -32,11 +32,11 @@ SUMS = [
     (0, 1024, 2048, "tensor"),
     (1, 0, 512, "gpsimd"),
     (1, 512, 1024, "tensor"),
-    (1, 1024, 1408, "gpsimd"),
-    (1, 1408, 1792, "vector"),
+    (1, 1024, 1280, "gpsimd"),
+    (1, 1280, 1792, "vector"),
     (1, 1792, 2048, "vector"),
 ]
-STORES = [(0, 0, 512), (1, 0, 128), (1, 128, 256), (1, 256, 352), (1, 352, 512)]
+STORES = [(0, 0, 512), (1, 0, 128), (1, 128, 256), (1, 256, 320), (1, 320, 512)]
 
 
 def tile_attend_gmp_sig_kernel(tc, dyT, hE, w_words, w_scales, offs, offs2, out):

@@ -24,19 +24,20 @@ PER_COLUMN = 16
 BANK = 512
 BANKS = 8
 A, B, C = 1024, 512, 512
+HELPED = 768
 SPARE = 32
 RUN = 4
 LAP = 32
 SUMS = [
-    (0, 0, 1024, "gpsimd"),
-    (0, 1024, 2048, "tensor"),
-    (1, 0, 512, "gpsimd"),
-    (1, 512, 1024, "tensor"),
-    (1, 1024, 1280, "gpsimd"),
-    (1, 1280, 1792, "vector"),
-    (1, 1792, 2048, "vector"),
+    (0, 0, 768, "gpsimd"),
+    (0, 768, 1536, "gpsimd"),
+    (0, 1536, 2048, "tensor"),
+    (1, 0, 512, "tensor"),
+    (1, 512, 1152, "gpsimd"),
+    (1, 1152, 1664, "vector"),
+    (1, 1664, 2048, "vector"),
 ]
-STORES = [(0, 0, 512), (1, 0, 128), (1, 128, 256), (1, 256, 320), (1, 320, 512)]
+STORES = [(0, 0, 512), (1, 0, 128), (1, 128, 416), (1, 416, 512)]
 
 
 def tile_attend_gmp_sig_kernel(tc, dyT, hE, w_words, w_scales, offs, offs2, out):
@@ -175,6 +176,7 @@ def tile_attend_gmp_sig_kernel(tc, dyT, hE, w_words, w_scales, offs, offs2, out)
         multiply_a(2, 0, A)
         centred_square(square_a[3][:, piece:], h_a[3][:, piece:])
         copy_b(3)
+        lower_on_scalar(slope_a[3][:, HELPED:], square_a[3][:, HELPED:])
 
         def turn(k):
             across = bank[4 + k % 2]
@@ -251,7 +253,7 @@ def tile_attend_gmp_sig_kernel(tc, dyT, hE, w_words, w_scales, offs, offs2, out)
 
         finish_block(2)
         finish_block(3)
-        lower_on_gpsimd(slope_a[3], square_a[3])
+        lower_on_gpsimd(slope_a[3][:, :HELPED], square_a[3][:, :HELPED])
         multiply_a(3, 0, A)
         for i in range(2):
             centred_square(square_c[i], h_c[i])

@@ -65,7 +65,8 @@ def tile_attend_gmp_sig_kernel(tc, dyT, hE, w_words, w_scales, offs, offs2, out)
         square2_at = PACK * B - LAP
         h3_at = PACK * B + 3 * A - 4 * LAP
         step = A + h3_at + A - LAP
-        rows = fresh("rows", PACK * step)
+        work = fresh("work", (PACK - 1) * C + PACK * step)
+        rows = work[:, (PACK - 1) * C :]
         product_a = rows.rearrange("p (t x) -> p t x", t=PACK)[:, :, :A]
         gaps = [rows[:, t * step + A : (t + 1) * step] for t in range(PACK)]
         ahead = rows[:, 2 * step + A :]
@@ -93,7 +94,7 @@ def tile_attend_gmp_sig_kernel(tc, dyT, hE, w_words, w_scales, offs, offs2, out)
         slope_a0 = [spare[1][:, piece:], fresh("slope_a0", piece)]
         slope_a = [None, spare[3], around_c[:, :A], around_c[:, A - LAP : 2 * A - LAP]]
         slope_c = [fresh("slope_c%d" % i, 2 * C) for i in range(2)]
-        product_c = keep.tile([P, PACK, C], F32, name="product_c")
+        product_c = work[:, : PACK * C].rearrange("p (t e) -> p t e", t=PACK)
         square_b = [spare[4][:, :BANK], spare[4][:, BANK:]] + [
             ahead[:, h3_at + i * BANK : h3_at + (i + 1) * BANK] for i in range(2)
         ]
@@ -259,7 +260,7 @@ def tile_attend_gmp_sig_kernel(tc, dyT, hE, w_words, w_scales, offs, offs2, out)
             centred_square(square_c[i], h_c[i])
         for i in range(2):
             lower_on_scalar(slope_c[i], square_c[i])
-        for t in range(PACK):
+        for t in range(PACK - 1):
             multiply_c(t)
         quantise(grouped_b[:, B // 2 :, :], A + B // 2)
         pieces = []
@@ -267,6 +268,8 @@ def tile_attend_gmp_sig_kernel(tc, dyT, hE, w_words, w_scales, offs, offs2, out)
             quantise(rounded(home, product_a[:, :, i * BANK : (i + 1) * BANK]), i * BANK)
             pieces.append(first_half(i * BANK, (i + 1) * BANK, bank[4 + 2 * i]))
             multiply(1, i * BANK, bank[5 + 2 * i])
+            if i == 0:
+                multiply_c(PACK - 1)
         finish_block(0)
         finish_block(1)
         grouped_c = [rounded(fresh("grouped_c%d" % i, C), product_c[:, :, i * C // 2 : (i + 1) * C // 2]) for i in range(2)]

@@ -27,6 +27,7 @@ A, B, C = 1024, 512, 512
 HELPED = 768
 SPARE = 32
 RUN = 4
+PAIR = 2
 LAP = 32
 SUMS = [
     (0, 0, 768, "gpsimd"),
@@ -65,8 +66,8 @@ def tile_attend_gmp_sig_kernel(tc, dyT, hE, w_words, w_scales, offs, offs2, out)
         square2_at = PACK * B - LAP
         h3_at = PACK * B + 3 * A - 4 * LAP
         step = A + h3_at + A - LAP
-        work = fresh("work", (PACK - 1) * C + PACK * step)
-        rows = work[:, (PACK - 1) * C :]
+        work = fresh("work", PACK * C - C + PACK * step)
+        rows = work[:, PACK * C - C :]
         product_a = rows.rearrange("p (t x) -> p t x", t=PACK)[:, :, :A]
         gaps = [rows[:, t * step + A : (t + 1) * step] for t in range(PACK)]
         ahead = rows[:, 2 * step + A :]
@@ -94,7 +95,7 @@ def tile_attend_gmp_sig_kernel(tc, dyT, hE, w_words, w_scales, offs, offs2, out)
         slope_a0 = [spare[1][:, piece:], fresh("slope_a0", piece)]
         slope_a = [None, spare[3], around_c[:, :A], around_c[:, A - LAP : 2 * A - LAP]]
         slope_c = [fresh("slope_c%d" % i, 2 * C) for i in range(2)]
-        product_c = work[:, : PACK * C].rearrange("p (t e) -> p t e", t=PACK)
+        product_c = [work[:, i * 2 * C : (i + 1) * 2 * C].rearrange("p (t e) -> p t e", t=PACK) for i in range(2)]
         square_b = [spare[4][:, :BANK], spare[4][:, BANK:]] + [
             ahead[:, h3_at + i * BANK : h3_at + (i + 1) * BANK] for i in range(2)
         ]
@@ -131,11 +132,11 @@ def tile_attend_gmp_sig_kernel(tc, dyT, hE, w_words, w_scales, offs, offs2, out)
             )
         nc.sync.dma_start(src[:], offs2)
 
-        def as_runs_out(values):
-            return values.rearrange("p (c i) t -> p c t i", i=RUN)
+        def as_runs_out(values, run=RUN):
+            return values.rearrange("p (c i) t -> p c t i", i=run)
 
-        def as_runs_in(values):
-            return values.rearrange("p t (c i) -> p c t i", i=RUN)
+        def as_runs_in(values, run=RUN):
+            return values.rearrange("p t (c i) -> p c t i", i=run)
 
         def columns(t, e0, e1):
             return dy[t][:].indirect(dst[:, e0 // PER_COLUMN : e1 // PER_COLUMN])
@@ -214,12 +215,14 @@ def tile_attend_gmp_sig_kernel(tc, dyT, hE, w_words, w_scales, offs, offs2, out)
                 ALU.mult,
             )
 
-        def multiply_c(t):
-            nc.vector.tensor_tensor(product_c[:, t, :], columns(t, A + B, E), slope_c[t // 2][:, t % 2 * C : (t % 2 + 1) * C], ALU.mult)
+        def multiply_c(t, i):
+            e0, e1 = i * C // 2, (i + 1) * C // 2
+            slope = slope_c[t // 2][:, t % 2 * C + e0 : t % 2 * C + e1]
+            nc.vector.tensor_tensor(product_c[i][:, t, :], columns(t, A + B + e0, A + B + e1), slope, ALU.mult)
 
         def rounded(home, values):
             grouped = home.bitcast(BF16).rearrange("p (e t) -> p e t", t=PACK)
-            nc.scalar.activation(as_runs_out(grouped), as_runs_in(values), COPY)
+            nc.scalar.activation(as_runs_out(grouped, PAIR), as_runs_in(values, PAIR), COPY)
             return grouped
 
         def multiply(half, e0, acc):
@@ -260,8 +263,10 @@ def tile_attend_gmp_sig_kernel(tc, dyT, hE, w_words, w_scales, offs, offs2, out)
             centred_square(square_c[i], h_c[i])
         for i in range(2):
             lower_on_scalar(slope_c[i], square_c[i])
-        for t in range(PACK - 1):
-            multiply_c(t)
+        for t in range(PACK):
+            multiply_c(t, 0)
+        for t in range(2):
+            multiply_c(t, 1)
         quantise(grouped_b[:, B // 2 :, :], A + B // 2)
         pieces = []
         for i, home in enumerate((grouped_a[:, :A], grouped_a[:, A:])):
@@ -269,10 +274,11 @@ def tile_attend_gmp_sig_kernel(tc, dyT, hE, w_words, w_scales, offs, offs2, out)
             pieces.append(first_half(i * BANK, (i + 1) * BANK, bank[4 + 2 * i]))
             multiply(1, i * BANK, bank[5 + 2 * i])
             if i == 0:
-                multiply_c(PACK - 1)
+                for t in range(2, PACK):
+                    multiply_c(t, 1)
         finish_block(0)
         finish_block(1)
-        grouped_c = [rounded(fresh("grouped_c%d" % i, C), product_c[:, :, i * C // 2 : (i + 1) * C // 2]) for i in range(2)]
+        grouped_c = [rounded(fresh("grouped_c%d" % i, C), product_c[i]) for i in range(2)]
         quantise(grouped_c[0], A + B)
         quantise(grouped_b[:, : B // 2, :], A)
         quantise(grouped_c[1], A + B + C // 2)

@@ -89,14 +89,14 @@ def tile_attend_gmp_sig_kernel(tc, dyT, hE, w_words, w_scales, offs, offs2, out)
             ahead[:, square2_at : square2_at + A],
             ahead[:, square1_at : square1_at + A],
         ]
-        h_c = spare[5:]
+        h_c = [spare[5], fresh("h_c1", 2 * C)]
         square_c = [spare[2], h_b_homes[0]]
         around_c = gaps[3][:, B + 2 * A : B + 4 * A - LAP]
         slope_a0 = [spare[1][:, piece:], fresh("slope_a0", piece)]
         slope_a = [None, spare[3], around_c[:, :A], around_c[:, A - LAP : 2 * A - LAP]]
         slope_c = [fresh("slope_c%d" % i, 2 * C) for i in range(2)]
         product_c = [work[:, i * 2 * C : (i + 1) * 2 * C].rearrange("p (t e) -> p t e", t=PACK) for i in range(2)]
-        square_b = [spare[4][:, :BANK], spare[4][:, BANK:]] + [
+        square_b = [h_c[1][:, :BANK], h_c[1][:, BANK:]] + [
             ahead[:, h3_at + i * BANK : h3_at + (i + 1) * BANK] for i in range(2)
         ]
 
@@ -185,9 +185,9 @@ def tile_attend_gmp_sig_kernel(tc, dyT, hE, w_words, w_scales, offs, offs2, out)
             for t in range(PACK):
                 e0 = k % 2 * P
                 nc.tensor.transpose(across[:, t * P : (t + 1) * P], h_b[k // 2][:, t, e0 : e0 + P], ident[:])
-            centred_square(square_b[k], across[:])
 
         def turn_back(k):
+            centred_square(square_b[k], bank[4 + k % 2][:])
             for t in range(PACK):
                 cols = slice(t * P, (t + 1) * P)
                 nc.tensor.matmul(
@@ -200,11 +200,11 @@ def tile_attend_gmp_sig_kernel(tc, dyT, hE, w_words, w_scales, offs, offs2, out)
                 nc.tensor.matmul(
                     bank[k][:, t * P : (t + 1) * P], quarter[:], ident[:], start=t == 0, stop=False, is_transpose=True
                 )
-        for pair in (order[:2], order[2:]):
-            for k in pair:
-                turn(k)
-            for k in pair:
-                turn_back(k)
+        for step_of_block in (turn, turn_back):
+            for k in order[:2]:
+                step_of_block(k)
+        for k in order[2:]:
+            turn(k)
 
         def finish_block(k):
             e0 = k * P
@@ -263,6 +263,8 @@ def tile_attend_gmp_sig_kernel(tc, dyT, hE, w_words, w_scales, offs, offs2, out)
             centred_square(square_c[i], h_c[i])
         for i in range(2):
             lower_on_scalar(slope_c[i], square_c[i])
+        for k in order[2:]:
+            turn_back(k)
         for t in range(PACK):
             multiply_c(t, 0)
         for t in range(2):

@@ -1,7 +1,6 @@
 from contextlib import ExitStack
 
 import concourse.mybir as mybir
-from concourse.masks import make_identity
 
 V, K, E, D, DV = 512, 4, 2048, 256, 512
 FLOPS = 2 * DV * D * E
@@ -16,29 +15,18 @@ E4M3X4 = mybir.dt.float8_e4m3fn_x4
 E5M2X4 = mybir.dt.float8_e5m2_x4
 ALU = mybir.AluOpType
 COPY = mybir.ActivationFunctionType.Copy
-SQUARE = mybir.ActivationFunctionType.Square
 
 P = 128
 PACK = 4
+HALVES = D // P
 PER_COLUMN = 16
 BANK = 512
-BANKS = 8
-A, B, C = 1024, 512, 512
-HELPED = 768
 SPARE = 32
-RUN = 4
 PAIR = 2
-LAP = 32
-SUMS = [
-    (0, 0, 768, "gpsimd"),
-    (0, 768, 1536, "gpsimd"),
-    (0, 1536, 2048, "tensor"),
-    (1, 0, 512, "tensor"),
-    (1, 512, 1152, "gpsimd"),
-    (1, 1152, 1664, "vector"),
-    (1, 1664, 2048, "vector"),
-]
-STORES = [(0, 0, 512), (1, 0, 128), (1, 128, 416), (1, 416, 512)]
+HEAD = 128
+LONG = 512
+CHUNKS = [(HEAD + i * LONG, HEAD + (i + 1) * LONG) for i in range(3)] + [(HEAD + 3 * LONG, E)]
+LAST = 128
 
 
 def tile_attend_gmp_sig_kernel(tc, dyT, hE, w_words, w_scales, offs, offs2, out):
@@ -49,282 +37,176 @@ def tile_attend_gmp_sig_kernel(tc, dyT, hE, w_words, w_scales, offs, offs2, out)
 
         dst = keep.tile([P, E // PER_COLUMN], U16, name="dst")
         src = keep.tile([P, E // PER_COLUMN], U16, name="src")
-        dy = [keep.tile([P, A + SPARE], F32, name="dy%d" % t) for t in range(PACK)]
-        ident = keep.tile([P, P], F32, name="ident")
-        quarter = keep.tile([P, P], F32, name="quarter")
+        dy = [keep.tile([P, V + SPARE], F32, name="dy%d" % t) for t in range(PACK)]
         dz_codes = keep.tile([P, E], U32, name="dz_codes", align_bytes=64)
         w_codes = keep.tile([P, D], U32, name="w_codes", align_bytes=64)
         w_scale = keep.tile([P, D], U8, name="w_scale", align_bytes=64)
         dz_scale = keep.tile([P, E], U8, name="dz_scale", align_bytes=64)
-        dm = [keep.tile([P, E], F32, name="dm%d" % half) for half in range(D // P)]
-        bank = [psum.tile([P, BANK], F32, name="bank%d" % b) for b in range(BANKS)]
+        dm = [keep.tile([P, E], F32, name="dm%d" % half) for half in range(HALVES)]
+        bank = [[psum.tile([P, BANK], F32, name="bank%d_%d" % (half, b)) for b in range(4)] for half in range(HALVES)]
 
-        def fresh(name, columns):
-            return keep.tile([P, columns], F32, name=name, align_bytes=64)[:]
+        def row_sets(name, edges, dtype=F32):
+            return keep.tile([P, PACK, edges], dtype, name=name, align_bytes=64)
 
-        piece = A // 2
-        square2_at = PACK * B - LAP
-        h3_at = PACK * B + 3 * A - 4 * LAP
-        step = A + h3_at + A - LAP
-        work = fresh("work", PACK * C - C + PACK * step)
-        rows = work[:, PACK * C - C :]
-        product_a = rows.rearrange("p (t x) -> p t x", t=PACK)[:, :, :A]
-        gaps = [rows[:, t * step + A : (t + 1) * step] for t in range(PACK)]
-        ahead = rows[:, 2 * step + A :]
-        grouped_b = rows[:, 3 * step + piece : 3 * step + piece + 2 * B]
-        grouped_b = grouped_b.bitcast(BF16).rearrange("p (e t) -> p e t", t=PACK)
-        looked_up = ahead[:, : PACK * B].rearrange("p (t e) -> p t e", t=PACK)
-        spare = [gaps[0][:, i * A : (i + 1) * A] for i in range(5)] + [gaps[1][:, i * A : (i + 1) * A] for i in (2, 3)]
-        grouped_a = gaps[3][:, B : B + 2 * A]
-        h_b_homes = [grouped_a[:, piece : piece + 2 * B], spare[0]]
-        h_b = [home.rearrange("p (t e) -> p t e", t=PACK) for home in h_b_homes]
-        square0_at = square2_at + A - LAP
-        square1_at = square0_at + A - 2 * LAP
-        h_a0 = [ahead[:, square0_at + piece - LAP : square0_at + A - LAP], spare[1][:, :piece]]
-        square_a0 = [looked_up[:, 2, :], ahead[:, square0_at : square0_at + piece]]
-        h_a = [None, gaps[1][:, :A], gaps[1][:, A : 2 * A], ahead[:, h3_at : h3_at + A]]
-        square_a = [
-            None,
-            ahead[:, square1_at : square1_at + A],
-            ahead[:, square2_at : square2_at + A],
-            ahead[:, square1_at : square1_at + A],
-        ]
-        h_c = [spare[5], fresh("h_c1", 2 * C)]
-        square_c = [spare[2], h_b_homes[0]]
-        around_c = gaps[3][:, B + 2 * A : B + 4 * A - LAP]
-        slope_a0 = [spare[1][:, piece:], fresh("slope_a0", piece)]
-        slope_a = [None, spare[3], around_c[:, :A], around_c[:, A - LAP : 2 * A - LAP]]
-        slope_c = [fresh("slope_c%d" % i, 2 * C) for i in range(2)]
-        product_c = [work[:, i * 2 * C : (i + 1) * 2 * C].rearrange("p (t e) -> p t e", t=PACK) for i in range(2)]
-        square_b = [h_c[1][:, :BANK], h_c[1][:, BANK:]] + [
-            ahead[:, h3_at + i * BANK : h3_at + (i + 1) * BANK] for i in range(2)
-        ]
+        h_head = [keep.tile([P, HEAD], F32, name="h_head%d" % t) for t in range(PACK)]
+        h = [[keep.tile([P, 2, e1 - e0], F32, name="h%d_%d" % (c, i)) for i in range(2)] for c, (e0, e1) in enumerate(CHUNKS)]
+        slope = [row_sets("slope%d" % c, e1 - e0) for c, (e0, e1) in enumerate(CHUNKS)]
+        homes = [row_sets("looked_up%d" % c, LONG) for c in range(3)]
+        looked_up = [homes[c % 3][:, :, : e1 - e0] for c, (e0, e1) in enumerate(CHUNKS)]
+        head_less_one = homes[1][:, :, :HEAD]
+        head_product = homes[2][:, :, :HEAD]
 
         dy_rows = dyT.rearrange("(p t) x -> t p x", t=PACK)
         h_rows = hE.rearrange("(p t) e -> p t e", t=PACK)
 
-        for t in range(2):
-            nc.vector.memset(dy[t][:, V:], 0.0)
-        make_identity(nc, ident[:])
-        for t in range(2, PACK):
+        for t in range(PACK):
             nc.gpsimd.memset(dy[t][:, V:], 0.0)
-        nc.gpsimd.memset(quarter[:], -0.25)
         nc.gpsimd.memset(w_scale[:].bitcast(I32), 0)
 
+        def load_h(c):
+            e0, e1 = CHUNKS[c]
+            for i in range(2):
+                nc.sync.dma_start(h[c][i][:], h_rows[:, 2 * i : 2 * i + 2, e0:e1])
+
         nc.sync.dma_start(dst[:], offs)
-        nc.sync.dma_start(dy[0][:, :V], dy_rows[0])
-        nc.sync.dma_start(h_a0[0], h_rows[:, 0, : A // 2])
-        nc.sync.dma_start(dy[1][:, :V], dy_rows[1])
-        nc.sync.dma_start(h_a0[1], h_rows[:, 0, A // 2 : A])
-        nc.sync.dma_start(h_a[1], h_rows[:, 1, :A])
-        nc.sync.dma_start(dy[2][:, :V], dy_rows[2])
-        nc.sync.dma_start(h_a[2], h_rows[:, 2, :A])
-        nc.sync.dma_start(h_a[3], h_rows[:, 3, :A])
-        nc.sync.dma_start(dy[3][:, :V], dy_rows[3])
-        for i in (1, 0):
-            nc.sync.dma_start(h_b[i], h_rows[:, :, A + i * B // 2 : A + (i + 1) * B // 2])
-        for i in range(2):
-            nc.sync.dma_start(h_c[i].rearrange("p (t e) -> p t e", t=2), h_rows[:, 2 * i : 2 * i + 2, A + B :])
+        for t in range(PACK):
+            nc.sync.dma_start(dy[t][:, :V], dy_rows[t])
+            nc.sync.dma_start(h_head[t][:], h_rows[:, t, :HEAD])
+        load_h(0)
+        load_h(1)
         nc.sync.dma_start(w_codes[:].bitcast(I32), w_words[0].rearrange("p d r -> p (d r)").bitcast(I32))
         for q in range(4):
             nc.sync.dma_start(
                 w_scale[32 * q : 32 * q + 4, :].bitcast(I32), w_scales[0, 4 * q : 4 * q + 4, :].bitcast(I32)
             )
+        load_h(2)
+        load_h(3)
         nc.sync.dma_start(src[:], offs2)
-
-        def as_runs_out(values, run=RUN):
-            return values.rearrange("p (c i) t -> p c t i", i=run)
-
-        def as_runs_in(values, run=RUN):
-            return values.rearrange("p t (c i) -> p c t i", i=run)
 
         def columns(t, e0, e1):
             return dy[t][:].indirect(dst[:, e0 // PER_COLUMN : e1 // PER_COLUMN])
 
-        def centred_square(square, h):
-            nc.scalar.activation(square, h, SQUARE, bias=-0.5, scale=1.0)
-            return square
-
-        def lower_on_scalar(slope, square):
-            nc.scalar.activation(slope, square, COPY, bias=-0.25, scale=1.0)
-
-        def lower_on_gpsimd(slope, square):
-            nc.gpsimd.tensor_scalar(slope, square, 1.0, -0.25, ALU.mult, ALU.add)
-
-        def copy_b(t):
-            nc.vector.tensor_copy(looked_up[:, t, :], columns(t, A, A + B))
-
-        def multiply_a(t, e0, e1):
-            nc.vector.tensor_tensor(product_a[:, t, e0:e1], columns(t, e0, e1), slope_a[t][:, e0:e1], ALU.mult)
-
-        copy_b(0)
-        copy_b(1)
-        def multiply_a0(i):
-            e0, e1 = i * piece, (i + 1) * piece
-            nc.vector.tensor_tensor(product_a[:, 0, e0:e1], columns(0, e0, e1), slope_a0[i], ALU.mult)
-
-        lower_on_scalar(slope_a0[0], centred_square(square_a0[0], h_a0[0]))
-        multiply_a0(0)
-        copy_b(2)
-        centred_square(square_a0[1], h_a0[1])
-        centred_square(square_a[1], h_a[1])
-        lower_on_scalar(slope_a0[1], square_a0[1])
-        multiply_a0(1)
-        lower_on_scalar(slope_a[1], square_a[1])
-        multiply_a(1, 0, A)
-        centred_square(square_a[2], h_a[2])
-        centred_square(square_a[3][:, :piece], h_a[3][:, :piece])
-        lower_on_scalar(slope_a[2], square_a[2])
-        multiply_a(2, 0, A)
-        centred_square(square_a[3][:, piece:], h_a[3][:, piece:])
-        copy_b(3)
-        lower_on_scalar(slope_a[3][:, HELPED:], square_a[3][:, HELPED:])
-
-        def turn(k):
-            across = bank[4 + k % 2]
+        def look_up(c):
             for t in range(PACK):
-                e0 = k % 2 * P
-                nc.tensor.transpose(across[:, t * P : (t + 1) * P], h_b[k // 2][:, t, e0 : e0 + P], ident[:])
+                nc.scalar.activation(looked_up[c][:, t, :], columns(t, *CHUNKS[c]), COPY)
 
-        def turn_back(k):
-            centred_square(square_b[k], bank[4 + k % 2][:])
-            for t in range(PACK):
-                cols = slice(t * P, (t + 1) * P)
-                nc.tensor.matmul(
-                    bank[k][:, cols], square_b[k][:, cols], ident[:], start=False, stop=t == PACK - 1, is_transpose=True
-                )
+        def make_slope(c):
+            for i in range(2):
+                rows = h[c][i][:].rearrange("p t e -> p (t e)")
+                lowered = slope[c][:, 2 * i : 2 * i + 2, :].rearrange("p t e -> p (t e)")
+                nc.vector.scalar_tensor_tensor(lowered, rows, 1.0, rows, ALU.subtract, ALU.mult)
 
-        order = [2, 3, 0, 1]
-        for k in order:
-            for t in range(PACK):
-                nc.tensor.matmul(
-                    bank[k][:, t * P : (t + 1) * P], quarter[:], ident[:], start=t == 0, stop=False, is_transpose=True
-                )
-        for step_of_block in (turn, turn_back):
-            for k in order[:2]:
-                step_of_block(k)
-        for k in order[2:]:
-            turn(k)
-
-        def finish_block(k):
-            e0 = k * P
+        def product(name, a, b):
+            grouped = keep.tile([P, a.shape[2], PACK], BF16, name=name, align_bytes=64)
             nc.vector.tensor_tensor(
-                as_runs_out(grouped_b[:, e0 : e0 + P, :]),
-                as_runs_in(looked_up[:, :, e0 : e0 + P]),
-                as_runs_in(bank[k][:].rearrange("p (t e) -> p t e", t=PACK)),
+                grouped[:].rearrange("p (c i) t -> p c t i", i=PAIR),
+                a.rearrange("p t (c i) -> p c t i", i=PAIR),
+                b.rearrange("p t (c i) -> p c t i", i=PAIR),
                 ALU.mult,
             )
-
-        def multiply_c(t, i):
-            e0, e1 = i * C // 2, (i + 1) * C // 2
-            slope = slope_c[t // 2][:, t % 2 * C + e0 : t % 2 * C + e1]
-            nc.vector.tensor_tensor(product_c[i][:, t, :], columns(t, A + B + e0, A + B + e1), slope, ALU.mult)
-
-        def rounded(home, values):
-            grouped = home.bitcast(BF16).rearrange("p (e t) -> p e t", t=PACK)
-            nc.scalar.activation(as_runs_out(grouped, PAIR), as_runs_in(values, PAIR), COPY)
             return grouped
-
-        def multiply(half, e0, acc):
-            d_cols = slice(half * P, (half + 1) * P)
-            nc.tensor.matmul_mx(
-                out=acc[:],
-                lhsT=w_codes[:, d_cols].bitcast(E4M3X4),
-                lhsT_scale=w_scale[:, d_cols],
-                rhs=dz_codes[:, e0 : e0 + BANK].bitcast(E5M2X4),
-                rhs_scale=dz_scale[:, e0 : e0 + BANK],
-                start=True,
-                stop=True,
-            )
 
         def quantise(grouped, e0):
             e1 = e0 + grouped.shape[1]
             nc.vector.quantize_mx(
                 out=dz_codes[:, e0:e1].bitcast(E5M2X4),
                 scales=dz_scale[:, e0:e1],
-                in_=grouped.rearrange("p e t -> p (e t)"),
+                in_=grouped[:].rearrange("p e t -> p (e t)"),
             )
 
-        def first_half(e0, e1, acc):
-            multiply(0, e1 - BANK, acc)
-            return dm[0][:, e0:e1], acc[:, BANK - (e1 - e0) :]
+        def multiply(e0, e1, b):
+            for half in range(HALVES):
+                d_cols = slice(half * P, (half + 1) * P)
+                nc.tensor.matmul_mx(
+                    out=bank[half][b][:, : e1 - e0],
+                    lhsT=w_codes[:, d_cols].bitcast(E4M3X4),
+                    lhsT_scale=w_scale[:, d_cols],
+                    rhs=dz_codes[:, e0:e1].bitcast(E5M2X4),
+                    rhs_scale=dz_scale[:, e0:e1],
+                    start=True,
+                    stop=True,
+                )
 
-        def empty_on_scalar(columns_of_dm, acc):
-            nc.scalar.activation(columns_of_dm, acc, COPY, scale=-1.0)
+        def empty_on_scalar(half, e0, e1, b):
+            nc.scalar.activation(dm[half][:, e0:e1], bank[half][b][:, : e1 - e0], COPY, scale=-1.0)
 
-        def empty_on_vector(columns_of_dm, acc):
-            nc.vector.tensor_scalar(columns_of_dm, acc, -1.0, None, ALU.mult)
+        def empty_on_vector(half, e0, e1, b):
+            nc.vector.tensor_scalar(dm[half][:, e0:e1], bank[half][b][:, : e1 - e0], -1.0, None, ALU.mult)
 
-        finish_block(2)
-        finish_block(3)
-        lower_on_gpsimd(slope_a[3][:, :HELPED], square_a[3][:, :HELPED])
-        multiply_a(3, 0, A)
-        for i in range(2):
-            centred_square(square_c[i], h_c[i])
-        for i in range(2):
-            lower_on_scalar(slope_c[i], square_c[i])
-        for k in order[2:]:
-            turn_back(k)
-        for t in range(PACK):
-            multiply_c(t, 0)
-        for t in range(2):
-            multiply_c(t, 1)
-        quantise(grouped_b[:, B // 2 :, :], A + B // 2)
-        pieces = []
-        for i, home in enumerate((grouped_a[:, :A], grouped_a[:, A:])):
-            quantise(rounded(home, product_a[:, :, i * BANK : (i + 1) * BANK]), i * BANK)
-            pieces.append(first_half(i * BANK, (i + 1) * BANK, bank[4 + 2 * i]))
-            multiply(1, i * BANK, bank[5 + 2 * i])
-            if i == 0:
-                for t in range(2, PACK):
-                    multiply_c(t, 1)
-        finish_block(0)
-        finish_block(1)
-        grouped_c = [rounded(fresh("grouped_c%d" % i, C), product_c[i]) for i in range(2)]
-        quantise(grouped_c[0], A + B)
-        quantise(grouped_b[:, : B // 2, :], A)
-        quantise(grouped_c[1], A + B + C // 2)
-        pieces.append(first_half(A + B // 2, A + B + C // 2, bank[2]))
-        pieces.append(first_half(A, A + B // 2, bank[3]))
-        last = first_half(A + B + C // 2, E, bank[0])
-        for piece in pieces:
-            empty_on_scalar(*piece)
-        empty_on_vector(*last)
-        multiply(1, 3 * BANK, bank[3])
-        multiply(1, 2 * BANK, bank[0])
-        for c, b in enumerate((5, 7, 0, 3)):
-            empty_on_scalar(dm[1][:, c * BANK : (c + 1) * BANK], bank[b][:])
+        for c in range(len(CHUNKS)):
+            if c == 1:
+                for t in range(PACK):
+                    nc.vector.tensor_tensor(head_product[:, t, :], columns(t, 0, HEAD), h_head[t][:], ALU.mult)
+                    nc.vector.tensor_scalar(head_less_one[:, t, :], h_head[t][:], -1.0, None, ALU.add)
+                grouped = product("grouped_head", head_product, head_less_one)
+            if c == 3:
+                continue
+            look_up(c)
 
-        def pick(half, s0, s1):
-            picked = keep.tile([P, s1 - s0], F32, name="picked%d_%d" % (half, s0))
-            nc.vector.tensor_copy(picked[:], dm[half][:].indirect(src[:, s0 // PER_COLUMN : s1 // PER_COLUMN]))
-            return picked[:].rearrange("p (x j) -> p x j", j=K)
+        waiting = (grouped, 0, HEAD, 0)
+        emptied = []
+        for c, (e0, e1) in enumerate(CHUNKS):
+            make_slope(c)
+            quantise(waiting[0], waiting[1])
+            multiply(*waiting[1:])
+            emptied.append(waiting[1:])
+            if c < 3:
+                waiting = (product("grouped%d" % c, looked_up[c], slope[c][:]), e0, e1, c + 1)
+            if c == 0:
+                look_up(3)
+        for piece in emptied:
+            for half in range(HALVES):
+                empty_on_scalar(half, *piece)
+        e0, e1 = CHUNKS[3]
+        cut = e1 - e0 - LAST
+        tail = [
+            (product("grouped_a", looked_up[3][:, :, :cut], slope[3][:, :, :cut]), e0, e0 + cut, 0),
+            (product("grouped_b", looked_up[3][:, :, cut:], slope[3][:, :, cut:]), e0 + cut, e1, 1),
+        ]
+        for piece in tail:
+            quantise(piece[0], piece[1])
+            multiply(*piece[1:])
+        for piece in tail:
+            empty_on_vector(0, *piece[1:])
+            empty_on_scalar(1, *piece[1:])
 
-        sums = [keep.tile([P, V], F32, name="sums%d" % half) for half in range(D // P)]
-        waiting = []
-        turns = 0
-        for half, s0, s1, adder in SUMS:
-            picked = pick(half, s0, s1)
-            x0, x1 = s0 // K, s1 // K
-            if adder == "gpsimd":
-                pairs = keep.tile([P, x1 - x0, 2], F32, name="pairs%d_%d" % (half, s0))
-                nc.gpsimd.tensor_tensor(pairs[:], picked[:, :, 0:2], picked[:, :, 2:4], ALU.add)
-                nc.gpsimd.tensor_tensor(sums[half][:, x0:x1], pairs[:, :, 0], pairs[:, :, 1], ALU.add)
-            elif adder == "tensor":
-                for x in range(0, x1 - x0, P):
-                    across, back = bank[4 - turns % 2], bank[5 + turns % 2]
-                    for j in range(K):
-                        nc.tensor.matmul(
-                            across[:, :P], picked[:, x : x + P, j], ident[:], start=j == 0, stop=j == K - 1, is_transpose=True
-                        )
-                    turned = keep.tile([P, P], F32, name="turned%d" % turns)
-                    nc.scalar.copy(turned[:], across[:, :P])
-                    nc.tensor.transpose(back[:, :P], turned[:], ident[:])
-                    nc.scalar.copy(sums[half][:, x0 + x : x0 + x + P], back[:, :P])
-                    turns = turns + 1
-            else:
-                waiting.append((half, x0, x1, picked))
-        for half, x0, x1, picked in waiting:
-            nc.vector.tensor_reduce(sums[half][:, x0:x1], picked, mybir.AxisListType.X, ALU.add)
-        for half, x0, x1 in STORES:
-            nc.sync.dma_start(out[half * P : (half + 1) * P, x0:x1], sums[half][:, x0:x1])
+        out_halves = out.rearrange("(h p) x -> p h x", h=HALVES)
+
+        def listed(half, s0, s1):
+            return dm[half][:].indirect(src[:, s0 // PER_COLUMN : s1 // PER_COLUMN])
+
+        def both(name, columns):
+            return keep.tile([P, HALVES, columns], F32, name=name)
+
+        def by_node(entries):
+            return entries.rearrange("p h (x j) -> p h x j", j=K)
+
+        def add_up(sums, entries):
+            nc.vector.tensor_reduce(sums, by_node(entries), mybir.AxisListType.X, ALU.add)
+
+        pairs = keep.tile([P, V // 2, HALVES, 2], F32, name="pairs")
+        for s0, s1 in ((0, 256), (256, 640), (640, 1024)):
+            picked = both("picked%d" % s0, s1 - s0)
+            nc.vector.tensor_copy(picked[:, 0, :], listed(0, s0, s1))
+            nc.scalar.activation(picked[:, 1, :], listed(1, s0, s1), COPY)
+            entries = picked[:].rearrange("p h (x j) -> p x h j", j=K)
+            nc.gpsimd.tensor_tensor(pairs[:, s0 // K : s1 // K], entries[:, :, :, 0:2], entries[:, :, :, 2:4], ALU.add)
+        front = both("front", V // 2)
+        nc.gpsimd.tensor_tensor(front[:].rearrange("p h x -> p x h"), pairs[:, :, :, 0], pairs[:, :, :, 1], ALU.add)
+
+        third, fourth = both("third", 512), both("fourth", 512)
+        middle, back = both("middle", 128), both("back", 128)
+        nc.vector.tensor_copy(third[:, 0, :], listed(0, 1024, 1536))
+        nc.vector.tensor_copy(fourth[:, 0, :128], listed(0, 1536, 1664))
+        nc.scalar.activation(third[:, 1, :], listed(1, 1024, 1536), COPY)
+        nc.scalar.activation(fourth[:, 1, :384], listed(1, 1536, 1920), COPY)
+        nc.scalar.activation(fourth[:, 0, 128:], listed(0, 1664, 2048), COPY)
+        nc.scalar.activation(fourth[:, 1, 384:], listed(1, 1920, 2048), COPY)
+        add_up(middle[:], third[:])
+        nc.sync.dma_start(out_halves[:, :, 256:384], middle[:])
+        nc.sync.dma_start(out_halves[:, :, :256], front[:])
+        add_up(back[:, 0:1, :32], fourth[:, 0:1, :128])
+        add_up(back[:, 1:2, :96], fourth[:, 1:2, :384])
+        add_up(back[:, 0:1, 32:], fourth[:, 0:1, 128:])
+        add_up(back[:, 1:2, 96:], fourth[:, 1:2, 384:])
+        nc.sync.dma_start(out_halves[:, :, 384:], back[:])

@@ -15,18 +15,19 @@ E4M3X4 = mybir.dt.float8_e4m3fn_x4
 E5M2X4 = mybir.dt.float8_e5m2_x4
 ALU = mybir.AluOpType
 COPY = mybir.ActivationFunctionType.Copy
+SQUARE = mybir.ActivationFunctionType.Square
 
 P = 128
 PACK = 4
 HALVES = D // P
 PER_COLUMN = 16
 BANK = 512
-SPARE = 32
-PAIR = 2
-HEAD = 128
-LONG = 512
-CHUNKS = [(HEAD + i * LONG, HEAD + (i + 1) * LONG) for i in range(3)] + [(HEAD + 3 * LONG, E)]
-LAST = 128
+FRONT = 896
+REAR = E - FRONT
+FIRST = 256
+SPARE = REAR + 32 - V
+STAGGER = 9
+PASSES = [(0, 512, 0), (512, 768, 1), (768, FRONT, 2), (FRONT, 1408, 3), (1408, 1664, 0), (1664, 1920, 1), (1920, E, 2)]
 
 
 def tile_attend_gmp_sig_kernel(tc, dyT, hE, w_words, w_scales, offs, offs2, out):
@@ -45,73 +46,74 @@ def tile_attend_gmp_sig_kernel(tc, dyT, hE, w_words, w_scales, offs, offs2, out)
         dm = [keep.tile([P, E], F32, name="dm%d" % half) for half in range(HALVES)]
         bank = [[psum.tile([P, BANK], F32, name="bank%d_%d" % (half, b)) for b in range(4)] for half in range(HALVES)]
 
-        def row_sets(name, edges, dtype=F32):
-            return keep.tile([P, PACK, edges], dtype, name=name, align_bytes=64)
+        def row_sets(name, edges):
+            return keep.tile([P, PACK, edges + STAGGER], F32, name=name, align_bytes=64)[:, :, :edges]
 
-        h_head = [keep.tile([P, HEAD], F32, name="h_head%d" % t) for t in range(PACK)]
-        h = [[keep.tile([P, 2, e1 - e0], F32, name="h%d_%d" % (c, i)) for i in range(2)] for c, (e0, e1) in enumerate(CHUNKS)]
-        slope = [row_sets("slope%d" % c, e1 - e0) for c, (e0, e1) in enumerate(CHUNKS)]
-        homes = [row_sets("looked_up%d" % c, LONG) for c in range(3)]
-        looked_up = [homes[c % 3][:, :, : e1 - e0] for c, (e0, e1) in enumerate(CHUNKS)]
-        head_less_one = homes[1][:, :, :HEAD]
-        head_product = homes[2][:, :, :HEAD]
+        h_front = row_sets("h_front", FRONT)
+        times_h = row_sets("times_h", FRONT)
+        h_rear = [keep.tile([P, PACK, e1 - e0], F32, name="h_rear%d" % e0) for e0, e1 in ((FRONT, 1408), (1408, E))]
+        square = row_sets("square", REAR)
+        looked_up = row_sets("looked_up", REAR)
+        grouped = keep.tile([P, E, PACK], BF16, name="grouped", align_bytes=64)
 
         dy_rows = dyT.rearrange("(p t) x -> t p x", t=PACK)
         h_rows = hE.rearrange("(p t) e -> p t e", t=PACK)
 
         for t in range(PACK):
-            nc.gpsimd.memset(dy[t][:, V:], 0.0)
+            nc.vector.memset(dy[t][:, V:], 0.0)
         nc.gpsimd.memset(w_scale[:].bitcast(I32), 0)
 
-        def load_h(c):
-            e0, e1 = CHUNKS[c]
-            for i in range(2):
-                nc.sync.dma_start(h[c][i][:], h_rows[:, 2 * i : 2 * i + 2, e0:e1])
-
         nc.sync.dma_start(dst[:], offs)
-        for t in range(PACK):
+        nc.sync.dma_start(dy[0][:, :V], dy_rows[0])
+        nc.sync.dma_start(h_front[:, 0, :FIRST], h_rows[:, 0, :FIRST])
+        nc.sync.dma_start(h_front[:, 0, FIRST:], h_rows[:, 0, FIRST:FRONT])
+        for t in range(1, PACK):
             nc.sync.dma_start(dy[t][:, :V], dy_rows[t])
-            nc.sync.dma_start(h_head[t][:], h_rows[:, t, :HEAD])
-        load_h(0)
-        load_h(1)
+            nc.sync.dma_start(h_front[:, t, :], h_rows[:, t, :FRONT])
+        nc.sync.dma_start(h_rear[0][:], h_rows[:, :, FRONT:1408])
+        nc.sync.dma_start(h_rear[1][:], h_rows[:, :, 1408:])
         nc.sync.dma_start(w_codes[:].bitcast(I32), w_words[0].rearrange("p d r -> p (d r)").bitcast(I32))
         for q in range(4):
             nc.sync.dma_start(
                 w_scale[32 * q : 32 * q + 4, :].bitcast(I32), w_scales[0, 4 * q : 4 * q + 4, :].bitcast(I32)
             )
-        load_h(2)
-        load_h(3)
         nc.sync.dma_start(src[:], offs2)
 
         def columns(t, e0, e1):
             return dy[t][:].indirect(dst[:, e0 // PER_COLUMN : e1 // PER_COLUMN])
 
-        def look_up(c):
-            for t in range(PACK):
-                nc.scalar.activation(looked_up[c][:, t, :], columns(t, *CHUNKS[c]), COPY)
+        def by_edge(values):
+            return values.rearrange("p t e -> p e t")
 
-        def make_slope(c):
-            for i in range(2):
-                rows = h[c][i][:].rearrange("p t e -> p (t e)")
-                lowered = slope[c][:, 2 * i : 2 * i + 2, :].rearrange("p t e -> p (t e)")
-                nc.vector.scalar_tensor_tensor(lowered, rows, 1.0, rows, ALU.subtract, ALU.mult)
-
-        def product(name, a, b):
-            grouped = keep.tile([P, a.shape[2], PACK], BF16, name=name, align_bytes=64)
-            nc.vector.tensor_tensor(
-                grouped[:].rearrange("p (c i) t -> p c t i", i=PAIR),
-                a.rearrange("p t (c i) -> p c t i", i=PAIR),
-                b.rearrange("p t (c i) -> p c t i", i=PAIR),
+        def finish_front(e0, e1):
+            nc.vector.scalar_tensor_tensor(
+                grouped[:, e0:e1, :],
+                by_edge(h_front[:, :, e0:e1]),
+                1.0,
+                by_edge(times_h[:, :, e0:e1]),
+                ALU.subtract,
                 ALU.mult,
             )
-            return grouped
 
-        def quantise(grouped, e0):
-            e1 = e0 + grouped.shape[1]
+        def finish_rear(e0, e1):
+            cols = slice(e0 - FRONT, e1 - FRONT)
+            nc.vector.scalar_tensor_tensor(
+                grouped[:, e0:e1, :],
+                by_edge(square[:, :, cols]),
+                0.25,
+                by_edge(looked_up[:, :, cols]),
+                ALU.subtract,
+                ALU.mult,
+            )
+
+        def centred_square(e0, e1, h):
+            nc.scalar.activation(square[:, :, e0 - FRONT : e1 - FRONT], h, SQUARE, bias=-0.5, scale=1.0)
+
+        def quantise(e0, e1):
             nc.vector.quantize_mx(
                 out=dz_codes[:, e0:e1].bitcast(E5M2X4),
                 scales=dz_scale[:, e0:e1],
-                in_=grouped[:].rearrange("p e t -> p (e t)"),
+                in_=grouped[:, e0:e1, :].rearrange("p e t -> p (e t)"),
             )
 
         def multiply(e0, e1, b):
@@ -133,42 +135,35 @@ def tile_attend_gmp_sig_kernel(tc, dyT, hE, w_words, w_scales, offs, offs2, out)
         def empty_on_vector(half, e0, e1, b):
             nc.vector.tensor_scalar(dm[half][:, e0:e1], bank[half][b][:, : e1 - e0], -1.0, None, ALU.mult)
 
-        for c in range(len(CHUNKS)):
-            if c == 1:
-                for t in range(PACK):
-                    nc.vector.tensor_tensor(head_product[:, t, :], columns(t, 0, HEAD), h_head[t][:], ALU.mult)
-                    nc.vector.tensor_scalar(head_less_one[:, t, :], h_head[t][:], -1.0, None, ALU.add)
-                grouped = product("grouped_head", head_product, head_less_one)
-            if c == 3:
-                continue
-            look_up(c)
+        def contract(i):
+            quantise(*PASSES[i][:2])
+            multiply(*PASSES[i])
 
-        waiting = (grouped, 0, HEAD, 0)
-        emptied = []
-        for c, (e0, e1) in enumerate(CHUNKS):
-            make_slope(c)
-            quantise(waiting[0], waiting[1])
-            multiply(*waiting[1:])
-            emptied.append(waiting[1:])
-            if c < 3:
-                waiting = (product("grouped%d" % c, looked_up[c], slope[c][:]), e0, e1, c + 1)
-            if c == 0:
-                look_up(3)
-        for piece in emptied:
+        for t in range(PACK):
+            for e0, e1 in ((0, FIRST), (FIRST, FRONT)) if t == 0 else ((0, FRONT),):
+                nc.vector.tensor_tensor(times_h[:, t, e0:e1], columns(t, e0, e1), h_front[:, t, e0:e1], ALU.mult)
+            nc.scalar.activation(looked_up[:, t, :], columns(t, FRONT, E), COPY)
+        centred_square(FRONT, 1408, h_rear[0][:])
+        centred_square(1408, 1664, h_rear[1][:, :, :256])
+        centred_square(1664, E, h_rear[1][:, :, 256:])
+        finish_front(0, 512)
+        finish_front(512, FRONT)
+        for i in range(3):
+            contract(i)
+        for i in range(3):
             for half in range(HALVES):
-                empty_on_scalar(half, *piece)
-        e0, e1 = CHUNKS[3]
-        cut = e1 - e0 - LAST
-        tail = [
-            (product("grouped_a", looked_up[3][:, :, :cut], slope[3][:, :, :cut]), e0, e0 + cut, 0),
-            (product("grouped_b", looked_up[3][:, :, cut:], slope[3][:, :, cut:]), e0 + cut, e1, 1),
-        ]
-        for piece in tail:
-            quantise(piece[0], piece[1])
-            multiply(*piece[1:])
-        for piece in tail:
-            empty_on_vector(0, *piece[1:])
-            empty_on_scalar(1, *piece[1:])
+                empty_on_scalar(half, *PASSES[i])
+        finish_rear(*PASSES[3][:2])
+        for i in range(3, 6):
+            finish_rear(*PASSES[i + 1][:2])
+            contract(i)
+        contract(6)
+        for i in range(3, 5):
+            for half in range(HALVES):
+                empty_on_scalar(half, *PASSES[i])
+        for i in range(5, 7):
+            empty_on_vector(0, *PASSES[i])
+            empty_on_scalar(1, *PASSES[i])
 
         out_halves = out.rearrange("(h p) x -> p h x", h=HALVES)
 
@@ -178,35 +173,28 @@ def tile_attend_gmp_sig_kernel(tc, dyT, hE, w_words, w_scales, offs, offs2, out)
         def both(name, columns):
             return keep.tile([P, HALVES, columns], F32, name=name)
 
-        def by_node(entries):
-            return entries.rearrange("p h (x j) -> p h x j", j=K)
-
-        def add_up(sums, entries):
-            nc.vector.tensor_reduce(sums, by_node(entries), mybir.AxisListType.X, ALU.add)
-
-        pairs = keep.tile([P, V // 2, HALVES, 2], F32, name="pairs")
-        for s0, s1 in ((0, 256), (256, 640), (640, 1024)):
+        early = 896
+        pairs = keep.tile([P, early // K, HALVES, 2], F32, name="pairs")
+        for s0, s1 in ((0, 256), (256, 576), (576, early)):
             picked = both("picked%d" % s0, s1 - s0)
             nc.vector.tensor_copy(picked[:, 0, :], listed(0, s0, s1))
             nc.scalar.activation(picked[:, 1, :], listed(1, s0, s1), COPY)
             entries = picked[:].rearrange("p h (x j) -> p x h j", j=K)
             nc.gpsimd.tensor_tensor(pairs[:, s0 // K : s1 // K], entries[:, :, :, 0:2], entries[:, :, :, 2:4], ALU.add)
-        front = both("front", V // 2)
-        nc.gpsimd.tensor_tensor(front[:].rearrange("p h x -> p x h"), pairs[:, :, :, 0], pairs[:, :, :, 1], ALU.add)
+        early_sums = both("early_sums", early // K)
+        nc.gpsimd.tensor_tensor(early_sums[:].rearrange("p h x -> p x h"), pairs[:, :, :, 0], pairs[:, :, :, 1], ALU.add)
 
-        third, fourth = both("third", 512), both("fourth", 512)
-        middle, back = both("middle", 128), both("back", 128)
-        nc.vector.tensor_copy(third[:, 0, :], listed(0, 1024, 1536))
-        nc.vector.tensor_copy(fourth[:, 0, :128], listed(0, 1536, 1664))
-        nc.scalar.activation(third[:, 1, :], listed(1, 1024, 1536), COPY)
-        nc.scalar.activation(fourth[:, 1, :384], listed(1, 1536, 1920), COPY)
-        nc.scalar.activation(fourth[:, 0, 128:], listed(0, 1664, 2048), COPY)
-        nc.scalar.activation(fourth[:, 1, 384:], listed(1, 1920, 2048), COPY)
-        add_up(middle[:], third[:])
-        nc.sync.dma_start(out_halves[:, :, 256:384], middle[:])
-        nc.sync.dma_start(out_halves[:, :, :256], front[:])
-        add_up(back[:, 0:1, :32], fourth[:, 0:1, :128])
-        add_up(back[:, 1:2, :96], fourth[:, 1:2, :384])
-        add_up(back[:, 0:1, 32:], fourth[:, 0:1, 128:])
-        add_up(back[:, 1:2, 96:], fourth[:, 1:2, 384:])
-        nc.sync.dma_start(out_halves[:, :, 384:], back[:])
+        late = [(1, early, 1408), (0, early, 1664), (1, 1408, 1920), (0, 1664, E), (1, 1920, E)]
+        picked = [keep.tile([P, s1 - s0], F32, name="late%d_%d" % (half, s0)) for half, s0, s1 in late]
+        for i, piece in enumerate(late):
+            if i == 1:
+                nc.vector.tensor_copy(picked[i][:], listed(*piece))
+            else:
+                nc.scalar.activation(picked[i][:], listed(*piece), COPY)
+        for i, (half, s0, s1) in enumerate(late):
+            sums = keep.tile([P, (s1 - s0) // K], F32, name="sums%d" % i)
+            nc.vector.tensor_reduce(sums[:], picked[i][:].rearrange("p (x j) -> p x j", j=K), mybir.AxisListType.X, ALU.add)
+            queue = nc.scalar if i == len(late) - 1 else nc.sync
+            queue.dma_start(out_halves[:, half, s0 // K : s1 // K], sums[:])
+            if i == 2:
+                nc.sync.dma_start(out_halves[:, :, : early // K], early_sums[:])

@@ -26,7 +26,7 @@ FRONT = 896
 REAR = E - FRONT
 FIRST = 256
 SPARE = REAR + 32 - V
-STAGGER = 9
+STAGGER = 8
 PASSES = [(0, 512, 0), (512, 768, 1), (768, FRONT, 2), (FRONT, 1408, 3), (1408, 1664, 0), (1664, 1920, 1), (1920, E, 2)]
 
 
@@ -60,7 +60,7 @@ def tile_attend_gmp_sig_kernel(tc, dyT, hE, w_words, w_scales, offs, offs2, out)
         h_rows = hE.rearrange("(p t) e -> p t e", t=PACK)
 
         for t in range(PACK):
-            nc.vector.memset(dy[t][:, V:], 0.0)
+            (nc.vector if t < 2 else nc.gpsimd).memset(dy[t][:, V:], 0.0)
         nc.gpsimd.memset(w_scale[:].bitcast(I32), 0)
 
         nc.sync.dma_start(dst[:], offs)
@@ -154,13 +154,17 @@ def tile_attend_gmp_sig_kernel(tc, dyT, hE, w_words, w_scales, offs, offs2, out)
             for half in range(HALVES):
                 empty_on_scalar(half, *PASSES[i])
         finish_rear(*PASSES[3][:2])
-        for i in range(3, 6):
-            finish_rear(*PASSES[i + 1][:2])
-            contract(i)
+        finish_rear(*PASSES[4][:2])
+        contract(3)
+        finish_rear(*PASSES[5][:2])
+        contract(4)
+        contract(5)
+        finish_rear(*PASSES[6][:2])
+        for half in range(HALVES):
+            empty_on_scalar(half, *PASSES[3])
+        empty_on_vector(0, *PASSES[4])
+        empty_on_scalar(1, *PASSES[4])
         contract(6)
-        for i in range(3, 5):
-            for half in range(HALVES):
-                empty_on_scalar(half, *PASSES[i])
         for i in range(5, 7):
             empty_on_vector(0, *PASSES[i])
             empty_on_scalar(1, *PASSES[i])
@@ -173,9 +177,9 @@ def tile_attend_gmp_sig_kernel(tc, dyT, hE, w_words, w_scales, offs, offs2, out)
         def both(name, columns):
             return keep.tile([P, HALVES, columns], F32, name=name)
 
-        early = 896
+        early = 768
         pairs = keep.tile([P, early // K, HALVES, 2], F32, name="pairs")
-        for s0, s1 in ((0, 256), (256, 576), (576, early)):
+        for s0, s1 in ((0, 256), (256, 512), (512, early)):
             picked = both("picked%d" % s0, s1 - s0)
             nc.vector.tensor_copy(picked[:, 0, :], listed(0, s0, s1))
             nc.scalar.activation(picked[:, 1, :], listed(1, s0, s1), COPY)
@@ -184,7 +188,7 @@ def tile_attend_gmp_sig_kernel(tc, dyT, hE, w_words, w_scales, offs, offs2, out)
         early_sums = both("early_sums", early // K)
         nc.gpsimd.tensor_tensor(early_sums[:].rearrange("p h x -> p x h"), pairs[:, :, :, 0], pairs[:, :, :, 1], ALU.add)
 
-        late = [(1, early, 1408), (0, early, 1664), (1, 1408, 1920), (0, 1664, E), (1, 1920, E)]
+        late = [(1, early, 1280), (0, early, 1536), (1, 1280, 1920), (0, 1536, E), (1, 1920, E)]
         picked = [keep.tile([P, s1 - s0], F32, name="late%d_%d" % (half, s0)) for half, s0, s1 in late]
         for i, piece in enumerate(late):
             if i == 1:
@@ -196,5 +200,5 @@ def tile_attend_gmp_sig_kernel(tc, dyT, hE, w_words, w_scales, offs, offs2, out)
             nc.vector.tensor_reduce(sums[:], picked[i][:].rearrange("p (x j) -> p x j", j=K), mybir.AxisListType.X, ALU.add)
             queue = nc.scalar if i == len(late) - 1 else nc.sync
             queue.dma_start(out_halves[:, half, s0 // K : s1 // K], sums[:])
-            if i == 2:
+            if i == 1:
                 nc.sync.dma_start(out_halves[:, :, : early // K], early_sums[:])

@@ -22,12 +22,13 @@ PACK = 4
 HALVES = D // P
 PER_COLUMN = 16
 BANK = 512
-FRONT = 896
+FRONT = 832
 REAR = E - FRONT
 FIRST = 256
 SPARE = REAR + 32 - V
-STAGGER = 8
-PASSES = [(0, 512, 0), (512, 768, 1), (768, FRONT, 2), (FRONT, 1408, 3), (1408, 1664, 0), (1664, 1920, 1), (1920, E, 2)]
+STAGGER = 9
+PASSES = [(0, 512, 0), (512, 768, 1), (768, 1280, 2), (1280, 1536, 3), (1536, 1792, 0), (1792, 1920, 1), (1920, E, 2)]
+NEXT = 1280 - FRONT
 
 
 def tile_attend_gmp_sig_kernel(tc, dyT, hE, w_words, w_scales, offs, offs2, out):
@@ -51,9 +52,16 @@ def tile_attend_gmp_sig_kernel(tc, dyT, hE, w_words, w_scales, offs, offs2, out)
 
         h_front = row_sets("h_front", FRONT)
         times_h = row_sets("times_h", FRONT)
-        h_rear = [keep.tile([P, PACK, e1 - e0], F32, name="h_rear%d" % e0) for e0, e1 in ((FRONT, 1408), (1408, E))]
         square = row_sets("square", REAR)
-        looked_up = row_sets("looked_up", REAR)
+        pitch = REAR + STAGGER
+        room = keep.tile([P, (PACK + 1) * pitch], F32, name="room", align_bytes=64)
+        looked_up = room[:, : PACK * pitch].rearrange("p (t e) -> p t e", t=PACK)[:, :, :REAR]
+        shared = (3 * pitch + NEXT) // 8 * 8 + 8
+        h_next = [
+            room[:, shared : shared + 2 * NEXT].rearrange("p (t e) -> p t e", t=2),
+            keep.tile([P, 2, NEXT], F32, name="h_next1")[:],
+        ]
+        h_late = keep.tile([P, PACK, E - 1280], F32, name="h_late")
         grouped = keep.tile([P, E, PACK], BF16, name="grouped", align_bytes=64)
 
         dy_rows = dyT.rearrange("(p t) x -> t p x", t=PACK)
@@ -70,8 +78,9 @@ def tile_attend_gmp_sig_kernel(tc, dyT, hE, w_words, w_scales, offs, offs2, out)
         for t in range(1, PACK):
             nc.sync.dma_start(dy[t][:, :V], dy_rows[t])
             nc.sync.dma_start(h_front[:, t, :], h_rows[:, t, :FRONT])
-        nc.sync.dma_start(h_rear[0][:], h_rows[:, :, FRONT:1408])
-        nc.sync.dma_start(h_rear[1][:], h_rows[:, :, 1408:])
+        for i in range(2):
+            nc.sync.dma_start(h_next[i], h_rows[:, 2 * i : 2 * i + 2, FRONT:1280])
+        nc.sync.dma_start(h_late[:], h_rows[:, :, 1280:])
         nc.sync.dma_start(w_codes[:].bitcast(I32), w_words[0].rearrange("p d r -> p (d r)").bitcast(I32))
         for q in range(4):
             nc.sync.dma_start(
@@ -106,8 +115,8 @@ def tile_attend_gmp_sig_kernel(tc, dyT, hE, w_words, w_scales, offs, offs2, out)
                 ALU.mult,
             )
 
-        def centred_square(e0, e1, h):
-            nc.scalar.activation(square[:, :, e0 - FRONT : e1 - FRONT], h, SQUARE, bias=-0.5, scale=1.0)
+        def centred_square(squared, h):
+            nc.scalar.activation(squared, h, SQUARE, bias=-0.5, scale=1.0)
 
         def quantise(e0, e1):
             nc.vector.quantize_mx(
@@ -142,28 +151,28 @@ def tile_attend_gmp_sig_kernel(tc, dyT, hE, w_words, w_scales, offs, offs2, out)
         for t in range(PACK):
             for e0, e1 in ((0, FIRST), (FIRST, FRONT)) if t == 0 else ((0, FRONT),):
                 nc.vector.tensor_tensor(times_h[:, t, e0:e1], columns(t, e0, e1), h_front[:, t, e0:e1], ALU.mult)
+        for t in range(PACK - 1):
             nc.scalar.activation(looked_up[:, t, :], columns(t, FRONT, E), COPY)
-        centred_square(FRONT, 1408, h_rear[0][:])
-        centred_square(1408, 1664, h_rear[1][:, :, :256])
-        centred_square(1664, E, h_rear[1][:, :, 256:])
+        nc.scalar.activation(looked_up[:, 3, :NEXT], columns(3, FRONT, 1280), COPY)
+        for i in range(2):
+            centred_square(square[:, 2 * i : 2 * i + 2, :NEXT], h_next[i])
+        nc.scalar.activation(looked_up[:, 3, NEXT:], columns(3, 1280, E), COPY)
+        for e0, e1 in ((1280, 1536), (1536, E)):
+            centred_square(square[:, :, e0 - FRONT : e1 - FRONT], h_late[:, :, e0 - 1280 : e1 - 1280])
         finish_front(0, 512)
         finish_front(512, FRONT)
-        for i in range(3):
+        for i in range(2):
             contract(i)
-        for i in range(3):
+        for i in range(2):
             for half in range(HALVES):
                 empty_on_scalar(half, *PASSES[i])
-        finish_rear(*PASSES[3][:2])
-        finish_rear(*PASSES[4][:2])
-        contract(3)
-        finish_rear(*PASSES[5][:2])
-        contract(4)
-        contract(5)
-        finish_rear(*PASSES[6][:2])
-        for half in range(HALVES):
-            empty_on_scalar(half, *PASSES[3])
-        empty_on_vector(0, *PASSES[4])
-        empty_on_scalar(1, *PASSES[4])
+        finish_rear(FRONT, 1280)
+        for i in range(2, 6):
+            finish_rear(*PASSES[i + 1][:2])
+            contract(i)
+            if i < 5:
+                for half in range(HALVES):
+                    empty_on_scalar(half, *PASSES[i])
         contract(6)
         for i in range(5, 7):
             empty_on_vector(0, *PASSES[i])
@@ -174,31 +183,23 @@ def tile_attend_gmp_sig_kernel(tc, dyT, hE, w_words, w_scales, offs, offs2, out)
         def listed(half, s0, s1):
             return dm[half][:].indirect(src[:, s0 // PER_COLUMN : s1 // PER_COLUMN])
 
-        def both(name, columns):
-            return keep.tile([P, HALVES, columns], F32, name=name)
+        early = 1536
+        pairs = keep.tile([P, 2, early // K], F32, name="pairs")
+        for s0 in range(0, early, 512):
+            picked = keep.tile([P, K, 128], F32, name="picked%d" % s0)
+            nc.vector.tensor_copy(picked[:].rearrange("p j x -> p x j"), listed(0, s0, s0 + 512))
+            nc.gpsimd.tensor_tensor(pairs[:, :, s0 // K : s0 // K + 128], picked[:, 0:2, :], picked[:, 2:4, :], ALU.add)
+        early_sums = keep.tile([P, early // K], F32, name="early_sums")
+        nc.gpsimd.tensor_tensor(early_sums[:], pairs[:, 0, :], pairs[:, 1, :], ALU.add)
 
-        early = 768
-        pairs = keep.tile([P, early // K, HALVES, 2], F32, name="pairs")
-        for s0, s1 in ((0, 256), (256, 512), (512, early)):
-            picked = both("picked%d" % s0, s1 - s0)
-            nc.vector.tensor_copy(picked[:, 0, :], listed(0, s0, s1))
-            nc.scalar.activation(picked[:, 1, :], listed(1, s0, s1), COPY)
-            entries = picked[:].rearrange("p h (x j) -> p x h j", j=K)
-            nc.gpsimd.tensor_tensor(pairs[:, s0 // K : s1 // K], entries[:, :, :, 0:2], entries[:, :, :, 2:4], ALU.add)
-        early_sums = both("early_sums", early // K)
-        nc.gpsimd.tensor_tensor(early_sums[:].rearrange("p h x -> p x h"), pairs[:, :, :, 0], pairs[:, :, :, 1], ALU.add)
-
-        late = [(1, early, 1280), (0, early, 1536), (1, 1280, 1920), (0, 1536, E), (1, 1920, E)]
+        late = [(1, 0, 768), (1, 768, 1408), (1, 1408, 1920), (0, early, E), (1, 1920, E)]
         picked = [keep.tile([P, s1 - s0], F32, name="late%d_%d" % (half, s0)) for half, s0, s1 in late]
         for i, piece in enumerate(late):
-            if i == 1:
-                nc.vector.tensor_copy(picked[i][:], listed(*piece))
-            else:
-                nc.scalar.activation(picked[i][:], listed(*piece), COPY)
+            nc.scalar.activation(picked[i][:], listed(*piece), COPY)
         for i, (half, s0, s1) in enumerate(late):
             sums = keep.tile([P, (s1 - s0) // K], F32, name="sums%d" % i)
             nc.vector.tensor_reduce(sums[:], picked[i][:].rearrange("p (x j) -> p x j", j=K), mybir.AxisListType.X, ALU.add)
             queue = nc.scalar if i == len(late) - 1 else nc.sync
             queue.dma_start(out_halves[:, half, s0 // K : s1 // K], sums[:])
-            if i == 1:
-                nc.sync.dma_start(out_halves[:, :, : early // K], early_sums[:])
+            if i == 2:
+                nc.sync.dma_start(out_halves[:, 0, : early // K], early_sums[:])

from contextlib import ExitStack

import concourse.mybir as mybir

V, K, E, D, DV = 512, 4, 2048, 256, 512
FLOPS = 2 * DV * D * E

F32 = mybir.dt.float32
BF16 = mybir.dt.bfloat16
I32 = mybir.dt.int32
U32 = mybir.dt.uint32
U16 = mybir.dt.uint16
U8 = mybir.dt.uint8
E4M3X4 = mybir.dt.float8_e4m3fn_x4
E5M2X4 = mybir.dt.float8_e5m2_x4
ALU = mybir.AluOpType
COPY = mybir.ActivationFunctionType.Copy
SQUARE = mybir.ActivationFunctionType.Square

P = 128
PACK = 4
HALVES = D // P
PER_COLUMN = 16
BANK = 512
FRONT = 832
REAR = E - FRONT
FIRST = 256
SPARE = REAR + 32 - V
STAGGER = 9
PASSES = [(0, 512, 0), (512, 768, 1), (768, 1280, 2), (1280, 1536, 3), (1536, 1792, 0), (1792, 1920, 1), (1920, E, 2)]
NEXT = 1280 - FRONT


def tile_attend_gmp_sig_kernel(tc, dyT, hE, w_words, w_scales, offs, offs2, out):
    nc = tc.nc
    with ExitStack() as ctx:
        keep = ctx.enter_context(tc.tile_pool(name="keep", bufs=1))
        psum = ctx.enter_context(tc.psum_pool(name="psum", bufs=1))

        dst = keep.tile([P, E // PER_COLUMN], U16, name="dst")
        src = keep.tile([P, E // PER_COLUMN], U16, name="src")
        dy = [keep.tile([P, V + SPARE], F32, name="dy%d" % t) for t in range(PACK)]
        dz_codes = keep.tile([P, E], U32, name="dz_codes", align_bytes=64)
        w_codes = keep.tile([P, D], U32, name="w_codes", align_bytes=64)
        w_scale = keep.tile([P, D], U8, name="w_scale", align_bytes=64)
        dz_scale = keep.tile([P, E], U8, name="dz_scale", align_bytes=64)
        dm = [keep.tile([P, E], F32, name="dm%d" % half) for half in range(HALVES)]
        bank = [[psum.tile([P, BANK], F32, name="bank%d_%d" % (half, b)) for b in range(4)] for half in range(HALVES)]

        def row_sets(name, edges):
            return keep.tile([P, PACK, edges + STAGGER], F32, name=name, align_bytes=64)[:, :, :edges]

        h_front = row_sets("h_front", FRONT)
        times_h = row_sets("times_h", FRONT)
        square = row_sets("square", REAR)
        pitch = REAR + STAGGER
        room = keep.tile([P, (PACK + 1) * pitch], F32, name="room", align_bytes=64)
        looked_up = room[:, : PACK * pitch].rearrange("p (t e) -> p t e", t=PACK)[:, :, :REAR]
        shared = (3 * pitch + NEXT) // 8 * 8 + 8
        h_next = [
            room[:, shared : shared + 2 * NEXT].rearrange("p (t e) -> p t e", t=2),
            keep.tile([P, 2, NEXT], F32, name="h_next1")[:],
        ]
        h_late = keep.tile([P, PACK, E - 1280], F32, name="h_late")
        grouped = keep.tile([P, E, PACK], BF16, name="grouped", align_bytes=64)

        dy_rows = dyT.rearrange("(p t) x -> t p x", t=PACK)
        h_rows = hE.rearrange("(p t) e -> p t e", t=PACK)

        for t in range(PACK):
            (nc.vector if t < 2 else nc.gpsimd).memset(dy[t][:, V:], 0.0)
        nc.gpsimd.memset(w_scale[:].bitcast(I32), 0)

        nc.sync.dma_start(dst[:], offs)
        nc.sync.dma_start(dy[0][:, :V], dy_rows[0])
        nc.sync.dma_start(h_front[:, 0, :FIRST], h_rows[:, 0, :FIRST])
        nc.sync.dma_start(h_front[:, 0, FIRST:], h_rows[:, 0, FIRST:FRONT])
        for t in range(1, PACK):
            nc.sync.dma_start(dy[t][:, :V], dy_rows[t])
            nc.sync.dma_start(h_front[:, t, :], h_rows[:, t, :FRONT])
        for i in range(2):
            nc.sync.dma_start(h_next[i], h_rows[:, 2 * i : 2 * i + 2, FRONT:1280])
        nc.sync.dma_start(h_late[:], h_rows[:, :, 1280:])
        nc.sync.dma_start(w_codes[:].bitcast(I32), w_words[0].rearrange("p d r -> p (d r)").bitcast(I32))
        for q in range(4):
            nc.sync.dma_start(
                w_scale[32 * q : 32 * q + 4, :].bitcast(I32), w_scales[0, 4 * q : 4 * q + 4, :].bitcast(I32)
            )
        nc.sync.dma_start(src[:], offs2)

        def columns(t, e0, e1):
            return dy[t][:].indirect(dst[:, e0 // PER_COLUMN : e1 // PER_COLUMN])

        def by_edge(values):
            return values.rearrange("p t e -> p e t")

        def finish_front(e0, e1):
            nc.vector.scalar_tensor_tensor(
                grouped[:, e0:e1, :],
                by_edge(h_front[:, :, e0:e1]),
                1.0,
                by_edge(times_h[:, :, e0:e1]),
                ALU.subtract,
                ALU.mult,
            )

        def finish_rear(e0, e1):
            cols = slice(e0 - FRONT, e1 - FRONT)
            nc.vector.scalar_tensor_tensor(
                grouped[:, e0:e1, :],
                by_edge(square[:, :, cols]),
                0.25,
                by_edge(looked_up[:, :, cols]),
                ALU.subtract,
                ALU.mult,
            )

        def centred_square(squared, h):
            nc.scalar.activation(squared, h, SQUARE, bias=-0.5, scale=1.0)

        def quantise(e0, e1):
            nc.vector.quantize_mx(
                out=dz_codes[:, e0:e1].bitcast(E5M2X4),
                scales=dz_scale[:, e0:e1],
                in_=grouped[:, e0:e1, :].rearrange("p e t -> p (e t)"),
            )

        def multiply(e0, e1, b):
            for half in range(HALVES):
                d_cols = slice(half * P, (half + 1) * P)
                nc.tensor.matmul_mx(
                    out=bank[half][b][:, : e1 - e0],
                    lhsT=w_codes[:, d_cols].bitcast(E4M3X4),
                    lhsT_scale=w_scale[:, d_cols],
                    rhs=dz_codes[:, e0:e1].bitcast(E5M2X4),
                    rhs_scale=dz_scale[:, e0:e1],
                    start=True,
                    stop=True,
                )

        def empty_on_scalar(half, e0, e1, b):
            nc.scalar.activation(dm[half][:, e0:e1], bank[half][b][:, : e1 - e0], COPY, scale=-1.0)

        def empty_on_vector(half, e0, e1, b):
            nc.vector.tensor_scalar(dm[half][:, e0:e1], bank[half][b][:, : e1 - e0], -1.0, None, ALU.mult)

        def contract(i):
            quantise(*PASSES[i][:2])
            multiply(*PASSES[i])

        for t in range(PACK):
            for e0, e1 in ((0, FIRST), (FIRST, FRONT)) if t == 0 else ((0, FRONT),):
                nc.vector.tensor_tensor(times_h[:, t, e0:e1], columns(t, e0, e1), h_front[:, t, e0:e1], ALU.mult)
        for t in range(PACK - 1):
            nc.scalar.activation(looked_up[:, t, :], columns(t, FRONT, E), COPY)
        nc.scalar.activation(looked_up[:, 3, :NEXT], columns(3, FRONT, 1280), COPY)
        for i in range(2):
            centred_square(square[:, 2 * i : 2 * i + 2, :NEXT], h_next[i])
        nc.scalar.activation(looked_up[:, 3, NEXT:], columns(3, 1280, E), COPY)
        for e0, e1 in ((1280, 1536), (1536, E)):
            centred_square(square[:, :, e0 - FRONT : e1 - FRONT], h_late[:, :, e0 - 1280 : e1 - 1280])
        finish_front(0, 512)
        finish_front(512, FRONT)
        for i in range(2):
            contract(i)
        for i in range(2):
            for half in range(HALVES):
                empty_on_scalar(half, *PASSES[i])
        finish_rear(FRONT, 1280)
        for i in range(2, 6):
            finish_rear(*PASSES[i + 1][:2])
            contract(i)
            if i < 5:
                for half in range(HALVES):
                    empty_on_scalar(half, *PASSES[i])
        contract(6)
        for i in range(5, 7):
            empty_on_vector(0, *PASSES[i])
            empty_on_scalar(1, *PASSES[i])

        out_halves = out.rearrange("(h p) x -> p h x", h=HALVES)

        def listed(half, s0, s1):
            return dm[half][:].indirect(src[:, s0 // PER_COLUMN : s1 // PER_COLUMN])

        early = 1536
        pairs = keep.tile([P, 2, early // K], F32, name="pairs")
        for s0 in range(0, early, 512):
            picked = keep.tile([P, K, 128], F32, name="picked%d" % s0)
            nc.vector.tensor_copy(picked[:].rearrange("p j x -> p x j"), listed(0, s0, s0 + 512))
            nc.gpsimd.tensor_tensor(pairs[:, :, s0 // K : s0 // K + 128], picked[:, 0:2, :], picked[:, 2:4, :], ALU.add)
        early_sums = keep.tile([P, early // K], F32, name="early_sums")
        nc.gpsimd.tensor_tensor(early_sums[:], pairs[:, 0, :], pairs[:, 1, :], ALU.add)

        late = [(1, 0, 768), (1, 768, 1408), (1, 1408, 1920), (0, early, E), (1, 1920, E)]
        picked = [keep.tile([P, s1 - s0], F32, name="late%d_%d" % (half, s0)) for half, s0, s1 in late]
        for i, piece in enumerate(late):
            nc.scalar.activation(picked[i][:], listed(*piece), COPY)
        for i, (half, s0, s1) in enumerate(late):
            sums = keep.tile([P, (s1 - s0) // K], F32, name="sums%d" % i)
            nc.vector.tensor_reduce(sums[:], picked[i][:].rearrange("p (x j) -> p x j", j=K), mybir.AxisListType.X, ALU.add)
            queue = nc.scalar if i == len(late) - 1 else nc.sync
            queue.dma_start(out_halves[:, half, s0 // K : s1 // K], sums[:])
            if i == 2:
                nc.sync.dma_start(out_halves[:, 0, : early // K], early_sums[:])
